import numpy as np
import ml_dtypes


def mxq(x, axis, fmt="e4m3"):
    dtype, down = {"e4m3": (ml_dtypes.float8_e4m3fn, 7), "e5m2": (ml_dtypes.float8_e5m2, 14)}[fmt]
    v = np.moveaxis(np.asarray(x, np.float32).astype(ml_dtypes.bfloat16).astype(np.float64), axis, -1)
    blocks = v.reshape(v.shape[:-1] + (-1, 32))
    amax = np.abs(blocks).max(-1, keepdims=True)
    byte = np.maximum(np.where(amax > 0, np.frexp(amax)[1] - 1 + 127, 0) - down, 1)
    scale = np.exp2(byte - 127.0)
    codes = (blocks / scale).astype(np.float32).astype(dtype).astype(np.float64)
    return np.moveaxis((codes * scale).reshape(v.shape), -1, axis)


WIDE = False


def mx_kscale(k):
    if not WIDE:
        return np.ones(k)
    levels = np.array([18, -18])
    if k % 512:
        return np.exp2(np.random.permutation(np.resize(levels, k // 32))).repeat(32)
    a = np.empty((k // 512, 16))
    for p in range(k // 512):
        a[p, :8] = np.random.permutation(np.resize(levels, 8))
        for g in range(8):
            far = levels[np.abs(levels - a[p, g]) >= 10]
            a[p, g + 8] = far[np.random.randint(len(far))]
    return np.exp2(a.ravel()).repeat(32)


def f64(x):
    return np.asarray(x).astype(np.float64)


def striped(idx):
    return np.tile(np.asarray(idx).reshape(-1, 16).T, (8, 1)).astype(np.uint16)


def unstriped(offs):
    return offs[:16].T.reshape(-1).astype(np.int64)


B = 2


def sig(x):
    return 1.0 / (1.0 + np.exp(-x))


def setup_inputs():
    n = np.random.standard_normal
    uni = np.random.uniform
    idx = np.random.permutation(2048)[:1024]
    f_d = mx_kscale(512)
    f_e = mx_kscale(512)
    f_f = mx_kscale(512)
    return {
        "xT": (n((512, 2048)) / np.sqrt(512) * f_d[:, None]).astype(np.float32),
        "dyT": (n((512, 2048)) * f_e[:, None]).astype(np.float32),
        "w1": (n((2, 512, 512)) / f_d[:, None] * f_f[None, :]).astype(np.float32),
        "w2": (n((2, 512, 512)) / np.sqrt(512) / f_e[None, :]).astype(np.float32),
        "ts": np.tile(uni(0.75, 1.3, 2048) / np.sqrt(512), (128, 1)).astype(np.float32),
        "tx": np.tile(uni(0.75, 1.3, 2048), (128, 1)).astype(np.float32),
        "cf": (uni(0.75, 1.3, (512, 1)) / f_f[:, None]).astype(np.float32),
        "offs": striped(idx),
    }


def reference(xT, dyT, w1, w2, ts, tx, cf, offs):
    idx = unstriped(offs).reshape(B, 512)
    xT_i = f64(xT)[:, idx].transpose(1, 0, 2)
    dyT_i = f64(dyT)[:, idx].transpose(1, 0, 2)
    ts_i = f64(ts)[:1][:, idx].transpose(1, 0, 2)
    tx_i = f64(tx)[:1][:, idx].transpose(1, 0, 2)
    a = mxq(f64(w1), 1, "e4m3").transpose(0, 2, 1) @ mxq(xT_i, 1, "e4m3")
    z = f64(cf) * tx_i * a
    dh = mxq(f64(w2), 2, "e4m3") @ mxq(dyT_i, 1, "e5m2")
    da = f64(cf) * tx_i * ts_i * dh * sig(z) * (1.0 + z * (1.0 - sig(z)))
    dx = mxq(f64(w1), 2, "e4m3") @ mxq(da, 1, "e5m2")
    out = np.zeros((512, 2048))
    out[:, idx] = dx.transpose(1, 0, 2)
    return out

@@ -1,0 +1,262 @@
+from contextlib import ExitStack
+
+import concourse.mybir as mybir
+from concourse.masks import make_identity
+
+F32 = mybir.dt.float32
+BF16 = mybir.dt.bfloat16
+U32 = mybir.dt.uint32
+U16 = mybir.dt.uint16
+U8 = mybir.dt.uint8
+E4M3 = mybir.dt.float8_e4m3fn_x4
+E5M2 = mybir.dt.float8_e5m2_x4
+ACT = mybir.ActivationFunctionType
+ALU = mybir.AluOpType
+
+P = 128
+PACK = 4
+K = P * PACK
+EXPERTS = 2
+SLOTS = 512
+TOKENS = 2048
+LIST_COLS = SLOTS // 16
+ROW = P - 1
+ALIGN = 64
+
+FLOPS = 3 * EXPERTS * 2 * K * K * SLOTS
+
+
+def tile_attend_gxfull_sil_x_kernel(tc, xT, dyT, w1, w2, ts, tx, cf, offs, out):
+    nc = tc.nc
+    with ExitStack() as ctx:
+        keep = ctx.enter_context(tc.tile_pool(name="keep", bufs=1))
+        work = ctx.enter_context(tc.tile_pool(name="work", bufs=1))
+        psum = ctx.enter_context(tc.psum_pool(name="psum", bufs=2))
+
+        def big(shape, name):
+            return work.tile(shape, F32, name=name, tag="big", bufs=8, align_bytes=ALIGN)
+
+        def mid(shape, name):
+            return work.tile(shape, F32, name=name, tag="mid", bufs=2, align_bytes=ALIGN)
+
+        def small(dtype, name):
+            return work.tile([P, SLOTS], dtype, name=name, tag="small", bufs=4, align_bytes=ALIGN)
+
+        def woven_tile(name):
+            return work.tile([P, K, PACK], BF16, name=name, tag="woven", bufs=4, align_bytes=ALIGN)
+
+        def bank(shape, name, tag):
+            return psum.tile(shape, F32, name=name, tag=tag)
+
+        def mx_tiles(name):
+            codes = keep.tile([P, K], U32, name=name + "_codes", align_bytes=ALIGN)
+            scales = keep.tile([P, K], U8, name=name + "_scales", align_bytes=ALIGN)
+            return codes, scales
+
+        def quantize(mx, woven, fmt, cols=slice(0, K)):
+            codes, scales = mx
+            nc.vector.quantize_mx(
+                out=codes[:, cols].bitcast(fmt),
+                scales=scales[:, cols],
+                in_=woven[:, cols, :].rearrange("p c t -> p (c t)"),
+            )
+
+        def product(acc, stat, stat_fmt, block, moving, moving_fmt):
+            cols = slice(block * P, (block + 1) * P)
+            nc.tensor.matmul_mx(
+                out=acc[:],
+                lhsT=stat[0][:, cols].bitcast(stat_fmt),
+                lhsT_scale=stat[1][:, cols],
+                rhs=moving[0][:].bitcast(moving_fmt),
+                rhs_scale=moving[1][:],
+                start=True,
+                stop=True,
+            )
+
+        offsets = keep.tile([P, EXPERTS * LIST_COLS], U16, name="offsets")
+        nc.sync.dma_start(offsets[:], offs)
+
+        def listed(window, b):
+            return window[:].indirect(offsets[:, b * LIST_COLS : (b + 1) * LIST_COLS])
+
+        ident = keep.tile([P, P], F32, name="ident")
+        make_identity(nc, ident[:])
+
+        ts_win = mid([P, TOKENS], "ts_win")
+        tx_win = mid([P, TOKENS], "tx_win")
+        for win, src in ((tx_win, tx), (ts_win, ts)):
+            nc.gpsimd.memset(win[0:ROW, :], 0.0)
+            nc.sync.dma_start(win[ROW:P, :], src[0:1, :])
+
+        out_win = [keep.tile([P, TOKENS], F32, name=f"out_win{j}") for j in range(PACK)]
+        for win in out_win:
+            nc.gpsimd.memset(win[:], 0.0)
+
+        w1_raw = [keep.tile([P, PACK, K], F32, name=f"w1_raw{b}") for b in range(EXPERTS)]
+        w2_raw = [keep.tile([P, PACK, K], F32, name=f"w2_raw{b}") for b in range(EXPERTS)]
+        x_win = [big([P, TOKENS], f"x_win{t}") for t in range(PACK)]
+        dy_win = [big([P, TOKENS], f"dy_win{t}") for t in range(PACK)]
+        cf_col = keep.tile([P, PACK], F32, name="cf_col")
+
+        def load_w1(b):
+            nc.sync.dma_start(w1_raw[b][:], w1[b].rearrange("(p j) f -> p j f", j=PACK))
+
+        def load_w2(b):
+            nc.sync.dma_start(w2_raw[b][:], w2[b].rearrange("(c p) e -> p c e", p=P))
+
+        def load_planes(wins, src):
+            planes = src.rearrange("(p t) n -> t p n", t=PACK)
+            for t in range(PACK):
+                nc.sync.dma_start(wins[t][:], planes[t])
+
+        load_w1(0)
+        with nc.allow_non_contiguous_dma(reason="512 scales, one element to a partition and block"):
+            nc.sync.dma_start(cf_col[:], cf.rearrange("(c p) o -> p (c o)", p=P))
+        load_w2(0)
+        load_planes(x_win, xT)
+        load_planes(dy_win, dyT)
+        load_w1(1)
+        load_w2(1)
+
+        def slot_columns(win, b, name):
+            picked = small(F32, name + "_picked")
+            nc.vector.tensor_copy(picked[:], listed(win, b))
+            turned = bank([P, PACK, P], name + "_turned", "held")
+            for r in range(PACK):
+                nc.tensor.transpose(turned[:, r, :], picked[:, r * P : (r + 1) * P], ident[:])
+            return turned[:, :, ROW]
+
+        half_tx, neg_tx, gate = [], [], []
+        for b in range(EXPERTS):
+            tx_cols = slot_columns(tx_win, b, f"tx{b}")
+            h = keep.tile([P, PACK], F32, name=f"half_tx{b}")
+            n = keep.tile([P, PACK], F32, name=f"neg_tx{b}")
+            nc.scalar.activation(h[:], tx_cols, ACT.Copy, scale=0.5)
+            nc.scalar.activation(n[:], tx_cols, ACT.Copy, scale=-1.0)
+            half_tx.append(h)
+            neg_tx.append(n)
+        for b in range(EXPERTS):
+            ts_cols = slot_columns(ts_win, b, f"ts{b}")
+            g = keep.tile([P, PACK], F32, name=f"gate{b}")
+            neg_ts = keep.tile([P, PACK], F32, name=f"neg_ts{b}")
+            nc.scalar.activation(neg_ts[:], ts_cols, ACT.Copy, scale=-1.0)
+            nc.gpsimd.tensor_tensor(g[:], neg_ts[:], half_tx[b][:], ALU.mult)
+            gate.append(g)
+
+        blocks = [slice(r * P, (r + 1) * P) for r in range(PACK)]
+
+        def weave(planes, name):
+            woven = woven_tile(name)
+            for cols in blocks:
+                nc.scalar.copy(woven[:, cols, :], planes[:, :, cols].rearrange("p t c -> p c t"))
+            return woven
+
+        def quantize_turned(raw, name):
+            woven = woven_tile(name)
+            for c in range(PACK):
+                turned = bank([P, PACK, P], name + "_turned", "weights")
+                for t in range(PACK):
+                    nc.tensor.transpose(turned[:, t, :], raw[:, c, t:K:PACK], ident[:])
+                nc.scalar.copy(woven[:, c * P : (c + 1) * P, :], turned[:].rearrange("p t m -> p m t"))
+            mx = mx_tiles(name)
+            quantize(mx, woven, E4M3)
+            return mx
+
+        def quantize_w1_d(b):
+            mx = mx_tiles(f"w1d{b}")
+            quantize(mx, weave(w1_raw[b], f"w1d{b}"), E4M3)
+            return mx
+
+        def picked_tile(name):
+            return keep.tile([P, PACK, SLOTS], BF16, name=name, align_bytes=ALIGN)
+
+        def gather_planes(wins, b, picked):
+            for t in range(PACK):
+                nc.vector.tensor_copy(picked[:, t, :], listed(wins[t], b))
+
+        slab = [keep.tile([P, 6 * SLOTS], F32, name=f"slab{b}", align_bytes=ALIGN) for b in range(EXPERTS)]
+
+        def factor_of(b, r):
+            return slab[b][:, r * K : (r + 1) * K]
+
+        def da_words_of(b):
+            return slab[b][:, PACK * K : 6 * K]
+
+        w1d0 = quantize_w1_d(0)
+        x_picked = [picked_tile(f"x_picked{b}") for b in range(EXPERTS)]
+        for b in range(EXPERTS):
+            gather_planes(x_win, b, x_picked[b])
+
+        cf_bank = bank([P, PACK, P], "cf_bank", "turned")
+        for c in range(PACK):
+            nc.tensor.transpose(cf_bank[:, c, :], cf_col[:, c : c + 1].to_broadcast([P, P]), ident[:])
+        cf_row = keep.tile([P, K], F32, name="cf_row")
+        nc.scalar.copy(cf_row[:], cf_bank[:].rearrange("p c m -> p (c m)"))
+
+        def slope(b, w1d_b):
+            xq = mx_tiles(f"x{b}")
+            quantize(xq, weave(x_picked[b], f"x{b}"), E4M3)
+            scaled = big([P, PACK, SLOTS], f"scaled{b}")
+            for c in range(PACK):
+                acc = bank([P, SLOTS], "a", "sums")
+                product(acc, w1d_b, E4M3, c, xq, E4M3)
+                nc.scalar.activation(scaled[:, c, :], acc[:], ACT.Copy, scale=cf_col[:, c : c + 1])
+            silu = big([P, PACK, K], f"silu{b}")
+            for r in range(PACK):
+                turned = bank([P, PACK, P], "z", "turned")
+                for c in range(PACK):
+                    nc.tensor.transpose(turned[:, c, :], scaled[:, c, r * P : (r + 1) * P], ident[:])
+                row = turned[:].rearrange("p c m -> p (c m)")
+                nc.scalar.activation(silu[:, r, :], row, ACT.Silu, scale=neg_tx[b][:, r : r + 1])
+                nc.scalar.activation(factor_of(b, r), row, ACT.Tanh, scale=half_tx[b][:, r : r + 1])
+                nc.vector.scalar_tensor_tensor(silu[:, r, :], silu[:, r, :], 1.0, cf_row[:], ALU.subtract, ALU.mult)
+                nc.vector.scalar_tensor_tensor(factor_of(b, r), factor_of(b, r), 1.0, silu[:, r, :], ALU.add, ALU.mult)
+
+        def gradient(b, dy_planes, w2q):
+            dyq = mx_tiles(f"dy{b}")
+            dy_woven = weave(dy_planes, f"dy{b}")
+            da_words = da_words_of(b).rearrange("p (r i u) -> p r i u", r=PACK, u=2)
+            for r in range(PACK):
+                quantize(dyq, dy_woven, E5M2, blocks[r])
+                acc = bank([P, K], "dh", "sums")
+                product(acc, dyq, E5M2, r, w2q, E4M3)
+                da = small(BF16, "da")
+                nc.vector.scalar_tensor_tensor(da[:], acc[:], gate[b][:, r : r + 1], factor_of(b, r), ALU.mult, ALU.mult)
+                words = da[:].bitcast(F32)
+                turned = bank([P, 2, P], "da_turned", "held" if b == 0 else "turned")
+                for u in range(2):
+                    nc.tensor.transpose(turned[:, u, :], words[:, u : K // 2 : 2], ident[:])
+                nc.scalar.copy(da_words[:, r], turned[:].rearrange("p u i -> p i u"))
+            daq = mx_tiles(f"da{b}")
+            nc.vector.quantize_mx(out=daq[0][:].bitcast(E5M2), scales=daq[1][:], in_=da_words_of(b).bitcast(BF16))
+            return daq
+
+        def put(b, j, w1f, daq, staging, tag="sums"):
+            acc = bank([P, SLOTS], "dx", tag)
+            product(acc, w1f, E4M3, j, daq, E5M2)
+            nc.scalar.copy(staging, acc[:])
+            nc.vector.tensor_copy(listed(out_win[j], b), staging)
+
+        slope(0, w1d0)
+        w2q0 = quantize_turned(w2_raw[0], "w2q0")
+        dy_picked0 = picked_tile("dy_picked0")
+        gather_planes(dy_win, 0, dy_picked0)
+        daq0 = gradient(0, dy_picked0, w2q0)
+        w1f0 = quantize_turned(w1_raw[0], "w1f0")
+        dx0 = mid([P, PACK, SLOTS], "dx0")
+        put(0, 0, w1f0, daq0, dx0[:, 0, :])
+        put(0, 1, w1f0, daq0, dx0[:, 1, :])
+
+        dy_picked1 = slab[0][:, 3 * K : 5 * K].bitcast(BF16).rearrange("p (t i) -> p t i", t=PACK)
+        gather_planes(dy_win, 1, dy_picked1)
+        slope(1, quantize_w1_d(1))
+        w2q1 = quantize_turned(w2_raw[1], "w2q1")
+        daq1 = gradient(1, dy_picked1, w2q1)
+        w1f1 = quantize_turned(w1_raw[1], "w1f1")
+        put(0, 2, w1f0, daq0, factor_of(1, 2), "held")
+        put(0, 3, w1f0, daq0, slab[1][:, PACK * K : 5 * K], "held")
+        dx1 = mid([P, PACK, SLOTS], "dx1")
+        rows = out.rearrange("(p j) n -> j p n", j=PACK)
+        for j in range(PACK):
+            put(1, j, w1f1, daq1, dx1[:, j, :])
+            nc.sync.dma_start(rows[j], out_win[j][:])

@@ -6,6 +6,7 @@ from concourse.masks import make_identity
 F32 = mybir.dt.float32
 BF16 = mybir.dt.bfloat16
 U32 = mybir.dt.uint32
+I32 = mybir.dt.int32
 U16 = mybir.dt.uint16
 U8 = mybir.dt.uint8
 E4M3 = mybir.dt.float8_e4m3fn_x4
@@ -22,6 +23,7 @@ TOKENS = 2048
 LIST_COLS = SLOTS // 16
 ROW = P - 1
 ALIGN = 64
+HALF = TOKENS // 2
 
 FLOPS = 3 * EXPERTS * 2 * K * K * SLOTS
 
@@ -30,43 +32,33 @@ def tile_attend_gxfull_sil_x_kernel(tc, xT, dyT, w1, w2, ts, tx, cf, offs, out):
     nc = tc.nc
     with ExitStack() as ctx:
         keep = ctx.enter_context(tc.tile_pool(name="keep", bufs=1))
-        work = ctx.enter_context(tc.tile_pool(name="work", bufs=1))
-        psum = ctx.enter_context(tc.psum_pool(name="psum", bufs=2))
+        psum = ctx.enter_context(tc.psum_pool(name="psum", bufs=1))
 
-        def big(shape, name):
-            return work.tile(shape, F32, name=name, tag="big", bufs=8, align_bytes=ALIGN)
+        def sbuf(shape, dtype, name, tag=None):
+            return keep.tile(shape, dtype, name=name, tag=tag or name, align_bytes=ALIGN)
 
-        def mid(shape, name):
-            return work.tile(shape, F32, name=name, tag="mid", bufs=2, align_bytes=ALIGN)
+        banks = [psum.tile([P, SLOTS], F32, name=f"bank{n}") for n in range(8)]
+        blocks = [slice(r * P, (r + 1) * P) for r in range(PACK)]
 
-        def small(dtype, name):
-            return work.tile([P, SLOTS], dtype, name=name, tag="small", bufs=4, align_bytes=ALIGN)
-
-        def woven_tile(name):
-            return work.tile([P, K, PACK], BF16, name=name, tag="woven", bufs=4, align_bytes=ALIGN)
-
-        def bank(shape, name, tag):
-            return psum.tile(shape, F32, name=name, tag=tag)
+        def quarters(ap):
+            return ap.rearrange("p (a m) -> p a m", m=P)
 
         def mx_tiles(name):
-            codes = keep.tile([P, K], U32, name=name + "_codes", align_bytes=ALIGN)
-            scales = keep.tile([P, K], U8, name=name + "_scales", align_bytes=ALIGN)
-            return codes, scales
+            return sbuf([P, K], U32, name + "_codes"), sbuf([P, K], U8, name + "_scales")
 
         def quantize(mx, woven, fmt, cols=slice(0, K)):
             codes, scales = mx
             nc.vector.quantize_mx(
                 out=codes[:, cols].bitcast(fmt),
                 scales=scales[:, cols],
-                in_=woven[:, cols, :].rearrange("p c t -> p (c t)"),
+                in_=woven[:, PACK * cols.start : PACK * cols.stop],
             )
 
         def product(acc, stat, stat_fmt, block, moving, moving_fmt):
-            cols = slice(block * P, (block + 1) * P)
             nc.tensor.matmul_mx(
                 out=acc[:],
-                lhsT=stat[0][:, cols].bitcast(stat_fmt),
-                lhsT_scale=stat[1][:, cols],
+                lhsT=stat[0][:, blocks[block]].bitcast(stat_fmt),
+                lhsT_scale=stat[1][:, blocks[block]],
                 rhs=moving[0][:].bitcast(moving_fmt),
                 rhs_scale=moving[1][:],
                 start=True,
@@ -77,26 +69,22 @@ def tile_attend_gxfull_sil_x_kernel(tc, xT, dyT, w1, w2, ts, tx, cf, offs, out):
         nc.sync.dma_start(offsets[:], offs)
 
         def listed(window, b):
-            return window[:].indirect(offsets[:, b * LIST_COLS : (b + 1) * LIST_COLS])
+            return window.indirect(offsets[:, b * LIST_COLS : (b + 1) * LIST_COLS])
 
-        ident = keep.tile([P, P], F32, name="ident")
+        ident = sbuf([P, P], F32, "ident")
         make_identity(nc, ident[:])
 
-        ts_win = mid([P, TOKENS], "ts_win")
-        tx_win = mid([P, TOKENS], "tx_win")
+        tx_win = sbuf([P, TOKENS], F32, "tx_win")
+        ts_win = sbuf([P, TOKENS], F32, "ts_win")
         for win, src in ((tx_win, tx), (ts_win, ts)):
-            nc.gpsimd.memset(win[0:ROW, :], 0.0)
+            nc.vector.memset(win[0:ROW, :], 0.0)
             nc.sync.dma_start(win[ROW:P, :], src[0:1, :])
 
-        out_win = [keep.tile([P, TOKENS], F32, name=f"out_win{j}") for j in range(PACK)]
-        for win in out_win:
-            nc.gpsimd.memset(win[:], 0.0)
-
-        w1_raw = [keep.tile([P, PACK, K], F32, name=f"w1_raw{b}") for b in range(EXPERTS)]
-        w2_raw = [keep.tile([P, PACK, K], F32, name=f"w2_raw{b}") for b in range(EXPERTS)]
-        x_win = [big([P, TOKENS], f"x_win{t}") for t in range(PACK)]
-        dy_win = [big([P, TOKENS], f"dy_win{t}") for t in range(PACK)]
-        cf_col = keep.tile([P, PACK], F32, name="cf_col")
+        w1_raw = [sbuf([P, PACK, K], F32, f"w1_raw{b}") for b in range(EXPERTS)]
+        w2_raw = [sbuf([P, PACK, K], F32, f"w2_raw{b}") for b in range(EXPERTS)]
+        x_raw = [[sbuf([P, 2, HALF], F32, f"x_raw{u}{h}") for h in range(2)] for u in range(2)]
+        dy_win = [sbuf([P, TOKENS], F32, f"dy_win{t}") for t in range(PACK)]
+        cf_col = sbuf([P, PACK], F32, "cf_col")
 
         def load_w1(b):
             nc.sync.dma_start(w1_raw[b][:], w1[b].rearrange("(p j) f -> p j f", j=PACK))
@@ -104,159 +92,214 @@ def tile_attend_gxfull_sil_x_kernel(tc, xT, dyT, w1, w2, ts, tx, cf, offs, out):
         def load_w2(b):
             nc.sync.dma_start(w2_raw[b][:], w2[b].rearrange("(c p) e -> p c e", p=P))
 
-        def load_planes(wins, src):
-            planes = src.rearrange("(p t) n -> t p n", t=PACK)
-            for t in range(PACK):
-                nc.sync.dma_start(wins[t][:], planes[t])
+        def load_x(u):
+            pairs = xT.rearrange("(p u e) n -> u p e n", u=2, e=2)
+            for h in range(2):
+                nc.sync.dma_start(x_raw[u][h][:], pairs[u][:, :, h * HALF : (h + 1) * HALF])
 
-        load_w1(0)
+        load_x(0)
         with nc.allow_non_contiguous_dma(reason="512 scales, one element to a partition and block"):
             nc.sync.dma_start(cf_col[:], cf.rearrange("(c p) o -> p (c o)", p=P))
+        load_w1(0)
+        load_x(1)
         load_w2(0)
-        load_planes(x_win, xT)
-        load_planes(dy_win, dyT)
+        dy_planes = dyT.rearrange("(p t) n -> t p n", t=PACK)
+        for t in range(PACK):
+            nc.sync.dma_start(dy_win[t][:], dy_planes[t])
         load_w1(1)
         load_w2(1)
 
-        def slot_columns(win, b, name):
-            picked = small(F32, name + "_picked")
-            nc.vector.tensor_copy(picked[:], listed(win, b))
-            turned = bank([P, PACK, P], name + "_turned", "held")
+        x_win = [sbuf([P, 2 * TOKENS], BF16, f"x_win{u}") for u in range(2)]
+
+        def pair_x(u):
+            for h in range(2):
+                paired = x_win[u][:, 2 * h * HALF : 2 * (h + 1) * HALF].rearrange("p (n e) -> p n e", e=2)
+                nc.scalar.activation(paired, x_raw[u][h][:].rearrange("p e n -> p n e"), ACT.Copy)
+
+        pair_x(0)
+
+        picked_scales = sbuf([P, 2 * EXPERTS * SLOTS], F32, "picked_scales")
+
+        def slot_columns(win, b, n):
+            picked = picked_scales[:, n * SLOTS : (n + 1) * SLOTS]
+            nc.vector.tensor_copy(picked, listed(win[:], b))
             for r in range(PACK):
-                nc.tensor.transpose(turned[:, r, :], picked[:, r * P : (r + 1) * P], ident[:])
-            return turned[:, :, ROW]
+                nc.tensor.transpose(banks[n][:, blocks[r]], picked[:, blocks[r]], ident[:])
+            return quarters(banks[n][:])[:, :, ROW]
 
         half_tx, neg_tx, gate = [], [], []
         for b in range(EXPERTS):
-            tx_cols = slot_columns(tx_win, b, f"tx{b}")
-            h = keep.tile([P, PACK], F32, name=f"half_tx{b}")
-            n = keep.tile([P, PACK], F32, name=f"neg_tx{b}")
-            nc.scalar.activation(h[:], tx_cols, ACT.Copy, scale=0.5)
-            nc.scalar.activation(n[:], tx_cols, ACT.Copy, scale=-1.0)
+            tx_cols = slot_columns(tx_win, b, 2 * b)
+            ts_cols = slot_columns(ts_win, b, 2 * b + 1)
+            h = sbuf([P, PACK], F32, f"half_tx{b}")
+            n = sbuf([P, PACK], F32, f"neg_tx{b}")
+            g = sbuf([P, PACK], F32, f"gate{b}")
+            nc.vector.tensor_scalar_mul(h[:], tx_cols, 0.5)
+            nc.vector.tensor_scalar_mul(n[:], tx_cols, -1.0)
+            nc.vector.scalar_tensor_tensor(g[:], ts_cols, -1.0, h[:], ALU.mult, ALU.mult)
             half_tx.append(h)
             neg_tx.append(n)
-        for b in range(EXPERTS):
-            ts_cols = slot_columns(ts_win, b, f"ts{b}")
-            g = keep.tile([P, PACK], F32, name=f"gate{b}")
-            neg_ts = keep.tile([P, PACK], F32, name=f"neg_ts{b}")
-            nc.scalar.activation(neg_ts[:], ts_cols, ACT.Copy, scale=-1.0)
-            nc.gpsimd.tensor_tensor(g[:], neg_ts[:], half_tx[b][:], ALU.mult)
             gate.append(g)
 
-        blocks = [slice(r * P, (r + 1) * P) for r in range(PACK)]
+        for c in range(PACK):
+            nc.tensor.transpose(banks[4][:, blocks[c]], cf_col[:, c : c + 1].to_broadcast([P, P]), ident[:])
+        cf_row = sbuf([P, K], F32, "cf_row")
+        nc.vector.tensor_copy(cf_row[:], banks[4][:])
 
-        def weave(planes, name):
-            woven = woven_tile(name)
-            for cols in blocks:
-                nc.scalar.copy(woven[:, cols, :], planes[:, :, cols].rearrange("p t c -> p c t"))
-            return woven
+        out_win = [sbuf([P, TOKENS], F32, "out_win0"), sbuf([P, TOKENS], F32, "out_win1")]
+        out_win.append(sbuf([P, TOKENS], F32, "out_win2", tag="tx_win"))
+        for win in out_win:
+            nc.vector.memset(win[:], 0.0)
 
-        def quantize_turned(raw, name):
-            woven = woven_tile(name)
-            for c in range(PACK):
-                turned = bank([P, PACK, P], name + "_turned", "weights")
-                for t in range(PACK):
-                    nc.tensor.transpose(turned[:, t, :], raw[:, c, t:K:PACK], ident[:])
-                nc.scalar.copy(woven[:, c * P : (c + 1) * P, :], turned[:].rearrange("p t m -> p m t"))
-            mx = mx_tiles(name)
-            quantize(mx, woven, E4M3)
-            return mx
+        x_words = sbuf([P, 2, EXPERTS * SLOTS], U32, "x_words")
+        nc.vector.tensor_copy(x_words[:, 0, :], x_win[0][:].bitcast(U32).indirect(offsets[:]))
 
-        def quantize_w1_d(b):
-            mx = mx_tiles(f"w1d{b}")
-            quantize(mx, weave(w1_raw[b], f"w1d{b}"), E4M3)
-            return mx
+        woven = [sbuf([P, PACK * K], BF16, f"woven{n}") for n in range(3)]
 
-        def picked_tile(name):
-            return keep.tile([P, PACK, SLOTS], BF16, name=name, align_bytes=ALIGN)
+        def weave(engine_copy, dst, planes, cols):
+            engine_copy(
+                dst[:, PACK * cols.start : PACK * cols.stop].rearrange("p (c t) -> p c t", t=PACK),
+                planes[:, :, cols].rearrange("p t c -> p c t"),
+            )
 
-        def gather_planes(wins, b, picked):
+        def turn_block(raw, c, dst, bank):
             for t in range(PACK):
-                nc.vector.tensor_copy(picked[:, t, :], listed(wins[t], b))
+                nc.tensor.transpose(bank[:, blocks[t]], raw[:, c, t:K:PACK], ident[:])
+            weave(nc.scalar.copy, dst, quarters(bank[:]), slice(0, P))
 
-        slab = [keep.tile([P, 6 * SLOTS], F32, name=f"slab{b}", align_bytes=ALIGN) for b in range(EXPERTS)]
+        def turn_weights(raw, dst, use):
+            for c in range(PACK):
+                turn_block(raw, c, dst[:, c * K : (c + 1) * K], use[c])
+
+        def quantized(name, src, fmt):
+            mx = mx_tiles(name)
+            quantize(mx, src, fmt)
+            return mx
+
+        weave(nc.vector.tensor_copy, woven[0], w1_raw[0], slice(0, K))
+        w1d0 = quantized("w1d0", woven[0], E4M3)
+        turn_block(w1_raw[0], 0, woven[1][:, 0:K], banks[5])
+
+        pair_x(1)
+        out_win.append(sbuf([P, TOKENS], F32, "out_win3", tag="x_raw10"))
+        nc.vector.memset(out_win[3][:], 0.0)
+        for b in range(EXPERTS):
+            nc.vector.tensor_copy(x_words[:, 1, b * SLOTS : (b + 1) * SLOTS], listed(x_win[1][:].bitcast(U32), b))
+
+        def weave_x(b, dst):
+            words = x_words[:, :, b * SLOTS : (b + 1) * SLOTS].rearrange("p u i -> p i u")
+            nc.scalar.copy(dst.bitcast(U32).rearrange("p (i u) -> p i u", u=2), words)
+
+        slab = [sbuf([P, 8 * K], F32, "slab0"), sbuf([P, 6 * K], F32, "slab1")]
+        factor_at = [(0, 1, 2, 5), (0, 1, 2, 3)]
 
         def factor_of(b, r):
-            return slab[b][:, r * K : (r + 1) * K]
+            return slab[b][:, factor_at[b][r] * K : (factor_at[b][r] + 1) * K]
 
         def da_words_of(b):
-            return slab[b][:, PACK * K : 6 * K]
+            return slab[b][:, (factor_at[b][3] + 1) * K : (factor_at[b][3] + 3) * K]
 
-        w1d0 = quantize_w1_d(0)
-        x_picked = [picked_tile(f"x_picked{b}") for b in range(EXPERTS)]
-        for b in range(EXPERTS):
-            gather_planes(x_win, b, x_picked[b])
-
-        cf_bank = bank([P, PACK, P], "cf_bank", "turned")
-        for c in range(PACK):
-            nc.tensor.transpose(cf_bank[:, c, :], cf_col[:, c : c + 1].to_broadcast([P, P]), ident[:])
-        cf_row = keep.tile([P, K], F32, name="cf_row")
-        nc.scalar.copy(cf_row[:], cf_bank[:].rearrange("p c m -> p (c m)"))
-
-        def slope(b, w1d_b):
-            xq = mx_tiles(f"x{b}")
-            quantize(xq, weave(x_picked[b], f"x{b}"), E4M3)
-            scaled = big([P, PACK, SLOTS], f"scaled{b}")
+        def first_product(w1d, xq, scaled, use):
             for c in range(PACK):
-                acc = bank([P, SLOTS], "a", "sums")
-                product(acc, w1d_b, E4M3, c, xq, E4M3)
-                nc.scalar.activation(scaled[:, c, :], acc[:], ACT.Copy, scale=cf_col[:, c : c + 1])
-            silu = big([P, PACK, K], f"silu{b}")
-            for r in range(PACK):
-                turned = bank([P, PACK, P], "z", "turned")
-                for c in range(PACK):
-                    nc.tensor.transpose(turned[:, c, :], scaled[:, c, r * P : (r + 1) * P], ident[:])
-                row = turned[:].rearrange("p c m -> p (c m)")
-                nc.scalar.activation(silu[:, r, :], row, ACT.Silu, scale=neg_tx[b][:, r : r + 1])
-                nc.scalar.activation(factor_of(b, r), row, ACT.Tanh, scale=half_tx[b][:, r : r + 1])
-                nc.vector.scalar_tensor_tensor(silu[:, r, :], silu[:, r, :], 1.0, cf_row[:], ALU.subtract, ALU.mult)
-                nc.vector.scalar_tensor_tensor(factor_of(b, r), factor_of(b, r), 1.0, silu[:, r, :], ALU.add, ALU.mult)
+                product(use[c], w1d, E4M3, c, xq, E4M3)
+                nc.scalar.activation(scaled[:, c, :], use[c][:], ACT.Copy, scale=cf_col[:, c : c + 1])
 
-        def gradient(b, dy_planes, w2q):
+        def slope(b, scaled, silu, use):
+            for r in range(PACK):
+                for c in range(PACK):
+                    nc.tensor.transpose(use[r][:, blocks[c]], scaled[:, c, blocks[r]], ident[:])
+                nc.scalar.activation(silu[:, r, :], use[r][:], ACT.Silu, scale=neg_tx[b][:, r : r + 1])
+                nc.scalar.activation(factor_of(b, r), use[r][:], ACT.Tanh, scale=half_tx[b][:, r : r + 1])
+            for r in range(PACK):
+                nc.vector.scalar_tensor_tensor(silu[:, r, :], silu[:, r, :], 1.0, cf_row[:], ALU.subtract, ALU.mult)
+                if r > 0:
+                    finish_factor(b, silu, r - 1)
+            finish_factor(b, silu, PACK - 1)
+
+        def finish_factor(b, silu, r):
+            nc.vector.scalar_tensor_tensor(factor_of(b, r), factor_of(b, r), 1.0, silu[:, r, :], ALU.add, ALU.mult)
+
+        def gather_dy(b, picked, ts_range):
+            for t in ts_range:
+                nc.vector.tensor_copy(picked[:, t, :], listed(dy_win[t][:], b))
+
+        def gradient(b, dy_picked, dy_woven, w2q, da, sums):
             dyq = mx_tiles(f"dy{b}")
-            dy_woven = weave(dy_planes, f"dy{b}")
             da_words = da_words_of(b).rearrange("p (r i u) -> p r i u", r=PACK, u=2)
             for r in range(PACK):
+                weave(nc.scalar.copy, dy_woven, dy_picked, blocks[r])
                 quantize(dyq, dy_woven, E5M2, blocks[r])
-                acc = bank([P, K], "dh", "sums")
-                product(acc, dyq, E5M2, r, w2q, E4M3)
-                da = small(BF16, "da")
-                nc.vector.scalar_tensor_tensor(da[:], acc[:], gate[b][:, r : r + 1], factor_of(b, r), ALU.mult, ALU.mult)
-                words = da[:].bitcast(F32)
-                turned = bank([P, 2, P], "da_turned", "held" if b == 0 else "turned")
+                product(sums[r], dyq, E5M2, r, w2q, E4M3)
+            for r in range(PACK):
+                rounded = da[:, r * K : (r + 1) * K]
+                nc.vector.scalar_tensor_tensor(rounded, sums[r][:], gate[b][:, r : r + 1], factor_of(b, r), ALU.mult, ALU.mult)
+                words = rounded.bitcast(F32)
                 for u in range(2):
-                    nc.tensor.transpose(turned[:, u, :], words[:, u : K // 2 : 2], ident[:])
-                nc.scalar.copy(da_words[:, r], turned[:].rearrange("p u i -> p i u"))
-            daq = mx_tiles(f"da{b}")
-            nc.vector.quantize_mx(out=daq[0][:].bitcast(E5M2), scales=daq[1][:], in_=da_words_of(b).bitcast(BF16))
-            return daq
+                    nc.tensor.transpose(sums[r][:, blocks[u]], words[:, u : K // 2 : 2], ident[:])
+                nc.scalar.copy(da_words[:, r], quarters(sums[r][:, 0 : 2 * P]).rearrange("p u i -> p i u"))
+            return quantized(f"da{b}", da_words_of(b).bitcast(BF16), E5M2)
 
-        def put(b, j, w1f, daq, staging, tag="sums"):
-            acc = bank([P, SLOTS], "dx", tag)
+        def last_product(j, w1f, daq, acc, staging):
             product(acc, w1f, E4M3, j, daq, E5M2)
             nc.scalar.copy(staging, acc[:])
-            nc.vector.tensor_copy(listed(out_win[j], b), staging)
 
-        slope(0, w1d0)
-        w2q0 = quantize_turned(w2_raw[0], "w2q0")
-        dy_picked0 = picked_tile("dy_picked0")
-        gather_planes(dy_win, 0, dy_picked0)
-        daq0 = gradient(0, dy_picked0, w2q0)
-        w1f0 = quantize_turned(w1_raw[0], "w1f0")
-        dx0 = mid([P, PACK, SLOTS], "dx0")
-        put(0, 0, w1f0, daq0, dx0[:, 0, :])
-        put(0, 1, w1f0, daq0, dx0[:, 1, :])
+        def put(b, window, staging):
+            nc.vector.tensor_copy(listed(window[:], b), staging)
 
-        dy_picked1 = slab[0][:, 3 * K : 5 * K].bitcast(BF16).rearrange("p (t i) -> p t i", t=PACK)
-        gather_planes(dy_win, 1, dy_picked1)
-        slope(1, quantize_w1_d(1))
-        w2q1 = quantize_turned(w2_raw[1], "w2q1")
-        daq1 = gradient(1, dy_picked1, w2q1)
-        w1f1 = quantize_turned(w1_raw[1], "w1f1")
-        put(0, 2, w1f0, daq0, factor_of(1, 2), "held")
-        put(0, 3, w1f0, daq0, slab[1][:, PACK * K : 5 * K], "held")
-        dx1 = mid([P, PACK, SLOTS], "dx1")
+        low, high = banks[0:4], banks[4:8]
+
+        x_woven0 = slab[0][:, 3 * K : 5 * K].bitcast(BF16)
+        weave_x(0, x_woven0)
+        xq0 = quantized("x0", x_woven0, E4M3)
+        late = sbuf([P, PACK * K], BF16, "late", tag="x_raw11")
+        for c in range(1, PACK):
+            turn_block(w1_raw[0], c, late[:, c * K : (c + 1) * K], banks[(5, 6, 7, 4)[c]])
+        w1f0 = mx_tiles("w1f0")
+        quantize(w1f0, woven[1], E4M3, blocks[0])
+        quantize(w1f0, late, E4M3, blocks[1])
+        quantize(w1f0, late, E4M3, slice(2 * P, K))
+        scaled0 = sbuf([P, PACK, SLOTS], F32, "scaled0", tag="x_raw00")
+        first_product(w1d0, xq0, scaled0, low)
+        turn_weights(w2_raw[0], woven[2], [banks[5], banks[6], banks[0], banks[1]])
+        w2q0 = quantized("w2q0", woven[2], E4M3)
+        dy_picked0 = late[:].rearrange("p (t i) -> p t i", t=PACK)
+        gather_dy(0, dy_picked0, range(PACK))
+        dy_picked1 = slab[0][:, 3 * K : 7 * K].bitcast(BF16).rearrange("p (t i) -> p t i", t=PACK)[:, :, 0:SLOTS]
+        gather_dy(1, dy_picked1, range(2))
+        silu0 = sbuf([P, PACK, K], F32, "silu0", tag="x_raw01")
+        slope(0, scaled0, silu0, [banks[7], banks[4], banks[2], banks[3]])
+        da = sbuf([P, PACK * K], BF16, "da", tag="picked_scales")
+        daq0 = gradient(0, dy_picked0, woven[1], w2q0, da, [banks[5], banks[6], banks[7], banks[4]])
+        dx0 = sbuf([P, 2, SLOTS], F32, "dx0", tag="w1_raw0")
+
+        gather_dy(1, dy_picked1, range(2, PACK))
+        last_product(0, w1f0, daq0, banks[0], dx0[:, 0, :])
+        put(0, out_win[0], dx0[:, 0, :])
+
+        weave_x(1, late[:])
+        xq1 = quantized("x1", late, E4M3)
+        for cols in blocks:
+            weave(nc.scalar.copy, woven[1], w1_raw[1], cols)
+        w1d1 = quantized("w1d1", woven[1], E4M3)
+        turn_weights(w1_raw[1], woven[0], [banks[1], banks[2], banks[3], banks[1]])
+        w1f1 = quantized("w1f1", woven[0], E4M3)
+        scaled1 = sbuf([P, PACK, SLOTS], F32, "scaled1", tag="x_raw11")
+        first_product(w1d1, xq1, scaled1, [banks[2], banks[3], banks[1], banks[2]])
+        last_product(1, w1f0, daq0, banks[0], dx0[:, 1, :])
+        put(0, out_win[1], dx0[:, 1, :])
+        silu1 = sbuf([P, PACK, K], F32, "silu1", tag="x_win0")
+        slope(1, scaled1, silu1, high)
+        turn_weights(w2_raw[1], woven[1], low)
+        w2q1 = quantized("w2q1", woven[1], E4M3)
+        daq1 = gradient(1, dy_picked1, woven[2], w2q1, da, high)
+        last_product(2, w1f0, daq0, low[0], factor_of(1, 1))
+        put(0, out_win[2], factor_of(1, 1))
+        last_product(3, w1f0, daq0, low[1], slab[1][:, PACK * K : 5 * K])
+        put(0, out_win[3], slab[1][:, PACK * K : 5 * K])
+
+        dx1 = sbuf([P, PACK, SLOTS], F32, "dx1", tag="ts_win")
         rows = out.rearrange("(p j) n -> j p n", j=PACK)
         for j in range(PACK):
-            put(1, j, w1f1, daq1, dx1[:, j, :])
+            last_product(j, w1f1, daq1, (low[2], low[3], high[0], high[1])[j], dx1[:, j, :])
+            put(1, out_win[j], dx1[:, j, :])
             nc.sync.dma_start(rows[j], out_win[j][:])

@@ -24,6 +24,7 @@ LIST_COLS = SLOTS // 16
 ROW = P - 1
 ALIGN = 64
 HALF = TOKENS // 2
+SPLIT = HALF // 2
 
 FLOPS = 3 * EXPERTS * 2 * K * K * SLOTS
 
@@ -77,7 +78,7 @@ def tile_attend_gxfull_sil_x_kernel(tc, xT, dyT, w1, w2, ts, tx, cf, offs, out):
         tx_win = sbuf([P, TOKENS], F32, "tx_win")
         ts_win = sbuf([P, TOKENS], F32, "ts_win")
         for win, src in ((tx_win, tx), (ts_win, ts)):
-            nc.vector.memset(win[0:ROW, :], 0.0)
+            nc.vector.memset(win[0:ROW, :].bitcast(I32), 0)
             nc.sync.dma_start(win[ROW:P, :], src[0:1, :])
 
         w1_raw = [sbuf([P, PACK, K], F32, f"w1_raw{b}") for b in range(EXPERTS)]
@@ -111,12 +112,13 @@ def tile_attend_gxfull_sil_x_kernel(tc, xT, dyT, w1, w2, ts, tx, cf, offs, out):
 
         x_win = [sbuf([P, 2 * TOKENS], BF16, f"x_win{u}") for u in range(2)]
 
-        def pair_x(u):
-            for h in range(2):
-                paired = x_win[u][:, 2 * h * HALF : 2 * (h + 1) * HALF].rearrange("p (n e) -> p n e", e=2)
-                nc.scalar.activation(paired, x_raw[u][h][:].rearrange("p e n -> p n e"), ACT.Copy)
+        def paired(u, h, cols):
+            first = h * HALF
+            dst = x_win[u][:, 2 * (first + cols.start) : 2 * (first + cols.stop)].rearrange("p (n e) -> p n e", e=2)
+            return dst, x_raw[u][h][:, :, cols].rearrange("p e n -> p n e")
 
-        pair_x(0)
+        for h in range(2):
+            nc.scalar.activation(*paired(0, h, slice(0, HALF)), ACT.Copy)
 
         picked_scales = sbuf([P, 2 * EXPERTS * SLOTS], F32, "picked_scales")
 
@@ -141,20 +143,24 @@ def tile_attend_gxfull_sil_x_kernel(tc, xT, dyT, w1, w2, ts, tx, cf, offs, out):
             neg_tx.append(n)
             gate.append(g)
 
-        for c in range(PACK):
-            nc.tensor.transpose(banks[4][:, blocks[c]], cf_col[:, c : c + 1].to_broadcast([P, P]), ident[:])
-        cf_row = sbuf([P, K], F32, "cf_row")
-        nc.vector.tensor_copy(cf_row[:], banks[4][:])
-
         out_win = [sbuf([P, TOKENS], F32, "out_win0"), sbuf([P, TOKENS], F32, "out_win1")]
         out_win.append(sbuf([P, TOKENS], F32, "out_win2", tag="tx_win"))
+        out_win.append(sbuf([P, TOKENS], F32, "out_win3", tag="ts_win"))
         for win in out_win:
-            nc.vector.memset(win[:], 0.0)
+            nc.vector.memset(win[:].bitcast(I32), 0)
+
+        slab = [sbuf([P, 10 * K], F32, "slab0"), sbuf([P, 6 * K], F32, "slab1")]
+        factor_at = [(0, 1, 6, 7), (0, 1, 2, 3)]
+        woven = [sbuf([P, PACK * K], BF16, f"woven{n}") for n in range(3)]
+        x_woven = slab[0][:, 2 * K : 6 * K]
 
         x_words = sbuf([P, 2, EXPERTS * SLOTS], U32, "x_words")
         nc.vector.tensor_copy(x_words[:, 0, :], x_win[0][:].bitcast(U32).indirect(offsets[:]))
 
-        woven = [sbuf([P, PACK * K], BF16, f"woven{n}") for n in range(3)]
+        for c in range(PACK):
+            nc.tensor.transpose(banks[3][:, blocks[c]], cf_col[:, c : c + 1].to_broadcast([P, P]), ident[:])
+        cf_row = sbuf([P, K], F32, "cf_row")
+        nc.vector.tensor_copy(cf_row[:], banks[3][:])
 
         def weave(engine_copy, dst, planes, cols):
             engine_copy(
@@ -176,25 +182,22 @@ def tile_attend_gxfull_sil_x_kernel(tc, xT, dyT, w1, w2, ts, tx, cf, offs, out):
             quantize(mx, src, fmt)
             return mx
 
-        weave(nc.vector.tensor_copy, woven[0], w1_raw[0], slice(0, K))
+        for cols in blocks:
+            weave(nc.scalar.copy, woven[0], w1_raw[0], cols)
         w1d0 = quantized("w1d0", woven[0], E4M3)
-        turn_block(w1_raw[0], 0, woven[1][:, 0:K], banks[5])
-
-        pair_x(1)
-        out_win.append(sbuf([P, TOKENS], F32, "out_win3", tag="x_raw10"))
-        nc.vector.memset(out_win[3][:], 0.0)
+        nc.scalar.activation(*paired(1, 0, slice(0, HALF)), ACT.Copy)
+        nc.scalar.activation(*paired(1, 1, slice(0, SPLIT)), ACT.Copy)
+        nc.vector.tensor_copy(*paired(1, 1, slice(SPLIT, HALF)))
         for b in range(EXPERTS):
-            nc.vector.tensor_copy(x_words[:, 1, b * SLOTS : (b + 1) * SLOTS], listed(x_win[1][:].bitcast(U32), b))
+            slots = slice(b * SLOTS, (b + 1) * SLOTS)
+            nc.vector.tensor_copy(x_words[:, 1, slots], listed(x_win[1][:].bitcast(U32), b))
+            nc.scalar.copy(
+                x_woven.bitcast(U32).rearrange("p (i u) -> p i u", u=2)[:, slots, :],
+                x_words[:, :, slots].rearrange("p u i -> p i u"),
+            )
 
-        def weave_x(b, dst):
-            words = x_words[:, :, b * SLOTS : (b + 1) * SLOTS].rearrange("p u i -> p i u")
-            nc.scalar.copy(dst.bitcast(U32).rearrange("p (i u) -> p i u", u=2), words)
-
-        slab = [sbuf([P, 8 * K], F32, "slab0"), sbuf([P, 6 * K], F32, "slab1")]
-        factor_at = [(0, 1, 2, 5), (0, 1, 2, 3)]
-
-        def factor_of(b, r):
-            return slab[b][:, factor_at[b][r] * K : (factor_at[b][r] + 1) * K]
+        def factor_of(b, r, count=1):
+            return slab[b][:, factor_at[b][r] * K : (factor_at[b][r] + count) * K]
 
         def da_words_of(b):
             return slab[b][:, (factor_at[b][3] + 1) * K : (factor_at[b][3] + 3) * K]
@@ -210,14 +213,12 @@ def tile_attend_gxfull_sil_x_kernel(tc, xT, dyT, w1, w2, ts, tx, cf, offs, out):
                     nc.tensor.transpose(use[r][:, blocks[c]], scaled[:, c, blocks[r]], ident[:])
                 nc.scalar.activation(silu[:, r, :], use[r][:], ACT.Silu, scale=neg_tx[b][:, r : r + 1])
                 nc.scalar.activation(factor_of(b, r), use[r][:], ACT.Tanh, scale=half_tx[b][:, r : r + 1])
-            for r in range(PACK):
-                nc.vector.scalar_tensor_tensor(silu[:, r, :], silu[:, r, :], 1.0, cf_row[:], ALU.subtract, ALU.mult)
-                if r > 0:
-                    finish_factor(b, silu, r - 1)
-            finish_factor(b, silu, PACK - 1)
-
-        def finish_factor(b, silu, r):
-            nc.vector.scalar_tensor_tensor(factor_of(b, r), factor_of(b, r), 1.0, silu[:, r, :], ALU.add, ALU.mult)
+            cf_twice = cf_row[:].unsqueeze(1).to_broadcast([P, 2, K])
+            for r in (0, 2):
+                pair = silu[:, r : r + 2, :]
+                nc.vector.scalar_tensor_tensor(pair, pair, 1.0, cf_twice, ALU.subtract, ALU.mult)
+                factor = factor_of(b, r, 2)
+                nc.vector.scalar_tensor_tensor(factor, factor, 1.0, pair.rearrange("p r f -> p (r f)"), ALU.add, ALU.mult)
 
         def gather_dy(b, picked, ts_range):
             for t in ts_range:
@@ -248,56 +249,53 @@ def tile_attend_gxfull_sil_x_kernel(tc, xT, dyT, w1, w2, ts, tx, cf, offs, out):
 
         low, high = banks[0:4], banks[4:8]
 
-        x_woven0 = slab[0][:, 3 * K : 5 * K].bitcast(BF16)
-        weave_x(0, x_woven0)
-        xq0 = quantized("x0", x_woven0, E4M3)
+        xq0 = quantized("x0", x_woven[:, 0 : 2 * K].bitcast(BF16), E4M3)
+        xq1 = quantized("x1", x_woven[:, 2 * K : 4 * K].bitcast(BF16), E4M3)
         late = sbuf([P, PACK * K], BF16, "late", tag="x_raw11")
-        for c in range(1, PACK):
-            turn_block(w1_raw[0], c, late[:, c * K : (c + 1) * K], banks[(5, 6, 7, 4)[c]])
-        w1f0 = mx_tiles("w1f0")
-        quantize(w1f0, woven[1], E4M3, blocks[0])
-        quantize(w1f0, late, E4M3, blocks[1])
-        quantize(w1f0, late, E4M3, slice(2 * P, K))
-        scaled0 = sbuf([P, PACK, SLOTS], F32, "scaled0", tag="x_raw00")
-        first_product(w1d0, xq0, scaled0, low)
-        turn_weights(w2_raw[0], woven[2], [banks[5], banks[6], banks[0], banks[1]])
+        turn_weights(w1_raw[0], late, low)
+        w1f0 = quantized("w1f0", late, E4M3)
+        turn_weights(w2_raw[0], woven[2], low)
         w2q0 = quantized("w2q0", woven[2], E4M3)
-        dy_picked0 = late[:].rearrange("p (t i) -> p t i", t=PACK)
-        gather_dy(0, dy_picked0, range(PACK))
-        dy_picked1 = slab[0][:, 3 * K : 7 * K].bitcast(BF16).rearrange("p (t i) -> p t i", t=PACK)[:, :, 0:SLOTS]
-        gather_dy(1, dy_picked1, range(2))
+        scaled0 = sbuf([P, PACK, SLOTS], F32, "scaled0", tag="x_raw00")
+        first_product(w1d0, xq0, scaled0, high)
+        dy_picked0 = slab[0][:, 2 * K : 6 * K].bitcast(BF16).rearrange("p (t i) -> p t i", t=PACK)[:, :, SLOTS : 2 * SLOTS]
+        dy_picked1 = slab[0][:, 2 * K : 10 * K].bitcast(BF16).rearrange("p (t i) -> p t i", t=PACK)[:, :, 0:SLOTS]
+        for t in range(PACK):
+            gather_dy(0, dy_picked0, [t])
+            if t < 2:
+                gather_dy(1, dy_picked1, [t])
         silu0 = sbuf([P, PACK, K], F32, "silu0", tag="x_raw01")
-        slope(0, scaled0, silu0, [banks[7], banks[4], banks[2], banks[3]])
+        slope(0, scaled0, silu0, low)
         da = sbuf([P, PACK * K], BF16, "da", tag="picked_scales")
-        daq0 = gradient(0, dy_picked0, woven[1], w2q0, da, [banks[5], banks[6], banks[7], banks[4]])
+        dy_woven0 = sbuf([P, PACK * K], BF16, "dy_woven0", tag="x_raw00")
+        daq0 = gradient(0, dy_picked0, dy_woven0, w2q0, da, high)
         dx0 = sbuf([P, 2, SLOTS], F32, "dx0", tag="w1_raw0")
 
         gather_dy(1, dy_picked1, range(2, PACK))
-        last_product(0, w1f0, daq0, banks[0], dx0[:, 0, :])
-        put(0, out_win[0], dx0[:, 0, :])
-
-        weave_x(1, late[:])
-        xq1 = quantized("x1", late, E4M3)
-        for cols in blocks:
-            weave(nc.scalar.copy, woven[1], w1_raw[1], cols)
-        w1d1 = quantized("w1d1", woven[1], E4M3)
-        turn_weights(w1_raw[1], woven[0], [banks[1], banks[2], banks[3], banks[1]])
-        w1f1 = quantized("w1f1", woven[0], E4M3)
-        scaled1 = sbuf([P, PACK, SLOTS], F32, "scaled1", tag="x_raw11")
-        first_product(w1d1, xq1, scaled1, [banks[2], banks[3], banks[1], banks[2]])
-        last_product(1, w1f0, daq0, banks[0], dx0[:, 1, :])
-        put(0, out_win[1], dx0[:, 1, :])
-        silu1 = sbuf([P, PACK, K], F32, "silu1", tag="x_win0")
-        slope(1, scaled1, silu1, high)
         turn_weights(w2_raw[1], woven[1], low)
         w2q1 = quantized("w2q1", woven[1], E4M3)
-        daq1 = gradient(1, dy_picked1, woven[2], w2q1, da, high)
+        for j in range(2):
+            last_product(j, w1f0, daq0, banks[j], dx0[:, j, :])
+            put(0, out_win[j], dx0[:, j, :])
+
+        for cols in blocks:
+            weave(nc.scalar.copy, dy_woven0, w1_raw[1], cols)
+        w1d1 = sbuf([P, K], U32, "w1d1_codes"), daq0[1][PACK:P, :]
+        quantize(w1d1, dy_woven0, E4M3)
+        scaled1 = sbuf([P, PACK, SLOTS], F32, "scaled1", tag="x_raw01")
+        first_product(w1d1, xq1, scaled1, [banks[2], banks[3], banks[0], banks[1]])
+        silu1 = sbuf([P, PACK, K], F32, "silu1", tag="x_win0")
+        slope(1, scaled1, silu1, high)
+        dy_woven1 = sbuf([P, PACK * K], BF16, "dy_woven1", tag="x_raw01")
+        daq1 = gradient(1, dy_picked1, dy_woven1, w2q1, da, high)
+        turn_weights(w1_raw[1], woven[0], [low[2], low[3], low[2], low[3]])
+        w1f1 = quantized("w1f1", woven[0], E4M3)
         last_product(2, w1f0, daq0, low[0], factor_of(1, 1))
         put(0, out_win[2], factor_of(1, 1))
         last_product(3, w1f0, daq0, low[1], slab[1][:, PACK * K : 5 * K])
         put(0, out_win[3], slab[1][:, PACK * K : 5 * K])
 
-        dx1 = sbuf([P, PACK, SLOTS], F32, "dx1", tag="ts_win")
+        dx1 = sbuf([P, PACK, SLOTS], F32, "dx1", tag="x_raw10")
         rows = out.rearrange("(p j) n -> j p n", j=PACK)
         for j in range(PACK):
             last_product(j, w1f1, daq1, (low[2], low[3], high[0], high[1])[j], dx1[:, j, :])

@@ -24,7 +24,6 @@ LIST_COLS = SLOTS // 16
 ROW = P - 1
 ALIGN = 64
 HALF = TOKENS // 2
-SPLIT = HALF // 2
 
 FLOPS = 3 * EXPERTS * 2 * K * K * SLOTS
 
@@ -77,8 +76,9 @@ def tile_attend_gxfull_sil_x_kernel(tc, xT, dyT, w1, w2, ts, tx, cf, offs, out):
 
         tx_win = sbuf([P, TOKENS], F32, "tx_win")
         ts_win = sbuf([P, TOKENS], F32, "ts_win")
+        nc.vector.memset(tx_win[0:ROW, :].bitcast(I32), 0)
+        nc.gpsimd.memset(ts_win[0:ROW, :], 0.0)
         for win, src in ((tx_win, tx), (ts_win, ts)):
-            nc.vector.memset(win[0:ROW, :].bitcast(I32), 0)
             nc.sync.dma_start(win[ROW:P, :], src[0:1, :])
 
         w1_raw = [sbuf([P, PACK, K], F32, f"w1_raw{b}") for b in range(EXPERTS)]
@@ -110,44 +110,30 @@ def tile_attend_gxfull_sil_x_kernel(tc, xT, dyT, w1, w2, ts, tx, cf, offs, out):
         load_w1(1)
         load_w2(1)
 
-        x_win = [sbuf([P, 2 * TOKENS], BF16, f"x_win{u}") for u in range(2)]
+        x_win = [sbuf([P, 2 * TOKENS], BF16, f"x_win{u}", tag="x_win0") for u in range(2)]
 
-        def paired(u, h, cols):
-            first = h * HALF
-            dst = x_win[u][:, 2 * (first + cols.start) : 2 * (first + cols.stop)].rearrange("p (n e) -> p n e", e=2)
-            return dst, x_raw[u][h][:, :, cols].rearrange("p e n -> p n e")
+        def paired(u, h):
+            dst = x_win[u][:, h * TOKENS : (h + 1) * TOKENS].rearrange("p (n e) -> p n e", e=2)
+            return dst, x_raw[u][h][:].rearrange("p e n -> p n e")
 
         for h in range(2):
-            nc.scalar.activation(*paired(0, h, slice(0, HALF)), ACT.Copy)
+            nc.scalar.activation(*paired(0, h), ACT.Copy)
 
         picked_scales = sbuf([P, 2 * EXPERTS * SLOTS], F32, "picked_scales")
 
-        def slot_columns(win, b, n):
-            picked = picked_scales[:, n * SLOTS : (n + 1) * SLOTS]
-            nc.vector.tensor_copy(picked, listed(win[:], b))
-            for r in range(PACK):
-                nc.tensor.transpose(banks[n][:, blocks[r]], picked[:, blocks[r]], ident[:])
-            return quarters(banks[n][:])[:, :, ROW]
-
-        half_tx, neg_tx, gate = [], [], []
-        for b in range(EXPERTS):
-            tx_cols = slot_columns(tx_win, b, 2 * b)
-            ts_cols = slot_columns(ts_win, b, 2 * b + 1)
-            h = sbuf([P, PACK], F32, f"half_tx{b}")
-            n = sbuf([P, PACK], F32, f"neg_tx{b}")
-            g = sbuf([P, PACK], F32, f"gate{b}")
-            nc.vector.tensor_scalar_mul(h[:], tx_cols, 0.5)
-            nc.vector.tensor_scalar_mul(n[:], tx_cols, -1.0)
-            nc.vector.scalar_tensor_tensor(g[:], ts_cols, -1.0, h[:], ALU.mult, ALU.mult)
-            half_tx.append(h)
-            neg_tx.append(n)
-            gate.append(g)
+        scale_cols = []
+        for n, win in enumerate((tx_win, ts_win)):
+            picked = picked_scales[:, n * EXPERTS * SLOTS : (n + 1) * EXPERTS * SLOTS]
+            nc.vector.tensor_copy(picked, win[:].indirect(offsets[:]))
+            for b in range(EXPERTS):
+                for r in range(PACK):
+                    first = b * SLOTS + r * P
+                    nc.tensor.transpose(banks[2 * n + b][:, blocks[r]], picked[:, first : first + P], ident[:])
+            scale_cols.append([quarters(banks[2 * n + b][:])[:, :, ROW] for b in range(EXPERTS)])
 
         out_win = [sbuf([P, TOKENS], F32, "out_win0"), sbuf([P, TOKENS], F32, "out_win1")]
-        out_win.append(sbuf([P, TOKENS], F32, "out_win2", tag="tx_win"))
-        out_win.append(sbuf([P, TOKENS], F32, "out_win3", tag="ts_win"))
-        for win in out_win:
-            nc.vector.memset(win[:].bitcast(I32), 0)
+        nc.vector.memset(out_win[0][:].bitcast(I32), 0)
+        nc.gpsimd.memset(out_win[1][:], 0.0)
 
         slab = [sbuf([P, 10 * K], F32, "slab0"), sbuf([P, 6 * K], F32, "slab1")]
         factor_at = [(0, 1, 6, 7), (0, 1, 2, 3)]
@@ -157,25 +143,17 @@ def tile_attend_gxfull_sil_x_kernel(tc, xT, dyT, w1, w2, ts, tx, cf, offs, out):
         x_words = sbuf([P, 2, EXPERTS * SLOTS], U32, "x_words")
         nc.vector.tensor_copy(x_words[:, 0, :], x_win[0][:].bitcast(U32).indirect(offsets[:]))
 
-        for c in range(PACK):
-            nc.tensor.transpose(banks[3][:, blocks[c]], cf_col[:, c : c + 1].to_broadcast([P, P]), ident[:])
-        cf_row = sbuf([P, K], F32, "cf_row")
-        nc.vector.tensor_copy(cf_row[:], banks[3][:])
-
         def weave(engine_copy, dst, planes, cols):
             engine_copy(
                 dst[:, PACK * cols.start : PACK * cols.stop].rearrange("p (c t) -> p c t", t=PACK),
                 planes[:, :, cols].rearrange("p t c -> p c t"),
             )
 
-        def turn_block(raw, c, dst, bank):
-            for t in range(PACK):
-                nc.tensor.transpose(bank[:, blocks[t]], raw[:, c, t:K:PACK], ident[:])
-            weave(nc.scalar.copy, dst, quarters(bank[:]), slice(0, P))
-
-        def turn_weights(raw, dst, use):
-            for c in range(PACK):
-                turn_block(raw, c, dst[:, c * K : (c + 1) * K], use[c])
+        def turn_weights(raw, dst, bank_of):
+            for c, bank in bank_of.items():
+                for t in range(PACK):
+                    nc.tensor.transpose(bank[:, blocks[t]], raw[:, c, t:K:PACK], ident[:])
+                weave(nc.scalar.copy, dst[:, c * K : (c + 1) * K], quarters(bank[:]), slice(0, P))
 
         def quantized(name, src, fmt):
             mx = mx_tiles(name)
@@ -184,10 +162,18 @@ def tile_attend_gxfull_sil_x_kernel(tc, xT, dyT, w1, w2, ts, tx, cf, offs, out):
 
         for cols in blocks:
             weave(nc.scalar.copy, woven[0], w1_raw[0], cols)
-        w1d0 = quantized("w1d0", woven[0], E4M3)
-        nc.scalar.activation(*paired(1, 0, slice(0, HALF)), ACT.Copy)
-        nc.scalar.activation(*paired(1, 1, slice(0, SPLIT)), ACT.Copy)
-        nc.vector.tensor_copy(*paired(1, 1, slice(SPLIT, HALF)))
+        half_tx, neg_tx, gate = [], [], []
+        slot_scales = sbuf([P, EXPERTS, 3, PACK], F32, "slot_scales", tag="x_raw01")
+        for b in range(EXPERTS):
+            h, n, g = (slot_scales[:, b, kind, :] for kind in range(3))
+            nc.scalar.activation(h, scale_cols[0][b], ACT.Copy, scale=0.5)
+            nc.scalar.activation(n, scale_cols[0][b], ACT.Copy, scale=-1.0)
+            nc.vector.scalar_tensor_tensor(g, scale_cols[1][b], -1.0, h, ALU.mult, ALU.mult)
+            half_tx.append(h)
+            neg_tx.append(n)
+            gate.append(g)
+        nc.scalar.activation(*paired(1, 0), ACT.Copy)
+        nc.vector.tensor_copy(*paired(1, 1))
         for b in range(EXPERTS):
             slots = slice(b * SLOTS, (b + 1) * SLOTS)
             nc.vector.tensor_copy(x_words[:, 1, slots], listed(x_win[1][:].bitcast(U32), b))
@@ -224,13 +210,16 @@ def tile_attend_gxfull_sil_x_kernel(tc, xT, dyT, w1, w2, ts, tx, cf, offs, out):
             for t in ts_range:
                 nc.vector.tensor_copy(picked[:, t, :], listed(dy_win[t][:], b))
 
-        def gradient(b, dy_picked, dy_woven, w2q, da, sums):
+        def gradient(b, dy_picked, dy_woven, w2q, da, sums, together):
             dyq = mx_tiles(f"dy{b}")
             da_words = da_words_of(b).rearrange("p (r i u) -> p r i u", r=PACK, u=2)
-            for r in range(PACK):
-                weave(nc.scalar.copy, dy_woven, dy_picked, blocks[r])
-                quantize(dyq, dy_woven, E5M2, blocks[r])
-                product(sums[r], dyq, E5M2, r, w2q, E4M3)
+            for first in range(0, PACK, together):
+                group = range(first, first + together)
+                for r in group:
+                    weave(nc.scalar.copy, dy_woven, dy_picked, blocks[r])
+                quantize(dyq, dy_woven, E5M2, slice(first * P, (first + together) * P))
+                for r in group:
+                    product(sums[r], dyq, E5M2, r, w2q, E4M3)
             for r in range(PACK):
                 rounded = da[:, r * K : (r + 1) * K]
                 nc.vector.scalar_tensor_tensor(rounded, sums[r][:], gate[b][:, r : r + 1], factor_of(b, r), ALU.mult, ALU.mult)
@@ -247,57 +236,69 @@ def tile_attend_gxfull_sil_x_kernel(tc, xT, dyT, w1, w2, ts, tx, cf, offs, out):
         def put(b, window, staging):
             nc.vector.tensor_copy(listed(window[:], b), staging)
 
-        low, high = banks[0:4], banks[4:8]
+        high = banks[4:8]
 
+        for c in range(PACK):
+            nc.tensor.transpose(banks[7][:, blocks[c]], cf_col[:, c : c + 1].to_broadcast([P, P]), ident[:])
+        cf_row = sbuf([P, K], F32, "cf_row", tag="x_raw10")
+        nc.scalar.copy(cf_row[:], banks[7][:])
+        w1d0 = sbuf([P, K], U32, "w1d0_codes", tag="x_win0"), sbuf([P, K], U8, "w1d0_scales")
+        quantize(w1d0, woven[0], E4M3)
         xq0 = quantized("x0", x_woven[:, 0 : 2 * K].bitcast(BF16), E4M3)
         xq1 = quantized("x1", x_woven[:, 2 * K : 4 * K].bitcast(BF16), E4M3)
         late = sbuf([P, PACK * K], BF16, "late", tag="x_raw11")
-        turn_weights(w1_raw[0], late, low)
-        w1f0 = quantized("w1f0", late, E4M3)
-        turn_weights(w2_raw[0], woven[2], low)
-        w2q0 = quantized("w2q0", woven[2], E4M3)
+        turn_weights(w1_raw[0], late, {0: banks[0], 1: banks[1]})
         scaled0 = sbuf([P, PACK, SLOTS], F32, "scaled0", tag="x_raw00")
         first_product(w1d0, xq0, scaled0, high)
+        turn_weights(w2_raw[0], woven[2], {0: banks[0], 1: banks[1]})
         dy_picked0 = slab[0][:, 2 * K : 6 * K].bitcast(BF16).rearrange("p (t i) -> p t i", t=PACK)[:, :, SLOTS : 2 * SLOTS]
         dy_picked1 = slab[0][:, 2 * K : 10 * K].bitcast(BF16).rearrange("p (t i) -> p t i", t=PACK)[:, :, 0:SLOTS]
         for t in range(PACK):
             gather_dy(0, dy_picked0, [t])
             if t < 2:
                 gather_dy(1, dy_picked1, [t])
-        silu0 = sbuf([P, PACK, K], F32, "silu0", tag="x_raw01")
-        slope(0, scaled0, silu0, low)
+        silu0 = sbuf([P, PACK, K], F32, "silu0")
+        slope(0, scaled0, silu0, high)
+        turn_weights(w2_raw[0], woven[2], {2: banks[4], 3: banks[5]})
+        w2q0 = quantized("w2q0", woven[2], E4M3)
         da = sbuf([P, PACK * K], BF16, "da", tag="picked_scales")
         dy_woven0 = sbuf([P, PACK * K], BF16, "dy_woven0", tag="x_raw00")
-        daq0 = gradient(0, dy_picked0, dy_woven0, w2q0, da, high)
-        dx0 = sbuf([P, 2, SLOTS], F32, "dx0", tag="w1_raw0")
+        ring = [banks[6], banks[7], banks[0], banks[1]]
+        daq0 = gradient(0, dy_picked0, dy_woven0, w2q0, da, ring, 1)
+        turn_weights(w1_raw[0], late, {2: banks[2], 3: banks[3]})
+        w1f0 = quantized("w1f0", late, E4M3)
+        dx0 = [sbuf([P, SLOTS], F32, "dx00", tag="tx_win"), sbuf([P, SLOTS], F32, "dx01", tag="ts_win")]
 
         gather_dy(1, dy_picked1, range(2, PACK))
-        turn_weights(w2_raw[1], woven[1], low)
-        w2q1 = quantized("w2q1", woven[1], E4M3)
-        for j in range(2):
-            last_product(j, w1f0, daq0, banks[j], dx0[:, j, :])
-            put(0, out_win[j], dx0[:, j, :])
-
         for cols in blocks:
             weave(nc.scalar.copy, dy_woven0, w1_raw[1], cols)
-        w1d1 = sbuf([P, K], U32, "w1d1_codes"), daq0[1][PACK:P, :]
-        quantize(w1d1, dy_woven0, E4M3)
-        scaled1 = sbuf([P, PACK, SLOTS], F32, "scaled1", tag="x_raw01")
-        first_product(w1d1, xq1, scaled1, [banks[2], banks[3], banks[0], banks[1]])
+        w1d1 = quantized("w1d1", dy_woven0, E4M3)
+        turn_weights(w2_raw[1], woven[1], {0: banks[4], 1: banks[5], 2: banks[4], 3: banks[5]})
+        w2q1 = quantized("w2q1", woven[1], E4M3)
+        for j in range(2):
+            last_product(j, w1f0, daq0, banks[2 + j], dx0[j][:])
+            put(0, out_win[j], dx0[j][:])
+        for name in ("tx_win", "ts_win"):
+            win = sbuf([P, TOKENS], F32, "late_" + name, tag=name)
+            nc.gpsimd.memset(win[:], 0.0)
+            out_win.append(win)
+
+        scaled1 = sbuf([P, PACK, SLOTS], F32, "scaled1", tag="silu0")
+        first_product(w1d1, xq1, scaled1, [banks[2], banks[3], banks[2], banks[3]])
         silu1 = sbuf([P, PACK, K], F32, "silu1", tag="x_win0")
-        slope(1, scaled1, silu1, high)
-        dy_woven1 = sbuf([P, PACK * K], BF16, "dy_woven1", tag="x_raw01")
-        daq1 = gradient(1, dy_picked1, dy_woven1, w2q1, da, high)
-        turn_weights(w1_raw[1], woven[0], [low[2], low[3], low[2], low[3]])
+        slope(1, scaled1, silu1, [banks[2], banks[3], banks[6], banks[7]])
+        dy_woven1 = sbuf([P, PACK * K], BF16, "dy_woven1", tag="silu0")
+        daq1 = gradient(1, dy_picked1, dy_woven1, w2q1, da, [banks[0], banks[1], banks[6], banks[7]], 2)
+        turn_weights(w1_raw[1], woven[0], {0: banks[2], 1: banks[3], 2: banks[2], 3: banks[3]})
         w1f1 = quantized("w1f1", woven[0], E4M3)
-        last_product(2, w1f0, daq0, low[0], factor_of(1, 1))
+        last_product(2, w1f0, daq0, banks[4], factor_of(1, 1))
         put(0, out_win[2], factor_of(1, 1))
-        last_product(3, w1f0, daq0, low[1], slab[1][:, PACK * K : 5 * K])
+        last_product(3, w1f0, daq0, banks[5], slab[1][:, PACK * K : 5 * K])
         put(0, out_win[3], slab[1][:, PACK * K : 5 * K])
 
         dx1 = sbuf([P, PACK, SLOTS], F32, "dx1", tag="x_raw10")
         rows = out.rearrange("(p j) n -> j p n", j=PACK)
         for j in range(PACK):
-            last_product(j, w1f1, daq1, (low[2], low[3], high[0], high[1])[j], dx1[:, j, :])
+            last_product(j, w1f1, daq1, (banks[0], banks[1], banks[6], banks[7])[j], dx1[:, j, :])
             put(1, out_win[j], dx1[:, j, :])
             nc.sync.dma_start(rows[j], out_win[j][:])

@@ -23,7 +23,7 @@ TOKENS = 2048
 LIST_COLS = SLOTS // 16
 ROW = P - 1
 ALIGN = 64
-HALF = TOKENS // 2
+RUN = 4
 
 FLOPS = 3 * EXPERTS * 2 * K * K * SLOTS
 
@@ -39,27 +39,23 @@ def tile_attend_gxfull_sil_x_kernel(tc, xT, dyT, w1, w2, ts, tx, cf, offs, out):
 
         banks = [psum.tile([P, SLOTS], F32, name=f"bank{n}") for n in range(8)]
         blocks = [slice(r * P, (r + 1) * P) for r in range(PACK)]
+        parts = [slice(r * K, (r + 1) * K) for r in range(PACK)]
 
         def quarters(ap):
             return ap.rearrange("p (a m) -> p a m", m=P)
 
-        def mx_tiles(name):
-            return sbuf([P, K], U32, name + "_codes"), sbuf([P, K], U8, name + "_scales")
+        def quantized(name, woven, fmt, tag=None):
+            codes = sbuf([P, K], U32, name + "_codes", tag)
+            scales = sbuf([P, K], U8, name + "_scales")
+            nc.vector.quantize_mx(out=codes[:].bitcast(fmt), scales=scales[:], in_=woven)
+            return codes, scales, fmt
 
-        def quantize(mx, woven, fmt, cols=slice(0, K)):
-            codes, scales = mx
-            nc.vector.quantize_mx(
-                out=codes[:, cols].bitcast(fmt),
-                scales=scales[:, cols],
-                in_=woven[:, PACK * cols.start : PACK * cols.stop],
-            )
-
-        def product(acc, stat, stat_fmt, block, moving, moving_fmt):
+        def product(acc, stat, block, moving):
             nc.tensor.matmul_mx(
                 out=acc[:],
-                lhsT=stat[0][:, blocks[block]].bitcast(stat_fmt),
+                lhsT=stat[0][:, blocks[block]].bitcast(stat[2]),
                 lhsT_scale=stat[1][:, blocks[block]],
-                rhs=moving[0][:].bitcast(moving_fmt),
+                rhs=moving[0][:].bitcast(moving[2]),
                 rhs_scale=moving[1][:],
                 start=True,
                 stop=True,
@@ -68,237 +64,263 @@ def tile_attend_gxfull_sil_x_kernel(tc, xT, dyT, w1, w2, ts, tx, cf, offs, out):
         offsets = keep.tile([P, EXPERTS * LIST_COLS], U16, name="offsets")
         nc.sync.dma_start(offsets[:], offs)
 
-        def listed(window, b):
-            return window.indirect(offsets[:, b * LIST_COLS : (b + 1) * LIST_COLS])
+        def listed(window, first, count):
+            return window[:].indirect(offsets[:, first // 16 : (first + count) // 16])
+
+        tx_win = sbuf([P, TOKENS], F32, "tx_win")
+        ts_win = sbuf([P, TOKENS], F32, "ts_win")
+        x_win = [sbuf([P, TOKENS], F32, f"x_win{t}") for t in range(PACK)]
+        dy_win = [sbuf([P, TOKENS], F32, f"dy_win{t}") for t in range(PACK)]
+        out_win = [sbuf([P, TOKENS], F32, f"out_win{j}") for j in range(PACK)]
+        w1_raw = [sbuf([P, PACK * K], F32, f"w1_raw{b}") for b in range(EXPERTS)]
+        w2_raw = [sbuf([P, PACK * K], F32, f"w2_raw{b}") for b in range(EXPERTS)]
+        cf_col = sbuf([P, PACK], F32, "cf_col")
+
+        x_planes = xT.rearrange("(p t) n -> t p n", t=PACK)
+        dy_planes = dyT.rearrange("(p t) n -> t p n", t=PACK)
+
+        def load_w1(b):
+            nc.sync.dma_start(w1_raw[b][:], w1[b].rearrange("(p j) f -> p (j f)", j=PACK))
+
+        def load_w2(b):
+            nc.sync.dma_start(w2_raw[b][:].rearrange("p (c e) -> p c e", c=PACK), w2[b].rearrange("(c p) e -> p c e", p=P))
+
+        nc.sync.dma_start(tx_win[ROW:P, :], tx[0:1, :])
+        nc.sync.dma_start(x_win[0][:], x_planes[0])
+        nc.sync.dma_start(ts_win[ROW:P, :], ts[0:1, :])
+        nc.sync.dma_start(cf_col[:], cf.rearrange("(p c) o -> p (c o)", c=PACK))
+        nc.sync.dma_start(x_win[1][:], x_planes[1])
+        load_w1(0)
+        nc.sync.dma_start(x_win[2][:], x_planes[2])
+        nc.sync.dma_start(x_win[3][:], x_planes[3])
+        nc.sync.dma_start(dy_win[0][:], dy_planes[0])
+        nc.sync.dma_start(dy_win[1][:], dy_planes[1])
+        load_w2(0)
+        load_w1(1)
+        nc.sync.dma_start(dy_win[2][:], dy_planes[2])
+        nc.sync.dma_start(dy_win[3][:], dy_planes[3])
+        load_w2(1)
 
         ident = sbuf([P, P], F32, "ident")
         make_identity(nc, ident[:])
 
-        tx_win = sbuf([P, TOKENS], F32, "tx_win")
-        ts_win = sbuf([P, TOKENS], F32, "ts_win")
         nc.vector.memset(tx_win[0:ROW, :].bitcast(I32), 0)
-        nc.gpsimd.memset(ts_win[0:ROW, :], 0.0)
-        for win, src in ((tx_win, tx), (ts_win, ts)):
-            nc.sync.dma_start(win[ROW:P, :], src[0:1, :])
+        nc.vector.memset(ts_win[0:ROW, :].bitcast(I32), 0)
+        for win in out_win:
+            nc.vector.memset(win[:].bitcast(I32), 0)
 
-        w1_raw = [sbuf([P, PACK, K], F32, f"w1_raw{b}") for b in range(EXPERTS)]
-        w2_raw = [sbuf([P, PACK, K], F32, f"w2_raw{b}") for b in range(EXPERTS)]
-        x_raw = [[sbuf([P, 2, HALF], F32, f"x_raw{u}{h}") for h in range(2)] for u in range(2)]
-        dy_win = [sbuf([P, TOKENS], F32, f"dy_win{t}") for t in range(PACK)]
-        cf_col = sbuf([P, PACK], F32, "cf_col")
+        def gather_on_scalar(dst, src):
+            nc.scalar.activation(dst, src, ACT.Copy)
 
-        def load_w1(b):
-            nc.sync.dma_start(w1_raw[b][:], w1[b].rearrange("(p j) f -> p j f", j=PACK))
+        def weave(copy, dst, planes):
+            copy(
+                dst.rearrange("p (c i t) -> p c t i", t=PACK, i=RUN),
+                planes.rearrange("p t (c i) -> p c t i", i=RUN),
+            )
 
-        def load_w2(b):
-            nc.sync.dma_start(w2_raw[b][:], w2[b].rearrange("(c p) e -> p c e", p=P))
+        def rounded(name, raw, tag=None):
+            dst = sbuf([P, PACK * K], BF16, name, tag)
+            nc.vector.tensor_copy(dst[:], raw[:])
+            return dst
 
-        def load_x(u):
-            pairs = xT.rearrange("(p u e) n -> u p e n", u=2, e=2)
+        def turn_pair(src, dst, h, bank):
+            for c in (2 * h, 2 * h + 1):
+                pairs = src[:, parts[c]].bitcast(F32)
+                for u in range(2):
+                    nc.tensor.transpose(bank[:, blocks[2 * (c % 2) + u]], pairs[:, u : K // 2 : 2], ident[:])
+            nc.scalar.copy(
+                dst[:].bitcast(F32)[:, parts[h]].rearrange("p (c m u) -> p c m u", c=2, u=2),
+                bank[:].rearrange("p (c u m) -> p c m u", c=2, u=2),
+            )
+
+        def turn_float32(raw, dst, use):
+            for c in use:
+                for t in range(PACK):
+                    nc.tensor.transpose(use[c][:, blocks[t]], raw[:, c * K + t : (c + 1) * K : PACK], ident[:])
+                nc.scalar.copy(dst[:, parts[c]].rearrange("p (m t) -> p m t", t=PACK), quarters(use[c][:]).rearrange("p t m -> p m t"))
+
+        def turn_weights(src, dst, use):
             for h in range(2):
-                nc.sync.dma_start(x_raw[u][h][:], pairs[u][:, :, h * HALF : (h + 1) * HALF])
+                turn_pair(src, dst, h, use[h])
 
-        load_x(0)
-        with nc.allow_non_contiguous_dma(reason="512 scales, one element to a partition and block"):
-            nc.sync.dma_start(cf_col[:], cf.rearrange("(c p) o -> p (c o)", p=P))
-        load_w1(0)
-        load_x(1)
-        load_w2(0)
-        dy_planes = dyT.rearrange("(p t) n -> t p n", t=PACK)
-        for t in range(PACK):
-            nc.sync.dma_start(dy_win[t][:], dy_planes[t])
-        load_w1(1)
-        load_w2(1)
+        picked = [sbuf([P, EXPERTS * SLOTS], F32, "tx_picked"), sbuf([P, EXPERTS * SLOTS], F32, "ts_picked")]
+        tx_col = sbuf([P, EXPERTS * PACK], F32, "tx_col")
+        gate = sbuf([P, EXPERTS * PACK], F32, "gate")
 
-        x_win = [sbuf([P, 2 * TOKENS], BF16, f"x_win{u}", tag="x_win0") for u in range(2)]
-
-        def paired(u, h):
-            dst = x_win[u][:, h * TOKENS : (h + 1) * TOKENS].rearrange("p (n e) -> p n e", e=2)
-            return dst, x_raw[u][h][:].rearrange("p e n -> p n e")
-
-        for h in range(2):
-            nc.scalar.activation(*paired(0, h), ACT.Copy)
-
-        picked_scales = sbuf([P, 2 * EXPERTS * SLOTS], F32, "picked_scales")
-
-        scale_cols = []
-        for n, win in enumerate((tx_win, ts_win)):
-            picked = picked_scales[:, n * EXPERTS * SLOTS : (n + 1) * EXPERTS * SLOTS]
-            nc.vector.tensor_copy(picked, win[:].indirect(offsets[:]))
+        def turn_scales(n, use):
             for b in range(EXPERTS):
                 for r in range(PACK):
                     first = b * SLOTS + r * P
-                    nc.tensor.transpose(banks[2 * n + b][:, blocks[r]], picked[:, first : first + P], ident[:])
-            scale_cols.append([quarters(banks[2 * n + b][:])[:, :, ROW] for b in range(EXPERTS)])
+                    nc.tensor.transpose(use[b][:, blocks[r]], picked[n][:, first : first + P], ident[:])
+            return [quarters(use[b][:])[:, :, ROW] for b in range(EXPERTS)]
 
-        out_win = [sbuf([P, TOKENS], F32, "out_win0"), sbuf([P, TOKENS], F32, "out_win1")]
-        nc.vector.memset(out_win[0][:].bitcast(I32), 0)
-        nc.gpsimd.memset(out_win[1][:], 0.0)
+        gather_on_scalar(picked[0][:], listed(tx_win, 0, EXPERTS * SLOTS))
+        x_picked = [sbuf([P, PACK * SLOTS], BF16, f"x_picked{b}") for b in range(EXPERTS)]
+        dy_picked = [sbuf([P, PACK * SLOTS], BF16, f"dy_picked{b}") for b in range(EXPERTS)]
 
-        slab = [sbuf([P, 10 * K], F32, "slab0"), sbuf([P, 6 * K], F32, "slab1")]
-        factor_at = [(0, 1, 6, 7), (0, 1, 2, 3)]
-        woven = [sbuf([P, PACK * K], BF16, f"woven{n}") for n in range(3)]
-        x_woven = slab[0][:, 2 * K : 6 * K]
+        def gather(dst, windows, t, b, copy=gather_on_scalar):
+            copy(dst[b][:, parts[t]], listed(windows[t], b * SLOTS, SLOTS))
 
-        x_words = sbuf([P, 2, EXPERTS * SLOTS], U32, "x_words")
-        nc.vector.tensor_copy(x_words[:, 0, :], x_win[0][:].bitcast(U32).indirect(offsets[:]))
+        def planes_of(src):
+            return src[:].rearrange("p (t i) -> p t i", t=PACK)
 
-        def weave(engine_copy, dst, planes, cols):
-            engine_copy(
-                dst[:, PACK * cols.start : PACK * cols.stop].rearrange("p (c t) -> p c t", t=PACK),
-                planes[:, :, cols].rearrange("p t c -> p c t"),
-            )
-
-        def turn_weights(raw, dst, bank_of):
-            for c, bank in bank_of.items():
-                for t in range(PACK):
-                    nc.tensor.transpose(bank[:, blocks[t]], raw[:, c, t:K:PACK], ident[:])
-                weave(nc.scalar.copy, dst[:, c * K : (c + 1) * K], quarters(bank[:]), slice(0, P))
-
-        def quantized(name, src, fmt):
-            mx = mx_tiles(name)
-            quantize(mx, src, fmt)
-            return mx
-
-        for cols in blocks:
-            weave(nc.scalar.copy, woven[0], w1_raw[0], cols)
-        half_tx, neg_tx, gate = [], [], []
-        slot_scales = sbuf([P, EXPERTS, 3, PACK], F32, "slot_scales", tag="x_raw01")
-        for b in range(EXPERTS):
-            h, n, g = (slot_scales[:, b, kind, :] for kind in range(3))
-            nc.scalar.activation(h, scale_cols[0][b], ACT.Copy, scale=0.5)
-            nc.scalar.activation(n, scale_cols[0][b], ACT.Copy, scale=-1.0)
-            nc.vector.scalar_tensor_tensor(g, scale_cols[1][b], -1.0, h, ALU.mult, ALU.mult)
-            half_tx.append(h)
-            neg_tx.append(n)
-            gate.append(g)
-        nc.scalar.activation(*paired(1, 0), ACT.Copy)
-        nc.vector.tensor_copy(*paired(1, 1))
-        for b in range(EXPERTS):
-            slots = slice(b * SLOTS, (b + 1) * SLOTS)
-            nc.vector.tensor_copy(x_words[:, 1, slots], listed(x_win[1][:].bitcast(U32), b))
-            nc.scalar.copy(
-                x_woven.bitcast(U32).rearrange("p (i u) -> p i u", u=2)[:, slots, :],
-                x_words[:, :, slots].rearrange("p u i -> p i u"),
-            )
-
-        def factor_of(b, r, count=1):
-            return slab[b][:, factor_at[b][r] * K : (factor_at[b][r] + count) * K]
-
-        def da_words_of(b):
-            return slab[b][:, (factor_at[b][3] + 1) * K : (factor_at[b][3] + 3) * K]
-
-        def first_product(w1d, xq, scaled, use):
-            for c in range(PACK):
-                product(use[c], w1d, E4M3, c, xq, E4M3)
-                nc.scalar.activation(scaled[:, c, :], use[c][:], ACT.Copy, scale=cf_col[:, c : c + 1])
-
-        def slope(b, scaled, silu, use):
-            for r in range(PACK):
-                for c in range(PACK):
-                    nc.tensor.transpose(use[r][:, blocks[c]], scaled[:, c, blocks[r]], ident[:])
-                nc.scalar.activation(silu[:, r, :], use[r][:], ACT.Silu, scale=neg_tx[b][:, r : r + 1])
-                nc.scalar.activation(factor_of(b, r), use[r][:], ACT.Tanh, scale=half_tx[b][:, r : r + 1])
-            cf_twice = cf_row[:].unsqueeze(1).to_broadcast([P, 2, K])
-            for r in (0, 2):
-                pair = silu[:, r : r + 2, :]
-                nc.vector.scalar_tensor_tensor(pair, pair, 1.0, cf_twice, ALU.subtract, ALU.mult)
-                factor = factor_of(b, r, 2)
-                nc.vector.scalar_tensor_tensor(factor, factor, 1.0, pair.rearrange("p r f -> p (r f)"), ALU.add, ALU.mult)
-
-        def gather_dy(b, picked, ts_range):
-            for t in ts_range:
-                nc.vector.tensor_copy(picked[:, t, :], listed(dy_win[t][:], b))
-
-        def gradient(b, dy_picked, dy_woven, w2q, da, sums, together):
-            dyq = mx_tiles(f"dy{b}")
-            da_words = da_words_of(b).rearrange("p (r i u) -> p r i u", r=PACK, u=2)
-            for first in range(0, PACK, together):
-                group = range(first, first + together)
-                for r in group:
-                    weave(nc.scalar.copy, dy_woven, dy_picked, blocks[r])
-                quantize(dyq, dy_woven, E5M2, slice(first * P, (first + together) * P))
-                for r in group:
-                    product(sums[r], dyq, E5M2, r, w2q, E4M3)
-            for r in range(PACK):
-                rounded = da[:, r * K : (r + 1) * K]
-                nc.vector.scalar_tensor_tensor(rounded, sums[r][:], gate[b][:, r : r + 1], factor_of(b, r), ALU.mult, ALU.mult)
-                words = rounded.bitcast(F32)
-                for u in range(2):
-                    nc.tensor.transpose(sums[r][:, blocks[u]], words[:, u : K // 2 : 2], ident[:])
-                nc.scalar.copy(da_words[:, r], quarters(sums[r][:, 0 : 2 * P]).rearrange("p u i -> p i u"))
-            return quantized(f"da{b}", da_words_of(b).bitcast(BF16), E5M2)
-
-        def last_product(j, w1f, daq, acc, staging):
-            product(acc, w1f, E4M3, j, daq, E5M2)
-            nc.scalar.copy(staging, acc[:])
-
-        def put(b, window, staging):
-            nc.vector.tensor_copy(listed(window[:], b), staging)
-
-        high = banks[4:8]
-
+        gather(x_picked, x_win, 0, 0)
+        gather_on_scalar(picked[1][:], listed(ts_win, 0, EXPERTS * SLOTS))
+        gather(x_picked, x_win, 0, 1)
+        tx_turned = turn_scales(0, banks[0:2])
         for c in range(PACK):
-            nc.tensor.transpose(banks[7][:, blocks[c]], cf_col[:, c : c + 1].to_broadcast([P, P]), ident[:])
-        cf_row = sbuf([P, K], F32, "cf_row", tag="x_raw10")
-        nc.scalar.copy(cf_row[:], banks[7][:])
-        w1d0 = sbuf([P, K], U32, "w1d0_codes", tag="x_win0"), sbuf([P, K], U8, "w1d0_scales")
-        quantize(w1d0, woven[0], E4M3)
-        xq0 = quantized("x0", x_woven[:, 0 : 2 * K].bitcast(BF16), E4M3)
-        xq1 = quantized("x1", x_woven[:, 2 * K : 4 * K].bitcast(BF16), E4M3)
-        late = sbuf([P, PACK * K], BF16, "late", tag="x_raw11")
-        turn_weights(w1_raw[0], late, {0: banks[0], 1: banks[1]})
-        scaled0 = sbuf([P, PACK, SLOTS], F32, "scaled0", tag="x_raw00")
-        first_product(w1d0, xq0, scaled0, high)
-        turn_weights(w2_raw[0], woven[2], {0: banks[0], 1: banks[1]})
-        dy_picked0 = slab[0][:, 2 * K : 6 * K].bitcast(BF16).rearrange("p (t i) -> p t i", t=PACK)[:, :, SLOTS : 2 * SLOTS]
-        dy_picked1 = slab[0][:, 2 * K : 10 * K].bitcast(BF16).rearrange("p (t i) -> p t i", t=PACK)[:, :, 0:SLOTS]
-        for t in range(PACK):
-            gather_dy(0, dy_picked0, [t])
-            if t < 2:
-                gather_dy(1, dy_picked1, [t])
-        silu0 = sbuf([P, PACK, K], F32, "silu0")
-        slope(0, scaled0, silu0, high)
-        turn_weights(w2_raw[0], woven[2], {2: banks[4], 3: banks[5]})
-        w2q0 = quantized("w2q0", woven[2], E4M3)
-        da = sbuf([P, PACK * K], BF16, "da", tag="picked_scales")
-        dy_woven0 = sbuf([P, PACK * K], BF16, "dy_woven0", tag="x_raw00")
-        ring = [banks[6], banks[7], banks[0], banks[1]]
-        daq0 = gradient(0, dy_picked0, dy_woven0, w2q0, da, ring, 1)
-        turn_weights(w1_raw[0], late, {2: banks[2], 3: banks[3]})
-        w1f0 = quantized("w1f0", late, E4M3)
-        dx0 = [sbuf([P, SLOTS], F32, "dx00", tag="tx_win"), sbuf([P, SLOTS], F32, "dx01", tag="ts_win")]
+            nc.tensor.transpose(banks[2][:, blocks[c]], cf_col[:, c : c + 1].to_broadcast([P, P]), ident[:])
+        cf_row = sbuf([P, K], F32, "cf_row")
+        woven = [sbuf([P, PACK * K], BF16, f"woven{n}") for n in range(4)]
 
-        gather_dy(1, dy_picked1, range(2, PACK))
-        for cols in blocks:
-            weave(nc.scalar.copy, dy_woven0, w1_raw[1], cols)
-        w1d1 = quantized("w1d1", dy_woven0, E4M3)
-        turn_weights(w2_raw[1], woven[1], {0: banks[4], 1: banks[5], 2: banks[4], 3: banks[5]})
-        w2q1 = quantized("w2q1", woven[1], E4M3)
-        for j in range(2):
-            last_product(j, w1f0, daq0, banks[2 + j], dx0[j][:])
-            put(0, out_win[j], dx0[j][:])
-        for name in ("tx_win", "ts_win"):
-            win = sbuf([P, TOKENS], F32, "late_" + name, tag=name)
-            nc.gpsimd.memset(win[:], 0.0)
-            out_win.append(win)
+        def interleave(src, stage):
+            weave(nc.vector.tensor_copy, stage[:], planes_of(src))
 
-        scaled1 = sbuf([P, PACK, SLOTS], F32, "scaled1", tag="silu0")
-        first_product(w1d1, xq1, scaled1, [banks[2], banks[3], banks[2], banks[3]])
-        silu1 = sbuf([P, PACK, K], F32, "silu1", tag="x_win0")
-        slope(1, scaled1, silu1, [banks[2], banks[3], banks[6], banks[7]])
-        dy_woven1 = sbuf([P, PACK * K], BF16, "dy_woven1", tag="silu0")
-        daq1 = gradient(1, dy_picked1, dy_woven1, w2q1, da, [banks[0], banks[1], banks[6], banks[7]], 2)
-        turn_weights(w1_raw[1], woven[0], {0: banks[2], 1: banks[3], 2: banks[2], 3: banks[3]})
-        w1f1 = quantized("w1f1", woven[0], E4M3)
-        last_product(2, w1f0, daq0, banks[4], factor_of(1, 1))
-        put(0, out_win[2], factor_of(1, 1))
-        last_product(3, w1f0, daq0, banks[5], slab[1][:, PACK * K : 5 * K])
-        put(0, out_win[3], slab[1][:, PACK * K : 5 * K])
+        nc.scalar.copy(cf_row[:].rearrange("p (m c) -> p m c", c=PACK), quarters(banks[2][:]).rearrange("p c m -> p m c"))
+        for b in range(EXPERTS):
+            nc.vector.tensor_copy(tx_col[:, b * PACK : (b + 1) * PACK], tx_turned[b])
+            gather(x_picked, x_win, 1, b)
+        w1_bf0 = rounded("w1_bf0", w1_raw[0])
+        interleave(w1_bf0, woven[0])
+        gather(x_picked, x_win, 2, 0, nc.vector.tensor_copy)
+        w1d0 = quantized("w1d0", woven[0][:], E4M3)
+        gather(x_picked, x_win, 3, 0, nc.vector.tensor_copy)
+        turn_pair(w1_bf0, woven[2], 0, banks[4])
+        gather(x_picked, x_win, 2, 1)
+        turn_pair(w1_bf0, woven[2], 1, banks[5])
+        gather(x_picked, x_win, 3, 1)
 
-        dx1 = sbuf([P, PACK, SLOTS], F32, "dx1", tag="x_raw10")
+        cf_rows = cf_row[:].unsqueeze(1).to_broadcast([P, 2, K])
+
+        def products(use, stat, moving):
+            for r in range(PACK):
+                product(use[r], stat, r, moving)
+
+        def preactivation(b, z, use):
+            for r in range(PACK):
+                col = b * PACK + r
+                nc.vector.scalar_tensor_tensor(z[:, parts[r]], use[r][:], tx_col[:, col : col + 1], cf_row[:], ALU.mult, ALU.mult)
+
+        halves = [slice(h * 2 * K, (h + 1) * 2 * K) for h in range(2)]
+
+        def activations(z, silu, tanh):
+            for h in halves:
+                nc.scalar.activation(silu[:, h], z[:, h], ACT.Silu, scale=-1.0)
+                nc.scalar.activation(tanh[:, h], z[:, h], ACT.Tanh, scale=0.5)
+
+        def scaled_silu(silu, h):
+            pair = silu[:, halves[h]].rearrange("p (r f) -> p r f", r=2)
+            nc.vector.scalar_tensor_tensor(pair, pair, 1.0, cf_rows, ALU.subtract, ALU.mult)
+
+        def slope(silu, tanh, h):
+            nc.vector.scalar_tensor_tensor(tanh[:, halves[h]], tanh[:, halves[h]], 1.0, silu[:, halves[h]], ALU.add, ALU.mult)
+
+        def gradient(b, factor, da, stage, use, turn):
+            for r in range(PACK):
+                col = b * PACK + r
+                nc.vector.scalar_tensor_tensor(da[:, parts[r]], use[r][:], gate[:, col : col + 1], factor[:, parts[r]], ALU.mult, ALU.mult)
+                if r % 2:
+                    turn_pair(da, stage, r // 2, turn[r // 2])
+
+        interleave(x_picked[0], woven[1])
+        xq0 = quantized("x0", woven[1][:], E4M3)
+        products(banks[0:4], xq0, w1d0)
+        interleave(x_picked[1], woven[1])
+        z0 = sbuf([P, PACK * K], F32, "z0", "x_win0")
+        for b in range(EXPERTS):
+            gather(dy_picked, dy_win, 0, b)
+        gather(dy_picked, dy_win, 1, 0)
+        preactivation(0, z0, banks[0:4])
+        xq1 = quantized("x1", woven[1][:], E4M3)
+        ts_turned = turn_scales(1, banks[0:2])
+        w1f0 = quantized("w1f0", woven[2][:], E4M3, "x_picked1")
+        for b in range(EXPERTS):
+            cols = slice(b * PACK, (b + 1) * PACK)
+            nc.vector.scalar_tensor_tensor(gate[:, cols], ts_turned[b], -0.5, tx_col[:, cols], ALU.mult, ALU.mult)
+        silu0 = sbuf([P, PACK * K], F32, "silu0", "x_win1")
+        tanh0 = sbuf([P, PACK * K], F32, "tanh0", "x_win2")
+        activations(z0, silu0, tanh0)
+        w1_bf1 = rounded("w1_bf1", w1_raw[1], "w1_bf0")
+        scaled_silu(silu0, 0)
+        interleave(w1_bf1, woven[2])
+        slope(silu0, tanh0, 0)
+        w1d1 = quantized("w1d1", woven[2][:], E4M3)
+        scaled_silu(silu0, 1)
+        products(banks[0:4], xq1, w1d1)
+        slope(silu0, tanh0, 1)
+        gather(dy_picked, dy_win, 2, 0)
+        gather(dy_picked, dy_win, 3, 0, nc.vector.tensor_copy)
+        turn_float32(w2_raw[0], woven[3], dict(enumerate(banks[4:8])))
+        z1 = sbuf([P, PACK * K], F32, "z1", "x_win3")
+        preactivation(1, z1, banks[0:4])
+        interleave(dy_picked[0], woven[0])
+        w2q0 = quantized("w2q0", woven[3][:], E4M3)
+        dyq0 = quantized("dy0", woven[0][:], E5M2)
+        products(banks[4:8], dyq0, w2q0)
+        w1f_stage = sbuf([P, PACK * K], BF16, "w1f_stage", "x_picked0")
+        turn_weights(w1_bf1, w1f_stage, banks[0:2])
+        da = sbuf([P, PACK * K], BF16, "da", "tx_picked")
+        silu1 = sbuf([P, PACK * K], F32, "silu1", "tx_win")
+        tanh1 = sbuf([P, PACK * K], F32, "tanh1", "ts_win")
+        activations(z1, silu1, tanh1)
+        for t in (1, 2, 3):
+            gather(dy_picked, dy_win, t, 1)
+        scaled_silu(silu1, 0)
+        gradient(0, tanh0, da, woven[1], banks[4:8], banks[2:4])
+        turn_float32(w2_raw[1], woven[3], {0: banks[0], 1: banks[1], 2: banks[4], 3: banks[5]})
+        slope(silu1, tanh1, 0)
+        scaled_silu(silu1, 1)
+        interleave(dy_picked[1], woven[0])
+        daq0 = quantized("da0", woven[1][:], E5M2)
+        dyq1 = quantized("dy1", woven[0][:], E5M2)
+        w2q1 = quantized("w2q1", woven[3][:], E4M3)
+        slope(silu1, tanh1, 1)
+
+        dx = [sbuf([P, EXPERTS * SLOTS], F32, f"dx{j}", f"x_win{j}") for j in range(3)]
         rows = out.rearrange("(p j) n -> j p n", j=PACK)
-        for j in range(PACK):
-            last_product(j, w1f1, daq1, (banks[0], banks[1], banks[6], banks[7])[j], dx1[:, j, :])
-            put(1, out_win[j], dx1[:, j, :])
+
+        def token_gradient(j, b, w1f, daq, acc, copy):
+            product(acc, w1f, j, daq)
+            copy(dx[j][:, parts[b]], acc[:])
+
+        def put(engine, j, first, count):
+            src = dx[j][:, first : first + count]
+            if engine == "vector":
+                nc.vector.tensor_copy(listed(out_win[j], first, count), src)
+            else:
+                nc.scalar.activation(listed(out_win[j], first, count), src, ACT.Copy)
+
+        def store(j):
             nc.sync.dma_start(rows[j], out_win[j][:])
+
+        PIECE = SLOTS // 2
+        token_gradient(1, 0, w1f0, daq0, banks[2], nc.scalar.copy)
+        token_gradient(0, 0, w1f0, daq0, banks[6], nc.scalar.copy)
+        second = [banks[7], banks[0], banks[1], banks[4]]
+        products(second, dyq1, w2q1)
+        put("scalar", 1, 0, PIECE)
+        put("scalar", 1, PIECE, PIECE)
+        w1f1 = quantized("w1f1", w1f_stage[:], E4M3)
+        last_stage = sbuf([P, PACK * K], BF16, "last_stage", "ts_picked")
+        gradient(1, tanh1, da, last_stage, second, [banks[5], banks[2]])
+        put("vector", 0, 0, PIECE)
+        daq1 = quantized("da1", last_stage[:], E5M2)
+        dx.append(sbuf([P, EXPERTS * SLOTS], F32, "dx3", "tx_picked"))
+        token_gradient(3, 0, w1f0, daq0, banks[5], nc.scalar.copy)
+        put("scalar", 3, 0, PIECE)
+        put("scalar", 3, PIECE, PIECE)
+
+        token_gradient(1, 1, w1f1, daq1, banks[6], nc.vector.tensor_copy)
+        token_gradient(3, 1, w1f1, daq1, banks[7], nc.vector.tensor_copy)
+        put("vector", 1, SLOTS, SLOTS)
+        store(1)
+        token_gradient(0, 1, w1f1, daq1, banks[0], nc.scalar.copy)
+        token_gradient(2, 1, w1f1, daq1, banks[1], nc.scalar.copy)
+        token_gradient(2, 0, w1f0, daq0, banks[7], nc.scalar.copy)
+        put("vector", 3, SLOTS, SLOTS)
+        store(3)
+        put("vector", 0, PIECE, SLOTS + PIECE)
+        store(0)
+        for first, count in ((0, 384), (384, 384), (768, 256)):
+            put("scalar", 2, first, count)
+        store(2)

@@ -94,9 +94,9 @@ def tile_attend_gxfull_sil_x_kernel(tc, xT, dyT, w1, w2, ts, tx, cf, offs, out):
         nc.sync.dma_start(x_win[2][:], x_planes[2])
         nc.sync.dma_start(x_win[3][:], x_planes[3])
         nc.sync.dma_start(dy_win[0][:], dy_planes[0])
-        nc.sync.dma_start(dy_win[1][:], dy_planes[1])
-        load_w2(0)
         load_w1(1)
+        load_w2(0)
+        nc.sync.dma_start(dy_win[1][:], dy_planes[1])
         nc.sync.dma_start(dy_win[2][:], dy_planes[2])
         nc.sync.dma_start(dy_win[3][:], dy_planes[3])
         load_w2(1)
@@ -229,7 +229,6 @@ def tile_attend_gxfull_sil_x_kernel(tc, xT, dyT, w1, w2, ts, tx, cf, offs, out):
         z0 = sbuf([P, PACK * K], F32, "z0", "x_win0")
         for b in range(EXPERTS):
             gather(dy_picked, dy_win, 0, b)
-        gather(dy_picked, dy_win, 1, 0)
         preactivation(0, z0, banks[0:4])
         xq1 = quantized("x1", woven[1][:], E4M3)
         ts_turned = turn_scales(1, banks[0:2])
@@ -240,87 +239,94 @@ def tile_attend_gxfull_sil_x_kernel(tc, xT, dyT, w1, w2, ts, tx, cf, offs, out):
         silu0 = sbuf([P, PACK * K], F32, "silu0", "x_win1")
         tanh0 = sbuf([P, PACK * K], F32, "tanh0", "x_win2")
         activations(z0, silu0, tanh0)
+        gather(dy_picked, dy_win, 1, 0)
+        turn_float32(w2_raw[0], woven[3], dict(enumerate(banks[4:8])))
         w1_bf1 = rounded("w1_bf1", w1_raw[1], "w1_bf0")
         scaled_silu(silu0, 0)
         interleave(w1_bf1, woven[2])
-        slope(silu0, tanh0, 0)
-        w1d1 = quantized("w1d1", woven[2][:], E4M3)
         scaled_silu(silu0, 1)
-        products(banks[0:4], xq1, w1d1)
+        w1d1 = quantized("w1d1", woven[2][:], E4M3)
+        slope(silu0, tanh0, 0)
         slope(silu0, tanh0, 1)
+        products(banks[0:4], xq1, w1d1)
         gather(dy_picked, dy_win, 2, 0)
-        gather(dy_picked, dy_win, 3, 0, nc.vector.tensor_copy)
-        turn_float32(w2_raw[0], woven[3], dict(enumerate(banks[4:8])))
+        gather(dy_picked, dy_win, 3, 0)
+        gather(dy_picked, dy_win, 1, 1)
         z1 = sbuf([P, PACK * K], F32, "z1", "x_win3")
         preactivation(1, z1, banks[0:4])
         interleave(dy_picked[0], woven[0])
         w2q0 = quantized("w2q0", woven[3][:], E4M3)
         dyq0 = quantized("dy0", woven[0][:], E5M2)
-        products(banks[4:8], dyq0, w2q0)
-        w1f_stage = sbuf([P, PACK * K], BF16, "w1f_stage", "x_picked0")
-        turn_weights(w1_bf1, w1f_stage, banks[0:2])
         da = sbuf([P, PACK * K], BF16, "da", "tx_picked")
         silu1 = sbuf([P, PACK * K], F32, "silu1", "tx_win")
         tanh1 = sbuf([P, PACK * K], F32, "tanh1", "ts_win")
         activations(z1, silu1, tanh1)
-        for t in (1, 2, 3):
+        for t in (2, 3):
             gather(dy_picked, dy_win, t, 1)
+        w2_stage = sbuf([P, PACK * K], BF16, "w2_stage", "x_picked0")
+        turn_float32(w2_raw[1], w2_stage, dict(enumerate(banks[4:8])))
+        products(banks[0:4], dyq0, w2q0)
         scaled_silu(silu1, 0)
-        gradient(0, tanh0, da, woven[1], banks[4:8], banks[2:4])
-        turn_float32(w2_raw[1], woven[3], {0: banks[0], 1: banks[1], 2: banks[4], 3: banks[5]})
-        slope(silu1, tanh1, 0)
+        gradient(0, tanh0, da, woven[1], banks[0:4], banks[0:2])
+        turn_weights(w1_bf1, woven[3], banks[2:4])
         scaled_silu(silu1, 1)
         interleave(dy_picked[1], woven[0])
+        w2q1 = quantized("w2q1", w2_stage[:], E4M3)
         daq0 = quantized("da0", woven[1][:], E5M2)
         dyq1 = quantized("dy1", woven[0][:], E5M2)
-        w2q1 = quantized("w2q1", woven[3][:], E4M3)
+        slope(silu1, tanh1, 0)
         slope(silu1, tanh1, 1)
 
-        dx = [sbuf([P, EXPERTS * SLOTS], F32, f"dx{j}", f"x_win{j}") for j in range(3)]
         rows = out.rearrange("(p j) n -> j p n", j=PACK)
+        PIECE = SLOTS // 2
 
-        def token_gradient(j, b, w1f, daq, acc, copy):
-            product(acc, w1f, j, daq)
-            copy(dx[j][:, parts[b]], acc[:])
+        def staged(name, acc, tag, copy=nc.scalar.copy):
+            dst = sbuf([P, SLOTS], F32, name, tag)
+            copy(dst[:], acc[:])
+            return dst
 
-        def put(engine, j, first, count):
-            src = dx[j][:, first : first + count]
-            if engine == "vector":
-                nc.vector.tensor_copy(listed(out_win[j], first, count), src)
-            else:
-                nc.scalar.activation(listed(out_win[j], first, count), src, ACT.Copy)
+        def on_vector(j, first, src):
+            nc.vector.tensor_copy(listed(out_win[j], first, src.shape[1]), src)
+
+        def on_scalar(j, first, src, pieces=(PIECE, PIECE)):
+            at = 0
+            for count in pieces:
+                nc.scalar.activation(listed(out_win[j], first + at, count), src[:, at : at + count], ACT.Copy)
+                at = at + count
 
         def store(j):
             nc.sync.dma_start(rows[j], out_win[j][:])
 
-        PIECE = SLOTS // 2
-        token_gradient(1, 0, w1f0, daq0, banks[2], nc.scalar.copy)
-        token_gradient(0, 0, w1f0, daq0, banks[6], nc.scalar.copy)
-        second = [banks[7], banks[0], banks[1], banks[4]]
-        products(second, dyq1, w2q1)
-        put("scalar", 1, 0, PIECE)
-        put("scalar", 1, PIECE, PIECE)
-        w1f1 = quantized("w1f1", w1f_stage[:], E4M3)
+        product(banks[0], w1f0, 1, daq0)
+        product(banks[1], w1f0, 0, daq0)
+        products(banks[4:8], dyq1, w2q1)
+        dx10 = staged("dx10", banks[0], "x_win0")
+        dx00 = sbuf([P, PIECE], F32, "dx00", "x_win1")
+        nc.scalar.copy(dx00[:], banks[1][:, 0:PIECE])
+        on_scalar(1, 0, dx10)
+        product(banks[0], w1f0, 3, daq0)
+        w1f1 = quantized("w1f1", woven[3][:], E4M3)
         last_stage = sbuf([P, PACK * K], BF16, "last_stage", "ts_picked")
-        gradient(1, tanh1, da, last_stage, second, [banks[5], banks[2]])
-        put("vector", 0, 0, PIECE)
+        gradient(1, tanh1, da, last_stage, banks[4:8], banks[2:4])
+        on_vector(0, 0, dx00[:])
         daq1 = quantized("da1", last_stage[:], E5M2)
-        dx.append(sbuf([P, EXPERTS * SLOTS], F32, "dx3", "tx_picked"))
-        token_gradient(3, 0, w1f0, daq0, banks[5], nc.scalar.copy)
-        put("scalar", 3, 0, PIECE)
-        put("scalar", 3, PIECE, PIECE)
+        late = sbuf([P, PIECE + SLOTS], F32, "late", "tx_picked")
+        nc.scalar.copy(late[:, 0:PIECE], banks[1][:, PIECE:SLOTS])
+        nc.scalar.copy(late[:, PIECE:], banks[0][:])
+        on_vector(0, PIECE, late[:, 0:PIECE])
+        on_scalar(3, 0, late[:, PIECE:])
 
-        token_gradient(1, 1, w1f1, daq1, banks[6], nc.vector.tensor_copy)
-        token_gradient(3, 1, w1f1, daq1, banks[7], nc.vector.tensor_copy)
-        put("vector", 1, SLOTS, SLOTS)
+        for j, acc in ((1, banks[4]), (3, banks[5]), (0, banks[6]), (2, banks[7])):
+            product(acc, w1f1, j, daq1)
+        on_vector(1, SLOTS, staged("dx11", banks[4], "x_win2", nc.vector.tensor_copy)[:])
         store(1)
-        token_gradient(0, 1, w1f1, daq1, banks[0], nc.scalar.copy)
-        token_gradient(2, 1, w1f1, daq1, banks[1], nc.scalar.copy)
-        token_gradient(2, 0, w1f0, daq0, banks[7], nc.scalar.copy)
-        put("vector", 3, SLOTS, SLOTS)
+        product(banks[4], w1f0, 2, daq0)
+        on_vector(3, SLOTS, staged("dx31", banks[5], "x_win3")[:])
         store(3)
-        put("vector", 0, PIECE, SLOTS + PIECE)
+        dx2 = sbuf([P, EXPERTS * SLOTS], F32, "dx2", "tx_win")
+        nc.scalar.copy(dx2[:, parts[0]], banks[4][:])
+        on_vector(0, SLOTS, staged("dx01", banks[6], "ts_win")[:])
         store(0)
-        for first, count in ((0, 384), (384, 384), (768, 256)):
-            put("scalar", 2, first, count)
+        nc.scalar.copy(dx2[:, parts[1]], banks[7][:])
+        on_scalar(2, 0, dx2, (384, 384, 256))
         store(2)

@@ -23,7 +23,6 @@ TOKENS = 2048
 LIST_COLS = SLOTS // 16
 ROW = P - 1
 ALIGN = 64
-RUN = 4
 
 FLOPS = 3 * EXPERTS * 2 * K * K * SLOTS
 
@@ -114,8 +113,8 @@ def tile_attend_gxfull_sil_x_kernel(tc, xT, dyT, w1, w2, ts, tx, cf, offs, out):
 
         def weave(copy, dst, planes):
             copy(
-                dst.rearrange("p (c i t) -> p c t i", t=PACK, i=RUN),
-                planes.rearrange("p t (c i) -> p c t i", i=RUN),
+                dst.rearrange("p (c t) -> p c t", t=PACK),
+                planes.rearrange("p t c -> p c t"),
             )
 
         def rounded(name, raw, tag=None):
@@ -165,7 +164,7 @@ def tile_attend_gxfull_sil_x_kernel(tc, xT, dyT, w1, w2, ts, tx, cf, offs, out):
             return src[:].rearrange("p (t i) -> p t i", t=PACK)
 
         gather(x_picked, x_win, 0, 0)
-        gather_on_scalar(picked[1][:], listed(ts_win, 0, EXPERTS * SLOTS))
+        nc.vector.tensor_copy(picked[1][:], listed(ts_win, 0, EXPERTS * SLOTS))
         gather(x_picked, x_win, 0, 1)
         tx_turned = turn_scales(0, banks[0:2])
         for c in range(PACK):
@@ -328,5 +327,6 @@ def tile_attend_gxfull_sil_x_kernel(tc, xT, dyT, w1, w2, ts, tx, cf, offs, out):
         on_vector(0, SLOTS, staged("dx01", banks[6], "ts_win")[:])
         store(0)
         nc.scalar.copy(dx2[:, parts[1]], banks[7][:])
-        on_scalar(2, 0, dx2, (384, 384, 256))
+        on_scalar(2, 0, dx2, (384, 384))
+        on_vector(2, 768, dx2[:, 768:])
         store(2)

@@ -181,12 +181,12 @@ def tile_attend_gxfull_sil_x_kernel(tc, xT, dyT, w1, w2, ts, tx, cf, offs, out):
             gather(x_picked, x_win, 1, b)
         w1_bf0 = rounded("w1_bf0", w1_raw[0])
         interleave(w1_bf0, woven[0])
-        gather(x_picked, x_win, 2, 0, nc.vector.tensor_copy)
+        gather(x_picked, x_win, 2, 0)
         w1d0 = quantized("w1d0", woven[0][:], E4M3)
         gather(x_picked, x_win, 3, 0, nc.vector.tensor_copy)
-        turn_pair(w1_bf0, woven[2], 0, banks[4])
         gather(x_picked, x_win, 2, 1)
-        turn_pair(w1_bf0, woven[2], 1, banks[5])
+        w1f_stage = sbuf([P, PACK * K], BF16, "w1f_stage", "x_win2")
+        turn_weights(w1_bf0, w1f_stage, banks[4:6])
         gather(x_picked, x_win, 3, 1)
 
         cf_rows = cf_row[:].unsqueeze(1).to_broadcast([P, 2, K])
@@ -231,12 +231,12 @@ def tile_attend_gxfull_sil_x_kernel(tc, xT, dyT, w1, w2, ts, tx, cf, offs, out):
         preactivation(0, z0, banks[0:4])
         xq1 = quantized("x1", woven[1][:], E4M3)
         ts_turned = turn_scales(1, banks[0:2])
-        w1f0 = quantized("w1f0", woven[2][:], E4M3, "x_picked1")
+        w1f0 = quantized("w1f0", w1f_stage[:], E4M3, "x_picked1")
         for b in range(EXPERTS):
             cols = slice(b * PACK, (b + 1) * PACK)
             nc.vector.scalar_tensor_tensor(gate[:, cols], ts_turned[b], -0.5, tx_col[:, cols], ALU.mult, ALU.mult)
         silu0 = sbuf([P, PACK * K], F32, "silu0", "x_win1")
-        tanh0 = sbuf([P, PACK * K], F32, "tanh0", "x_win2")
+        tanh0 = sbuf([P, PACK * K], F32, "tanh0")
         activations(z0, silu0, tanh0)
         gather(dy_picked, dy_win, 1, 0)
         turn_float32(w2_raw[0], woven[3], dict(enumerate(banks[4:8])))
@@ -249,7 +249,7 @@ def tile_attend_gxfull_sil_x_kernel(tc, xT, dyT, w1, w2, ts, tx, cf, offs, out):
         slope(silu0, tanh0, 1)
         products(banks[0:4], xq1, w1d1)
         gather(dy_picked, dy_win, 2, 0)
-        gather(dy_picked, dy_win, 3, 0)
+        gather(dy_picked, dy_win, 3, 0, nc.vector.tensor_copy)
         gather(dy_picked, dy_win, 1, 1)
         z1 = sbuf([P, PACK * K], F32, "z1", "x_win3")
         preactivation(1, z1, banks[0:4])
@@ -327,6 +327,5 @@ def tile_attend_gxfull_sil_x_kernel(tc, xT, dyT, w1, w2, ts, tx, cf, offs, out):
         on_vector(0, SLOTS, staged("dx01", banks[6], "ts_win")[:])
         store(0)
         nc.scalar.copy(dx2[:, parts[1]], banks[7][:])
-        on_scalar(2, 0, dx2, (384, 384))
-        on_vector(2, 768, dx2[:, 768:])
+        on_scalar(2, 0, dx2, (384, 384, 256))
         store(2)

@@ -23,6 +23,7 @@ TOKENS = 2048
 LIST_COLS = SLOTS // 16
 ROW = P - 1
 ALIGN = 64
+RUN = 4
 
 FLOPS = 3 * EXPERTS * 2 * K * K * SLOTS
 
@@ -113,8 +114,8 @@ def tile_attend_gxfull_sil_x_kernel(tc, xT, dyT, w1, w2, ts, tx, cf, offs, out):
 
         def weave(copy, dst, planes):
             copy(
-                dst.rearrange("p (c t) -> p c t", t=PACK),
-                planes.rearrange("p t c -> p c t"),
+                dst.rearrange("p (c i t) -> p c t i", t=PACK, i=RUN),
+                planes.rearrange("p t (c i) -> p c t i", i=RUN),
             )
 
         def rounded(name, raw, tag=None):

@@ -156,7 +156,8 @@ def tile_attend_gxfull_sil_x_kernel(tc, xT, dyT, w1, w2, ts, tx, cf, offs, out):
 
         gather_on_scalar(picked[0][:], listed(tx_win, 0, EXPERTS * SLOTS))
         x_picked = [sbuf([P, PACK * SLOTS], BF16, f"x_picked{b}") for b in range(EXPERTS)]
-        dy_picked = [sbuf([P, PACK * SLOTS], BF16, f"dy_picked{b}") for b in range(EXPERTS)]
+        dy_planes_tile = sbuf([P, (PACK + 1) * SLOTS], BF16, "dy_picked")
+        dy_picked = [dy_planes_tile[:, SLOTS:], dy_planes_tile[:, : PACK * SLOTS]]
 
         def gather(dst, windows, t, b, copy=gather_on_scalar):
             copy(dst[b][:, parts[t]], listed(windows[t], b * SLOTS, SLOTS))
@@ -223,16 +224,16 @@ def tile_attend_gxfull_sil_x_kernel(tc, xT, dyT, w1, w2, ts, tx, cf, offs, out):
                     turn_pair(da, stage, r // 2, turn[r // 2])
 
         interleave(x_picked[0], woven[1])
+        w1f0 = quantized("w1f0", w1f_stage[:], E4M3, "x_win3")
         xq0 = quantized("x0", woven[1][:], E4M3)
         products(banks[0:4], xq0, w1d0)
-        interleave(x_picked[1], woven[1])
+        interleave(x_picked[1], woven[3])
         z0 = sbuf([P, PACK * K], F32, "z0", "x_win0")
         for b in range(EXPERTS):
             gather(dy_picked, dy_win, 0, b)
         preactivation(0, z0, banks[0:4])
-        xq1 = quantized("x1", woven[1][:], E4M3)
+        xq1 = quantized("x1", woven[3][:], E4M3)
         ts_turned = turn_scales(1, banks[0:2])
-        w1f0 = quantized("w1f0", w1f_stage[:], E4M3, "x_picked1")
         for b in range(EXPERTS):
             cols = slice(b * PACK, (b + 1) * PACK)
             nc.vector.scalar_tensor_tensor(gate[:, cols], ts_turned[b], -0.5, tx_col[:, cols], ALU.mult, ALU.mult)
@@ -246,35 +247,34 @@ def tile_attend_gxfull_sil_x_kernel(tc, xT, dyT, w1, w2, ts, tx, cf, offs, out):
         interleave(w1_bf1, woven[2])
         scaled_silu(silu0, 1)
         w1d1 = quantized("w1d1", woven[2][:], E4M3)
-        slope(silu0, tanh0, 0)
-        slope(silu0, tanh0, 1)
+        nc.vector.scalar_tensor_tensor(tanh0[:], tanh0[:], 1.0, silu0[:], ALU.add, ALU.mult)
         products(banks[0:4], xq1, w1d1)
         gather(dy_picked, dy_win, 2, 0)
-        gather(dy_picked, dy_win, 3, 0, nc.vector.tensor_copy)
-        gather(dy_picked, dy_win, 1, 1)
-        z1 = sbuf([P, PACK * K], F32, "z1", "x_win3")
+        gather(dy_picked, dy_win, 3, 0)
+        z1 = sbuf([P, PACK * K], F32, "z1", "x_win2")
         preactivation(1, z1, banks[0:4])
         interleave(dy_picked[0], woven[0])
         w2q0 = quantized("w2q0", woven[3][:], E4M3)
         dyq0 = quantized("dy0", woven[0][:], E5M2)
+        w2_bf1 = rounded("w2_bf1", w2_raw[1], "w1_raw0")
         da = sbuf([P, PACK * K], BF16, "da", "tx_picked")
         silu1 = sbuf([P, PACK * K], F32, "silu1", "tx_win")
         tanh1 = sbuf([P, PACK * K], F32, "tanh1", "ts_win")
         activations(z1, silu1, tanh1)
-        for t in (2, 3):
+        for t in (1, 2, 3):
             gather(dy_picked, dy_win, t, 1)
-        w2_stage = sbuf([P, PACK * K], BF16, "w2_stage", "x_picked0")
-        turn_float32(w2_raw[1], w2_stage, dict(enumerate(banks[4:8])))
         products(banks[0:4], dyq0, w2q0)
         scaled_silu(silu1, 0)
         gradient(0, tanh0, da, woven[1], banks[0:4], banks[0:2])
+        w2_stage = sbuf([P, PACK * K], BF16, "w2_stage", "x_picked0")
+        turn_weights(w2_bf1, w2_stage, banks[4:6])
         turn_weights(w1_bf1, woven[3], banks[2:4])
         scaled_silu(silu1, 1)
         interleave(dy_picked[1], woven[0])
-        w2q1 = quantized("w2q1", w2_stage[:], E4M3)
-        daq0 = quantized("da0", woven[1][:], E5M2)
+        daq0 = quantized("da0", woven[1][:], E5M2, "dy_picked")
         dyq1 = quantized("dy1", woven[0][:], E5M2)
         slope(silu1, tanh1, 0)
+        w2q1 = quantized("w2q1", w2_stage[:], E4M3)
         slope(silu1, tanh1, 1)
 
         rows = out.rearrange("(p j) n -> j p n", j=PACK)
@@ -310,23 +310,26 @@ def tile_attend_gxfull_sil_x_kernel(tc, xT, dyT, w1, w2, ts, tx, cf, offs, out):
         gradient(1, tanh1, da, last_stage, banks[4:8], banks[2:4])
         on_vector(0, 0, dx00[:])
         daq1 = quantized("da1", last_stage[:], E5M2)
-        late = sbuf([P, PIECE + SLOTS], F32, "late", "tx_picked")
+        late = sbuf([P, PIECE + 2 * SLOTS], F32, "late", "tx_picked")
+        dx3 = late[:, PIECE:]
         nc.scalar.copy(late[:, 0:PIECE], banks[1][:, PIECE:SLOTS])
-        nc.scalar.copy(late[:, PIECE:], banks[0][:])
+        nc.scalar.copy(dx3[:, parts[0]], banks[0][:])
         on_vector(0, PIECE, late[:, 0:PIECE])
-        on_scalar(3, 0, late[:, PIECE:])
+        on_scalar(3, 0, dx3, (384,))
 
         for j, acc in ((1, banks[4]), (3, banks[5]), (0, banks[6]), (2, banks[7])):
             product(acc, w1f1, j, daq1)
-        on_vector(1, SLOTS, staged("dx11", banks[4], "x_win2", nc.vector.tensor_copy)[:])
+        on_vector(1, SLOTS, staged("dx11", banks[4], "w1_bf0", nc.vector.tensor_copy)[:])
         store(1)
         product(banks[4], w1f0, 2, daq0)
-        on_vector(3, SLOTS, staged("dx31", banks[5], "x_win3")[:])
-        store(3)
+        nc.scalar.copy(dx3[:, parts[1]], banks[5][:])
+        on_scalar(3, 384, dx3[:, 384:], (256,))
         dx2 = sbuf([P, EXPERTS * SLOTS], F32, "dx2", "tx_win")
         nc.scalar.copy(dx2[:, parts[0]], banks[4][:])
         on_vector(0, SLOTS, staged("dx01", banks[6], "ts_win")[:])
         store(0)
+        on_vector(3, 640, dx3[:, 640:])
+        store(3)
         nc.scalar.copy(dx2[:, parts[1]], banks[7][:])
         on_scalar(2, 0, dx2, (384, 384, 256))
         store(2)

@@ -90,19 +90,21 @@ def tile_attend_gxfull_sil_x_kernel(tc, xT, dyT, w1, w2, ts, tx, cf, offs, out):
         nc.sync.dma_start(ts_win[ROW:P, :], ts[0:1, :])
         nc.sync.dma_start(cf_col[:], cf.rearrange("(p c) o -> p (c o)", c=PACK))
         nc.sync.dma_start(x_win[1][:], x_planes[1])
-        load_w1(0)
         nc.sync.dma_start(x_win[2][:], x_planes[2])
+        load_w1(0)
         nc.sync.dma_start(x_win[3][:], x_planes[3])
         nc.sync.dma_start(dy_win[0][:], dy_planes[0])
-        load_w1(1)
-        load_w2(0)
         nc.sync.dma_start(dy_win[1][:], dy_planes[1])
+        load_w2(0)
+        load_w1(1)
+        load_w2(1)
         nc.sync.dma_start(dy_win[2][:], dy_planes[2])
         nc.sync.dma_start(dy_win[3][:], dy_planes[3])
-        load_w2(1)
 
         ident = sbuf([P, P], F32, "ident")
         make_identity(nc, ident[:])
+        warm = sbuf([P, 1], F32, "warm")
+        nc.scalar.activation(warm[:], ident[:, 0:1], ACT.Silu)
 
         nc.vector.memset(tx_win[0:ROW, :].bitcast(I32), 0)
         nc.vector.memset(ts_win[0:ROW, :].bitcast(I32), 0)
@@ -112,16 +114,11 @@ def tile_attend_gxfull_sil_x_kernel(tc, xT, dyT, w1, w2, ts, tx, cf, offs, out):
         def gather_on_scalar(dst, src):
             nc.scalar.activation(dst, src, ACT.Copy)
 
-        def weave(copy, dst, planes):
-            copy(
-                dst.rearrange("p (c i t) -> p c t i", t=PACK, i=RUN),
-                planes.rearrange("p t (c i) -> p c t i", i=RUN),
+        def interleave(src, stage):
+            nc.vector.tensor_copy(
+                stage[:].rearrange("p (c i t) -> p c t i", t=PACK, i=RUN),
+                src[:].rearrange("p (t c i) -> p c t i", t=PACK, i=RUN),
             )
-
-        def rounded(name, raw, tag=None):
-            dst = sbuf([P, PACK * K], BF16, name, tag)
-            nc.vector.tensor_copy(dst[:], raw[:])
-            return dst
 
         def turn_pair(src, dst, h, bank):
             for c in (2 * h, 2 * h + 1):
@@ -133,19 +130,26 @@ def tile_attend_gxfull_sil_x_kernel(tc, xT, dyT, w1, w2, ts, tx, cf, offs, out):
                 bank[:].rearrange("p (c u m) -> p c m u", c=2, u=2),
             )
 
-        def turn_float32(raw, dst, use):
+        def turn_w2(raw, dst, use):
             for c in use:
                 for t in range(PACK):
                     nc.tensor.transpose(use[c][:, blocks[t]], raw[:, c * K + t : (c + 1) * K : PACK], ident[:])
                 nc.scalar.copy(dst[:, parts[c]].rearrange("p (m t) -> p m t", t=PACK), quarters(use[c][:]).rearrange("p t m -> p m t"))
 
-        def turn_weights(src, dst, use):
-            for h in range(2):
-                turn_pair(src, dst, h, use[h])
+        halves = [slice(h * 2 * K, (h + 1) * 2 * K) for h in range(2)]
+
+        def turn_w1(src, dst, use):
+            words = src[:].bitcast(F32)
+            for u in range(2):
+                for t in range(PACK):
+                    nc.tensor.transpose(use[u][:, blocks[t]], words[:, 2 * t + u : 2 * K : 2 * PACK], ident[:])
+                nc.scalar.copy(
+                    dst[:, halves[u]].rearrange("q (e p t) -> q e p t", e=2, t=PACK),
+                    use[u][:].bitcast(BF16).rearrange("q (t p e) -> q e p t", t=PACK, e=2),
+                )
 
         picked = [sbuf([P, EXPERTS * SLOTS], F32, "tx_picked"), sbuf([P, EXPERTS * SLOTS], F32, "ts_picked")]
         tx_col = sbuf([P, EXPERTS * PACK], F32, "tx_col")
-        gate = sbuf([P, EXPERTS * PACK], F32, "gate")
 
         def turn_scales(n, use):
             for b in range(EXPERTS):
@@ -154,43 +158,19 @@ def tile_attend_gxfull_sil_x_kernel(tc, xT, dyT, w1, w2, ts, tx, cf, offs, out):
                     nc.tensor.transpose(use[b][:, blocks[r]], picked[n][:, first : first + P], ident[:])
             return [quarters(use[b][:])[:, :, ROW] for b in range(EXPERTS)]
 
-        gather_on_scalar(picked[0][:], listed(tx_win, 0, EXPERTS * SLOTS))
         x_picked = [sbuf([P, PACK * SLOTS], BF16, f"x_picked{b}") for b in range(EXPERTS)]
-        dy_planes_tile = sbuf([P, (PACK + 1) * SLOTS], BF16, "dy_picked")
-        dy_picked = [dy_planes_tile[:, SLOTS:], dy_planes_tile[:, : PACK * SLOTS]]
+        dy_picked = [sbuf([P, PACK * SLOTS], BF16, f"dy_picked{b}") for b in range(EXPERTS)]
 
         def gather(dst, windows, t, b, copy=gather_on_scalar):
             copy(dst[b][:, parts[t]], listed(windows[t], b * SLOTS, SLOTS))
 
-        def planes_of(src):
-            return src[:].rearrange("p (t i) -> p t i", t=PACK)
+        def stage(name, tag=None):
+            return sbuf([P, PACK * K], BF16, name, tag)
 
-        gather(x_picked, x_win, 0, 0)
-        nc.vector.tensor_copy(picked[1][:], listed(ts_win, 0, EXPERTS * SLOTS))
-        gather(x_picked, x_win, 0, 1)
-        tx_turned = turn_scales(0, banks[0:2])
-        for c in range(PACK):
-            nc.tensor.transpose(banks[2][:, blocks[c]], cf_col[:, c : c + 1].to_broadcast([P, P]), ident[:])
+        def wide(name, tag=None):
+            return sbuf([P, PACK * K], F32, name, tag)
+
         cf_row = sbuf([P, K], F32, "cf_row")
-        woven = [sbuf([P, PACK * K], BF16, f"woven{n}") for n in range(4)]
-
-        def interleave(src, stage):
-            weave(nc.vector.tensor_copy, stage[:], planes_of(src))
-
-        nc.scalar.copy(cf_row[:].rearrange("p (m c) -> p m c", c=PACK), quarters(banks[2][:]).rearrange("p c m -> p m c"))
-        for b in range(EXPERTS):
-            nc.vector.tensor_copy(tx_col[:, b * PACK : (b + 1) * PACK], tx_turned[b])
-            gather(x_picked, x_win, 1, b)
-        w1_bf0 = rounded("w1_bf0", w1_raw[0])
-        interleave(w1_bf0, woven[0])
-        gather(x_picked, x_win, 2, 0)
-        w1d0 = quantized("w1d0", woven[0][:], E4M3)
-        gather(x_picked, x_win, 3, 0, nc.vector.tensor_copy)
-        gather(x_picked, x_win, 2, 1)
-        w1f_stage = sbuf([P, PACK * K], BF16, "w1f_stage", "x_win2")
-        turn_weights(w1_bf0, w1f_stage, banks[4:6])
-        gather(x_picked, x_win, 3, 1)
-
         cf_rows = cf_row[:].unsqueeze(1).to_broadcast([P, 2, K])
 
         def products(use, stat, moving):
@@ -202,134 +182,169 @@ def tile_attend_gxfull_sil_x_kernel(tc, xT, dyT, w1, w2, ts, tx, cf, offs, out):
                 col = b * PACK + r
                 nc.vector.scalar_tensor_tensor(z[:, parts[r]], use[r][:], tx_col[:, col : col + 1], cf_row[:], ALU.mult, ALU.mult)
 
-        halves = [slice(h * 2 * K, (h + 1) * 2 * K) for h in range(2)]
-
-        def activations(z, silu, tanh):
+        def activations(z, silu):
             for h in halves:
                 nc.scalar.activation(silu[:, h], z[:, h], ACT.Silu, scale=-1.0)
-                nc.scalar.activation(tanh[:, h], z[:, h], ACT.Tanh, scale=0.5)
+            for h in halves:
+                nc.scalar.activation(z[:, h], z[:, h], ACT.Tanh, scale=0.5)
 
-        def scaled_silu(silu, h):
-            pair = silu[:, halves[h]].rearrange("p (r f) -> p r f", r=2)
-            nc.vector.scalar_tensor_tensor(pair, pair, 1.0, cf_rows, ALU.subtract, ALU.mult)
+        def scaled_silu(silu, scaled, h):
+            nc.vector.scalar_tensor_tensor(
+                scaled[:, halves[h]].rearrange("p (r f) -> p r f", r=2),
+                silu[:, halves[h]].rearrange("p (r f) -> p r f", r=2),
+                1.0,
+                cf_rows,
+                ALU.subtract,
+                ALU.mult,
+            )
 
-        def slope(silu, tanh, h):
-            nc.vector.scalar_tensor_tensor(tanh[:, halves[h]], tanh[:, halves[h]], 1.0, silu[:, halves[h]], ALU.add, ALU.mult)
+        def slope(scaled, tanh, h):
+            nc.vector.scalar_tensor_tensor(tanh[:, halves[h]], tanh[:, halves[h]], 1.0, scaled[:, halves[h]], ALU.add, ALU.mult)
 
-        def gradient(b, factor, da, stage, use, turn):
-            for r in range(PACK):
-                col = b * PACK + r
-                nc.vector.scalar_tensor_tensor(da[:, parts[r]], use[r][:], gate[:, col : col + 1], factor[:, parts[r]], ALU.mult, ALU.mult)
-                if r % 2:
-                    turn_pair(da, stage, r // 2, turn[r // 2])
+        def gradient(b, factor, da, use, r):
+            col = b * PACK + r
+            nc.vector.scalar_tensor_tensor(da[:, parts[r]], use[r][:], gate[:, col : col + 1], factor[:, parts[r]], ALU.mult, ALU.mult)
 
-        interleave(x_picked[0], woven[1])
-        w1f0 = quantized("w1f0", w1f_stage[:], E4M3, "x_win3")
-        xq0 = quantized("x0", woven[1][:], E4M3)
-        products(banks[0:4], xq0, w1d0)
-        interleave(x_picked[1], woven[3])
-        z0 = sbuf([P, PACK * K], F32, "z0", "x_win0")
+        gather_on_scalar(picked[0][:], listed(tx_win, 0, EXPERTS * SLOTS))
+        nc.vector.tensor_copy(picked[1][:], listed(ts_win, 0, EXPERTS * SLOTS))
         for b in range(EXPERTS):
-            gather(dy_picked, dy_win, 0, b)
-        preactivation(0, z0, banks[0:4])
-        xq1 = quantized("x1", woven[3][:], E4M3)
-        ts_turned = turn_scales(1, banks[0:2])
+            gather(x_picked, x_win, 0, b)
+        tx_turned = turn_scales(0, banks[0:2])
+        for c in range(PACK):
+            nc.tensor.transpose(banks[4][:, blocks[c]], cf_col[:, c : c + 1].to_broadcast([P, P]), ident[:])
+        nc.scalar.copy(cf_row[:].rearrange("p (m c) -> p m c", c=PACK), quarters(banks[4][:]).rearrange("p c m -> p m c"))
+        ts_turned = turn_scales(1, banks[2:4])
+        for b in range(EXPERTS):
+            nc.vector.tensor_copy(tx_col[:, b * PACK : (b + 1) * PACK], tx_turned[b])
+        for t in (1, 2):
+            for b in range(EXPERTS):
+                gather(x_picked, x_win, t, b)
+        w1d_stage = [stage(f"w1d_stage{b}") for b in range(EXPERTS)]
+        interleave(w1_raw[0], w1d_stage[0])
+        gate = sbuf([P, EXPERTS * PACK], F32, "gate", "w1_raw0")
         for b in range(EXPERTS):
             cols = slice(b * PACK, (b + 1) * PACK)
             nc.vector.scalar_tensor_tensor(gate[:, cols], ts_turned[b], -0.5, tx_col[:, cols], ALU.mult, ALU.mult)
-        silu0 = sbuf([P, PACK * K], F32, "silu0", "x_win1")
-        tanh0 = sbuf([P, PACK * K], F32, "tanh0")
-        activations(z0, silu0, tanh0)
-        gather(dy_picked, dy_win, 1, 0)
-        turn_float32(w2_raw[0], woven[3], dict(enumerate(banks[4:8])))
-        w1_bf1 = rounded("w1_bf1", w1_raw[1], "w1_bf0")
-        scaled_silu(silu0, 0)
-        interleave(w1_bf1, woven[2])
-        scaled_silu(silu0, 1)
-        w1d1 = quantized("w1d1", woven[2][:], E4M3)
-        nc.vector.scalar_tensor_tensor(tanh0[:], tanh0[:], 1.0, silu0[:], ALU.add, ALU.mult)
+        w1d0 = quantized("w1d0", w1d_stage[0][:], E4M3)
+        gather(x_picked, x_win, 3, 0, nc.vector.tensor_copy)
+        gather(x_picked, x_win, 3, 1)
+        w1f_stage0 = stage("w1f_stage0", "x_win3")
+        turn_w1(w1d_stage[0], w1f_stage0, banks[4:6])
+        x_stage = [stage(f"x_stage{b}") for b in range(EXPERTS)]
+        interleave(x_picked[0], x_stage[0])
+        xq0 = quantized("x0", x_stage[0][:], E4M3)
+        products(banks[0:4], xq0, w1d0)
+        interleave(x_picked[1], x_stage[1])
+        for t in range(2):
+            for b in range(EXPERTS):
+                gather(dy_picked, dy_win, t, b)
+
+        z0 = wide("z0", "x_win0")
+        preactivation(0, z0, banks[0:4])
+        xq1 = quantized("x1", x_stage[1][:], E4M3)
+        w1f0 = quantized("w1f0", w1f_stage0[:], E4M3)
+        silu0 = wide("silu0", "dy_win1")
+        activations(z0, silu0)
+        w2_stage0 = stage("w2_stage0", "x_picked0")
+        turn_w2(w2_raw[0], w2_stage0, dict(enumerate(banks[4:8])))
+        interleave(w1_raw[1], w1d_stage[1])
+        w1d1 = quantized("w1d1", w1d_stage[1][:], E4M3)
         products(banks[0:4], xq1, w1d1)
-        gather(dy_picked, dy_win, 2, 0)
-        gather(dy_picked, dy_win, 3, 0)
-        z1 = sbuf([P, PACK * K], F32, "z1", "x_win2")
+        scaled0 = wide("scaled0", "w1_raw1")
+        scaled_silu(silu0, scaled0, 0)
+        scaled_silu(silu0, scaled0, 1)
+        for t in range(2, PACK):
+            for b in range(EXPERTS):
+                gather(dy_picked, dy_win, t, b)
+        z1 = wide("z1", "x_win1")
         preactivation(1, z1, banks[0:4])
-        interleave(dy_picked[0], woven[0])
-        w2q0 = quantized("w2q0", woven[3][:], E4M3)
-        dyq0 = quantized("dy0", woven[0][:], E5M2)
-        w2_bf1 = rounded("w2_bf1", w2_raw[1], "w1_raw0")
-        da = sbuf([P, PACK * K], BF16, "da", "tx_picked")
-        silu1 = sbuf([P, PACK * K], F32, "silu1", "tx_win")
-        tanh1 = sbuf([P, PACK * K], F32, "tanh1", "ts_win")
-        activations(z1, silu1, tanh1)
-        for t in (1, 2, 3):
-            gather(dy_picked, dy_win, t, 1)
-        products(banks[0:4], dyq0, w2q0)
-        scaled_silu(silu1, 0)
-        gradient(0, tanh0, da, woven[1], banks[0:4], banks[0:2])
-        w2_stage = sbuf([P, PACK * K], BF16, "w2_stage", "x_picked0")
-        turn_weights(w2_bf1, w2_stage, banks[4:6])
-        turn_weights(w1_bf1, woven[3], banks[2:4])
-        scaled_silu(silu1, 1)
-        interleave(dy_picked[1], woven[0])
-        daq0 = quantized("da0", woven[1][:], E5M2, "dy_picked")
-        dyq1 = quantized("dy1", woven[0][:], E5M2)
-        slope(silu1, tanh1, 0)
-        w2q1 = quantized("w2q1", w2_stage[:], E4M3)
-        slope(silu1, tanh1, 1)
+        slope(scaled0, z0, 0)
+        slope(scaled0, z0, 1)
+        w2_round = stage("w2_round", "x_picked1")
+        nc.vector.tensor_copy(w2_round[:], w2_raw[1][:])
+        dy_stage = [stage(f"dy_stage{b}", f"x_stage{b}") for b in range(EXPERTS)]
+        interleave(dy_picked[0], dy_stage[0])
+        silu1 = wide("silu1", "dy_win3")
+        activations(z1, silu1)
+        w2q0 = quantized("w2q0", w2_stage0[:], E4M3)
+        dyq0 = quantized("dy0", dy_stage[0][:], E5M2)
+        products(banks[4:8], dyq0, w2q0)
+        interleave(dy_picked[1], dy_stage[1])
+
+        w2_stage1 = stage("w2_stage1", "dy_picked0")
+        for h in range(2):
+            turn_pair(w2_round, w2_stage1, h, banks[h])
+        da0 = stage("da0", "tx_picked")
+        da_stage0 = stage("da_stage0", "w2_raw0")
+        for r in range(PACK):
+            gradient(0, z0, da0, banks[4:8], r)
+            if r % 2:
+                turn_pair(da0, da_stage0, r // 2, banks[4 + r // 2])
+        w1f_stage1 = stage("w1f_stage1", "tx_picked")
+        turn_w1(w1d_stage[1], w1f_stage1, banks[2:4])
+        for h in range(2):
+            scaled_silu(silu1, silu1, h)
+        daq0 = quantized("da0", da_stage0[:], E5M2)
+        dyq1 = quantized("dy1", dy_stage[1][:], E5M2)
+        w2q1 = quantized("w2q1", w2_stage1[:], E4M3)
 
         rows = out.rearrange("(p j) n -> j p n", j=PACK)
         PIECE = SLOTS // 2
 
-        def staged(name, acc, tag, copy=nc.scalar.copy):
-            dst = sbuf([P, SLOTS], F32, name, tag)
-            copy(dst[:], acc[:])
-            return dst
-
         def on_vector(j, first, src):
             nc.vector.tensor_copy(listed(out_win[j], first, src.shape[1]), src)
 
-        def on_scalar(j, first, src, pieces=(PIECE, PIECE)):
-            at = 0
-            for count in pieces:
-                nc.scalar.activation(listed(out_win[j], first + at, count), src[:, at : at + count], ACT.Copy)
-                at = at + count
+        def on_scalar(j, first, src):
+            nc.scalar.activation(listed(out_win[j], first, src.shape[1]), src, ACT.Copy)
 
         def store(j):
             nc.sync.dma_start(rows[j], out_win[j][:])
 
-        product(banks[0], w1f0, 1, daq0)
-        product(banks[1], w1f0, 0, daq0)
-        products(banks[4:8], dyq1, w2q1)
-        dx10 = staged("dx10", banks[0], "x_win0")
-        dx00 = sbuf([P, PIECE], F32, "dx00", "x_win1")
-        nc.scalar.copy(dx00[:], banks[1][:, 0:PIECE])
-        on_scalar(1, 0, dx10)
-        product(banks[0], w1f0, 3, daq0)
-        w1f1 = quantized("w1f1", woven[3][:], E4M3)
-        last_stage = sbuf([P, PACK * K], BF16, "last_stage", "ts_picked")
-        gradient(1, tanh1, da, last_stage, banks[4:8], banks[2:4])
-        on_vector(0, 0, dx00[:])
-        daq1 = quantized("da1", last_stage[:], E5M2)
-        late = sbuf([P, PIECE + 2 * SLOTS], F32, "late", "tx_picked")
-        dx3 = late[:, PIECE:]
-        nc.scalar.copy(late[:, 0:PIECE], banks[1][:, PIECE:SLOTS])
-        nc.scalar.copy(dx3[:, parts[0]], banks[0][:])
-        on_vector(0, PIECE, late[:, 0:PIECE])
-        on_scalar(3, 0, dx3, (384,))
-
-        for j, acc in ((1, banks[4]), (3, banks[5]), (0, banks[6]), (2, banks[7])):
-            product(acc, w1f1, j, daq1)
-        on_vector(1, SLOTS, staged("dx11", banks[4], "w1_bf0", nc.vector.tensor_copy)[:])
-        store(1)
+        dx0 = sbuf([P, EXPERTS * SLOTS], F32, "dx0", "x_win2")
+        dx1_head = sbuf([P, PIECE], F32, "dx1_head", "dy_win0")
+        dh1 = [banks[6], banks[7], banks[0], banks[1]]
+        product(banks[4], w1f0, 0, daq0)
+        product(banks[5], w1f0, 1, daq0)
+        products(dh1, dyq1, w2q1)
+        nc.scalar.copy(dx0[:, parts[0]], banks[4][:])
+        nc.scalar.copy(dx1_head[:], banks[5][:, 0:PIECE])
+        on_scalar(0, 0, dx0[:, 0:PIECE])
+        on_scalar(1, 0, dx1_head[:])
         product(banks[4], w1f0, 2, daq0)
-        nc.scalar.copy(dx3[:, parts[1]], banks[5][:])
-        on_scalar(3, 384, dx3[:, 384:], (256,))
-        dx2 = sbuf([P, EXPERTS * SLOTS], F32, "dx2", "tx_win")
+        product(banks[2], w1f0, 3, daq0)
+        for h in range(2):
+            slope(silu1, z1, h)
+        w1f1 = quantized("w1f1", w1f_stage1[:], E4M3)
+        da1 = stage("da1", "dy_picked1")
+        da_stage1 = stage("da_stage1", "ts_picked")
+        for r in range(PACK):
+            gradient(1, z1, da1, dh1, r)
+            if r % 2:
+                turn_pair(da1, da_stage1, r // 2, dh1[r // 2])
+        on_vector(0, PIECE, dx0[:, PIECE:SLOTS])
+        daq1 = quantized("da1", da_stage1[:], E5M2)
+        late = sbuf([P, 3 * EXPERTS * SLOTS], F32, "late", "dy_picked1")
+        dx1, dx2, dx3 = [late[:, n * EXPERTS * SLOTS : (n + 1) * EXPERTS * SLOTS] for n in range(3)]
+        nc.scalar.copy(dx1[:, PIECE:SLOTS], banks[5][:, PIECE:SLOTS])
         nc.scalar.copy(dx2[:, parts[0]], banks[4][:])
-        on_vector(0, SLOTS, staged("dx01", banks[6], "ts_win")[:])
+        nc.scalar.copy(dx3[:, parts[0]], banks[2][:])
+        on_vector(1, PIECE, dx1[:, PIECE:SLOTS])
+        on_scalar(2, 0, dx2[:, 0:384])
+        on_scalar(3, 0, dx3[:, 0:384])
+
+        for j, acc in ((1, banks[0]), (0, banks[1]), (2, banks[3]), (3, banks[6])):
+            product(acc, w1f1, j, daq1)
+        nc.vector.tensor_copy(dx1[:, parts[1]], banks[0][:])
+        nc.vector.tensor_copy(dx0[:, parts[1]], banks[1][:])
+        on_vector(1, SLOTS, dx1[:, parts[1]])
+        store(1)
+        on_vector(0, SLOTS, dx0[:, parts[1]])
         store(0)
-        on_vector(3, 640, dx3[:, 640:])
-        store(3)
-        nc.scalar.copy(dx2[:, parts[1]], banks[7][:])
-        on_scalar(2, 0, dx2, (384, 384, 256))
+        nc.scalar.copy(dx2[:, parts[1]], banks[3][:])
+        nc.scalar.copy(dx3[:, parts[1]], banks[6][:])
+        on_scalar(2, 384, dx2[:, 384:768])
+        on_vector(2, 768, dx2[:, 768:])
         store(2)
+        on_scalar(3, 384, dx3[:, 384:768])
+        on_scalar(3, 768, dx3[:, 768:])
+        store(3)

@@ -90,16 +90,16 @@ def tile_attend_gxfull_sil_x_kernel(tc, xT, dyT, w1, w2, ts, tx, cf, offs, out):
         nc.sync.dma_start(ts_win[ROW:P, :], ts[0:1, :])
         nc.sync.dma_start(cf_col[:], cf.rearrange("(p c) o -> p (c o)", c=PACK))
         nc.sync.dma_start(x_win[1][:], x_planes[1])
-        nc.sync.dma_start(x_win[2][:], x_planes[2])
         load_w1(0)
+        nc.sync.dma_start(x_win[2][:], x_planes[2])
         nc.sync.dma_start(x_win[3][:], x_planes[3])
-        nc.sync.dma_start(dy_win[0][:], dy_planes[0])
-        nc.sync.dma_start(dy_win[1][:], dy_planes[1])
         load_w2(0)
+        nc.sync.dma_start(dy_win[0][:], dy_planes[0])
         load_w1(1)
-        load_w2(1)
+        nc.sync.dma_start(dy_win[1][:], dy_planes[1])
         nc.sync.dma_start(dy_win[2][:], dy_planes[2])
         nc.sync.dma_start(dy_win[3][:], dy_planes[3])
+        load_w2(1)
 
         ident = sbuf([P, P], F32, "ident")
         make_identity(nc, ident[:])
@@ -130,23 +130,11 @@ def tile_attend_gxfull_sil_x_kernel(tc, xT, dyT, w1, w2, ts, tx, cf, offs, out):
                 bank[:].rearrange("p (c u m) -> p c m u", c=2, u=2),
             )
 
-        def turn_w2(raw, dst, use):
-            for c in use:
-                for t in range(PACK):
-                    nc.tensor.transpose(use[c][:, blocks[t]], raw[:, c * K + t : (c + 1) * K : PACK], ident[:])
-                nc.scalar.copy(dst[:, parts[c]].rearrange("p (m t) -> p m t", t=PACK), quarters(use[c][:]).rearrange("p t m -> p m t"))
-
         halves = [slice(h * 2 * K, (h + 1) * 2 * K) for h in range(2)]
 
-        def turn_w1(src, dst, use):
-            words = src[:].bitcast(F32)
-            for u in range(2):
-                for t in range(PACK):
-                    nc.tensor.transpose(use[u][:, blocks[t]], words[:, 2 * t + u : 2 * K : 2 * PACK], ident[:])
-                nc.scalar.copy(
-                    dst[:, halves[u]].rearrange("q (e p t) -> q e p t", e=2, t=PACK),
-                    use[u][:].bitcast(BF16).rearrange("q (t p e) -> q e p t", t=PACK, e=2),
-                )
+        def turn_weights(src, dst, use):
+            for h in range(2):
+                turn_pair(src, dst, h, use[h])
 
         picked = [sbuf([P, EXPERTS * SLOTS], F32, "tx_picked"), sbuf([P, EXPERTS * SLOTS], F32, "ts_picked")]
         tx_col = sbuf([P, EXPERTS * PACK], F32, "tx_col")
@@ -159,7 +147,8 @@ def tile_attend_gxfull_sil_x_kernel(tc, xT, dyT, w1, w2, ts, tx, cf, offs, out):
             return [quarters(use[b][:])[:, :, ROW] for b in range(EXPERTS)]
 
         x_picked = [sbuf([P, PACK * SLOTS], BF16, f"x_picked{b}") for b in range(EXPERTS)]
-        dy_picked = [sbuf([P, PACK * SLOTS], BF16, f"dy_picked{b}") for b in range(EXPERTS)]
+        dy_planes_tile = sbuf([P, (PACK + 1) * SLOTS], BF16, "dy_picked")
+        dy_picked = [dy_planes_tile[:, SLOTS:], dy_planes_tile[:, : PACK * SLOTS]]
 
         def gather(dst, windows, t, b, copy=gather_on_scalar):
             copy(dst[b][:, parts[t]], listed(windows[t], b * SLOTS, SLOTS))
@@ -220,7 +209,9 @@ def tile_attend_gxfull_sil_x_kernel(tc, xT, dyT, w1, w2, ts, tx, cf, offs, out):
             for b in range(EXPERTS):
                 gather(x_picked, x_win, t, b)
         w1d_stage = [stage(f"w1d_stage{b}") for b in range(EXPERTS)]
-        interleave(w1_raw[0], w1d_stage[0])
+        w1_round0 = stage("w1_round0")
+        nc.vector.tensor_copy(w1_round0[:], w1_raw[0][:])
+        interleave(w1_round0, w1d_stage[0])
         gate = sbuf([P, EXPERTS * PACK], F32, "gate", "w1_raw0")
         for b in range(EXPERTS):
             cols = slice(b * PACK, (b + 1) * PACK)
@@ -229,64 +220,71 @@ def tile_attend_gxfull_sil_x_kernel(tc, xT, dyT, w1, w2, ts, tx, cf, offs, out):
         gather(x_picked, x_win, 3, 0, nc.vector.tensor_copy)
         gather(x_picked, x_win, 3, 1)
         w1f_stage0 = stage("w1f_stage0", "x_win3")
-        turn_w1(w1d_stage[0], w1f_stage0, banks[4:6])
+        turn_weights(w1_round0, w1f_stage0, banks[4:6])
         x_stage = [stage(f"x_stage{b}") for b in range(EXPERTS)]
         interleave(x_picked[0], x_stage[0])
         xq0 = quantized("x0", x_stage[0][:], E4M3)
         products(banks[0:4], xq0, w1d0)
         interleave(x_picked[1], x_stage[1])
-        for t in range(2):
-            for b in range(EXPERTS):
-                gather(dy_picked, dy_win, t, b)
+        w2_round0 = stage("w2_round0")
+        nc.scalar.copy(w2_round0[:], w2_raw[0][:])
+        for b in range(EXPERTS):
+            gather(dy_picked, dy_win, 0, b)
 
         z0 = wide("z0", "x_win0")
-        preactivation(0, z0, banks[0:4])
         xq1 = quantized("x1", x_stage[1][:], E4M3)
         w1f0 = quantized("w1f0", w1f_stage0[:], E4M3)
-        silu0 = wide("silu0", "dy_win1")
+        preactivation(0, z0, banks[0:4])
+        silu0 = wide("silu0", "x_win2")
         activations(z0, silu0)
-        w2_stage0 = stage("w2_stage0", "x_picked0")
-        turn_w2(w2_raw[0], w2_stage0, dict(enumerate(banks[4:8])))
-        interleave(w1_raw[1], w1d_stage[1])
-        w1d1 = quantized("w1d1", w1d_stage[1][:], E4M3)
-        products(banks[0:4], xq1, w1d1)
+        gather(dy_picked, dy_win, 1, 0)
+        gather(dy_picked, dy_win, 2, 0)
+        w1_round1 = stage("w1_round1", "w1_round0")
+        nc.vector.tensor_copy(w1_round1[:], w1_raw[1][:])
         scaled0 = wide("scaled0", "w1_raw1")
         scaled_silu(silu0, scaled0, 0)
+        interleave(w1_round1, w1d_stage[1])
         scaled_silu(silu0, scaled0, 1)
-        for t in range(2, PACK):
-            for b in range(EXPERTS):
-                gather(dy_picked, dy_win, t, b)
+        w2_stage0 = stage("w2_stage0", "x_win2")
+        turn_weights(w2_round0, w2_stage0, banks[6:8])
+        gather(dy_picked, dy_win, 3, 0)
+        w1d1 = quantized("w1d1", w1d_stage[1][:], E4M3)
+        products(banks[0:4], xq1, w1d1)
+        slope(scaled0, z0, 0)
         z1 = wide("z1", "x_win1")
         preactivation(1, z1, banks[0:4])
-        slope(scaled0, z0, 0)
-        slope(scaled0, z0, 1)
-        w2_round = stage("w2_round", "x_picked1")
-        nc.vector.tensor_copy(w2_round[:], w2_raw[1][:])
         dy_stage = [stage(f"dy_stage{b}", f"x_stage{b}") for b in range(EXPERTS)]
         interleave(dy_picked[0], dy_stage[0])
-        silu1 = wide("silu1", "dy_win3")
+        slope(scaled0, z0, 1)
+        silu1 = wide("silu1", "w2_raw0")
         activations(z1, silu1)
-        w2q0 = quantized("w2q0", w2_stage0[:], E4M3)
+        for t in (1, 2):
+            gather(dy_picked, dy_win, t, 1)
         dyq0 = quantized("dy0", dy_stage[0][:], E5M2)
+        w2q0 = quantized("w2q0", w2_stage0[:], E4M3)
         products(banks[4:8], dyq0, w2q0)
-        interleave(dy_picked[1], dy_stage[1])
+        w2_round1 = stage("w2_round1", "w2_round0")
+        nc.vector.tensor_copy(w2_round1[:], w2_raw[1][:])
 
-        w2_stage1 = stage("w2_stage1", "dy_picked0")
-        for h in range(2):
-            turn_pair(w2_round, w2_stage1, h, banks[h])
         da0 = stage("da0", "tx_picked")
-        da_stage0 = stage("da_stage0", "w2_raw0")
-        for r in range(PACK):
-            gradient(0, z0, da0, banks[4:8], r)
-            if r % 2:
-                turn_pair(da0, da_stage0, r // 2, banks[4 + r // 2])
-        w1f_stage1 = stage("w1f_stage1", "tx_picked")
-        turn_w1(w1d_stage[1], w1f_stage1, banks[2:4])
+        da_stage0 = stage("da_stage0", "x_picked1")
+        for h in range(2):
+            for r in (2 * h, 2 * h + 1):
+                gradient(0, z0, da0, banks[4:8], r)
+            if h:
+                gather(dy_picked, dy_win, 3, 1)
+            turn_pair(da0, da_stage0, h, banks[4 + h])
+        weight_stages = sbuf([P, 2 * PACK * K], BF16, "weight_stages", "tx_picked")
+        w2_stage1 = weight_stages[:, : PACK * K]
+        w1f_stage1 = weight_stages[:, PACK * K :]
+        turn_weights(w2_round1, w2_stage1, banks[0:2])
+        turn_weights(w1_round1, w1f_stage1, banks[2:4])
         for h in range(2):
             scaled_silu(silu1, silu1, h)
         daq0 = quantized("da0", da_stage0[:], E5M2)
-        dyq1 = quantized("dy1", dy_stage[1][:], E5M2)
+        interleave(dy_picked[1], dy_stage[1])
         w2q1 = quantized("w2q1", w2_stage1[:], E4M3)
+        dyq1 = quantized("dy1", dy_stage[1][:], E5M2)
 
         rows = out.rearrange("(p j) n -> j p n", j=PACK)
         PIECE = SLOTS // 2
@@ -300,51 +298,52 @@ def tile_attend_gxfull_sil_x_kernel(tc, xT, dyT, w1, w2, ts, tx, cf, offs, out):
         def store(j):
             nc.sync.dma_start(rows[j], out_win[j][:])
 
-        dx0 = sbuf([P, EXPERTS * SLOTS], F32, "dx0", "x_win2")
-        dx1_head = sbuf([P, PIECE], F32, "dx1_head", "dy_win0")
+        dx_early = sbuf([P, 2 * SLOTS], F32, "dx_early", "dy_win0")
         dh1 = [banks[6], banks[7], banks[0], banks[1]]
         product(banks[4], w1f0, 0, daq0)
         product(banks[5], w1f0, 1, daq0)
         products(dh1, dyq1, w2q1)
-        nc.scalar.copy(dx0[:, parts[0]], banks[4][:])
-        nc.scalar.copy(dx1_head[:], banks[5][:, 0:PIECE])
-        on_scalar(0, 0, dx0[:, 0:PIECE])
-        on_scalar(1, 0, dx1_head[:])
-        product(banks[4], w1f0, 2, daq0)
-        product(banks[2], w1f0, 3, daq0)
+        product(banks[2], w1f0, 2, daq0)
+        product(banks[3], w1f0, 3, daq0)
+        for j in range(2):
+            nc.scalar.copy(dx_early[:, parts[j]], banks[4 + j][:])
+        on_scalar(0, 0, dx_early[:, 0:PIECE])
+        on_scalar(1, 0, dx_early[:, SLOTS : SLOTS + PIECE])
+        on_scalar(0, PIECE, dx_early[:, PIECE:SLOTS])
         for h in range(2):
             slope(silu1, z1, h)
         w1f1 = quantized("w1f1", w1f_stage1[:], E4M3)
-        da1 = stage("da1", "dy_picked1")
+        da1 = stage("da1", "dy_picked")
         da_stage1 = stage("da_stage1", "ts_picked")
         for r in range(PACK):
             gradient(1, z1, da1, dh1, r)
             if r % 2:
                 turn_pair(da1, da_stage1, r // 2, dh1[r // 2])
-        on_vector(0, PIECE, dx0[:, PIECE:SLOTS])
+        on_vector(1, PIECE, dx_early[:, SLOTS + PIECE :])
         daq1 = quantized("da1", da_stage1[:], E5M2)
-        late = sbuf([P, 3 * EXPERTS * SLOTS], F32, "late", "dy_picked1")
-        dx1, dx2, dx3 = [late[:, n * EXPERTS * SLOTS : (n + 1) * EXPERTS * SLOTS] for n in range(3)]
-        nc.scalar.copy(dx1[:, PIECE:SLOTS], banks[5][:, PIECE:SLOTS])
-        nc.scalar.copy(dx2[:, parts[0]], banks[4][:])
-        nc.scalar.copy(dx3[:, parts[0]], banks[2][:])
-        on_vector(1, PIECE, dx1[:, PIECE:SLOTS])
-        on_scalar(2, 0, dx2[:, 0:384])
-        on_scalar(3, 0, dx3[:, 0:384])
+        late = sbuf([P, 2 * EXPERTS * SLOTS], F32, "late", "dy_picked")
+        dx2 = late[:, : EXPERTS * SLOTS]
+        dx3 = late[:, EXPERTS * SLOTS :]
+        nc.scalar.copy(dx2[:, parts[0]], banks[2][:])
+        nc.scalar.copy(dx3[:, parts[0]], banks[3][:])
+        on_vector(2, 0, dx2[:, 0:PIECE])
+        on_scalar(3, 0, dx3[:, 0:PIECE])
 
-        for j, acc in ((1, banks[0]), (0, banks[1]), (2, banks[3]), (3, banks[6])):
+        for j, acc in ((1, banks[4]), (0, banks[5]), (3, banks[0]), (2, banks[1])):
             product(acc, w1f1, j, daq1)
-        nc.vector.tensor_copy(dx1[:, parts[1]], banks[0][:])
-        nc.vector.tensor_copy(dx0[:, parts[1]], banks[1][:])
-        on_vector(1, SLOTS, dx1[:, parts[1]])
+        dx1 = sbuf([P, SLOTS], F32, "dx1", "dy_win1")
+        nc.vector.tensor_copy(dx1[:], banks[4][:])
+        on_vector(1, SLOTS, dx1[:])
         store(1)
-        on_vector(0, SLOTS, dx0[:, parts[1]])
+        dx0 = sbuf([P, SLOTS], F32, "dx0", "dy_win3")
+        nc.scalar.copy(dx0[:], banks[5][:])
+        nc.scalar.copy(dx3[:, parts[1]], banks[0][:])
+        on_scalar(0, SLOTS, dx0[:, 0:PIECE])
+        nc.scalar.copy(dx2[:, parts[1]], banks[1][:])
+        on_scalar(0, SLOTS + PIECE, dx0[:, PIECE:])
         store(0)
-        nc.scalar.copy(dx2[:, parts[1]], banks[3][:])
-        nc.scalar.copy(dx3[:, parts[1]], banks[6][:])
-        on_scalar(2, 384, dx2[:, 384:768])
-        on_vector(2, 768, dx2[:, 768:])
+        on_vector(2, PIECE, dx2[:, PIECE:])
         store(2)
-        on_scalar(3, 384, dx3[:, 384:768])
-        on_scalar(3, 768, dx3[:, 768:])
+        on_scalar(3, PIECE, dx3[:, PIECE:640])
+        on_scalar(3, 640, dx3[:, 640:])
         store(3)

@@ -72,39 +72,42 @@ def tile_attend_gxfull_sil_x_kernel(tc, xT, dyT, w1, w2, ts, tx, cf, offs, out):
         x_win = [sbuf([P, TOKENS], F32, f"x_win{t}") for t in range(PACK)]
         dy_win = [sbuf([P, TOKENS], F32, f"dy_win{t}") for t in range(PACK)]
         out_win = [sbuf([P, TOKENS], F32, f"out_win{j}") for j in range(PACK)]
-        w1_raw = [sbuf([P, PACK * K], F32, f"w1_raw{b}") for b in range(EXPERTS)]
+        w1_raw0 = sbuf([P, PACK * K], F32, "w1_raw0")
+        w1_raw1 = [sbuf([P, 2 * K], F32, f"w1_raw1{h}") for h in range(2)]
         w2_raw = [sbuf([P, PACK * K], F32, f"w2_raw{b}") for b in range(EXPERTS)]
         cf_col = sbuf([P, PACK], F32, "cf_col")
 
         x_planes = xT.rearrange("(p t) n -> t p n", t=PACK)
         dy_planes = dyT.rearrange("(p t) n -> t p n", t=PACK)
 
-        def load_w1(b):
-            nc.sync.dma_start(w1_raw[b][:], w1[b].rearrange("(p j) f -> p (j f)", j=PACK))
+        w1_rows = [w1[b].rearrange("(p j) f -> p (j f)", j=PACK) for b in range(EXPERTS)]
 
         def load_w2(b):
             nc.sync.dma_start(w2_raw[b][:].rearrange("p (c e) -> p c e", c=PACK), w2[b].rearrange("(c p) e -> p c e", p=P))
 
-        nc.sync.dma_start(tx_win[ROW:P, :], tx[0:1, :])
+        nc.scalar.dma_start(tx_win[ROW:P, :], tx[0:1, :])
+        nc.scalar.dma_start(ts_win[ROW:P, :], ts[0:1, :])
+        nc.scalar.dma_start(cf_col[:], cf.rearrange("(p c) o -> p (c o)", c=PACK))
         nc.sync.dma_start(x_win[0][:], x_planes[0])
-        nc.sync.dma_start(ts_win[ROW:P, :], ts[0:1, :])
-        nc.sync.dma_start(cf_col[:], cf.rearrange("(p c) o -> p (c o)", c=PACK))
         nc.sync.dma_start(x_win[1][:], x_planes[1])
-        load_w1(0)
+        nc.sync.dma_start(w1_raw0[:], w1_rows[0])
         nc.sync.dma_start(x_win[2][:], x_planes[2])
         nc.sync.dma_start(x_win[3][:], x_planes[3])
-        load_w2(0)
         nc.sync.dma_start(dy_win[0][:], dy_planes[0])
-        load_w1(1)
-        nc.sync.dma_start(dy_win[1][:], dy_planes[1])
-        nc.sync.dma_start(dy_win[2][:], dy_planes[2])
-        nc.sync.dma_start(dy_win[3][:], dy_planes[3])
+        for h in range(2):
+            nc.sync.dma_start(w1_raw1[h][:], w1_rows[1][:, h * 2 * K : (h + 1) * 2 * K])
+        load_w2(0)
+        for t in (2, 3, 1):
+            nc.sync.dma_start(dy_win[t][:], dy_planes[t])
         load_w2(1)
+
+        zero = sbuf([P, 8], F32, "zero")
+        nc.vector.memset(zero[:], 0.0)
+        warm = sbuf([P, 1], F32, "warm")
+        nc.scalar.activation(warm[:], zero[:, 0:1], ACT.Silu)
 
         ident = sbuf([P, P], F32, "ident")
         make_identity(nc, ident[:])
-        warm = sbuf([P, 1], F32, "warm")
-        nc.scalar.activation(warm[:], ident[:, 0:1], ACT.Silu)
 
         nc.vector.memset(tx_win[0:ROW, :].bitcast(I32), 0)
         nc.vector.memset(ts_win[0:ROW, :].bitcast(I32), 0)
@@ -130,6 +133,12 @@ def tile_attend_gxfull_sil_x_kernel(tc, xT, dyT, w1, w2, ts, tx, cf, offs, out):
                 bank[:].rearrange("p (c u m) -> p c m u", c=2, u=2),
             )
 
+        def turn_float32(raw, dst, use):
+            for c in range(PACK):
+                for t in range(PACK):
+                    nc.tensor.transpose(use[c][:, blocks[t]], raw[:, c * K + t : (c + 1) * K : PACK], ident[:])
+                nc.scalar.copy(dst[:, parts[c]].rearrange("p (m t) -> p m t", t=PACK), quarters(use[c][:]).rearrange("p t m -> p m t"))
+
         halves = [slice(h * 2 * K, (h + 1) * 2 * K) for h in range(2)]
 
         def turn_weights(src, dst, use):
@@ -147,8 +156,8 @@ def tile_attend_gxfull_sil_x_kernel(tc, xT, dyT, w1, w2, ts, tx, cf, offs, out):
             return [quarters(use[b][:])[:, :, ROW] for b in range(EXPERTS)]
 
         x_picked = [sbuf([P, PACK * SLOTS], BF16, f"x_picked{b}") for b in range(EXPERTS)]
-        dy_planes_tile = sbuf([P, (PACK + 1) * SLOTS], BF16, "dy_picked")
-        dy_picked = [dy_planes_tile[:, SLOTS:], dy_planes_tile[:, : PACK * SLOTS]]
+        dy_planes_tile = sbuf([P, (PACK + 2) * SLOTS], BF16, "dy_picked")
+        dy_picked = [dy_planes_tile[:, 2 * SLOTS :], dy_planes_tile[:, : PACK * SLOTS]]
 
         def gather(dst, windows, t, b, copy=gather_on_scalar):
             copy(dst[b][:, parts[t]], listed(windows[t], b * SLOTS, SLOTS))
@@ -171,16 +180,17 @@ def tile_attend_gxfull_sil_x_kernel(tc, xT, dyT, w1, w2, ts, tx, cf, offs, out):
                 col = b * PACK + r
                 nc.vector.scalar_tensor_tensor(z[:, parts[r]], use[r][:], tx_col[:, col : col + 1], cf_row[:], ALU.mult, ALU.mult)
 
-        def activations(z, silu):
-            for h in halves:
-                nc.scalar.activation(silu[:, h], z[:, h], ACT.Silu, scale=-1.0)
-            for h in halves:
-                nc.scalar.activation(z[:, h], z[:, h], ACT.Tanh, scale=0.5)
+        def silu_of(z, silu):
+            for h in range(2):
+                nc.scalar.activation(silu[h][:], z[:, halves[h]], ACT.Silu, scale=-1.0)
 
-        def scaled_silu(silu, scaled, h):
+        def tanh_of(z, h):
+            nc.scalar.activation(z[:, halves[h]], z[:, halves[h]], ACT.Tanh, scale=0.5)
+
+        def scaled_silu(silu, scaled):
             nc.vector.scalar_tensor_tensor(
-                scaled[:, halves[h]].rearrange("p (r f) -> p r f", r=2),
-                silu[:, halves[h]].rearrange("p (r f) -> p r f", r=2),
+                scaled[:].rearrange("p (r f) -> p r f", r=2),
+                silu[:].rearrange("p (r f) -> p r f", r=2),
                 1.0,
                 cf_rows,
                 ALU.subtract,
@@ -188,7 +198,10 @@ def tile_attend_gxfull_sil_x_kernel(tc, xT, dyT, w1, w2, ts, tx, cf, offs, out):
             )
 
         def slope(scaled, tanh, h):
-            nc.vector.scalar_tensor_tensor(tanh[:, halves[h]], tanh[:, halves[h]], 1.0, scaled[:, halves[h]], ALU.add, ALU.mult)
+            nc.vector.scalar_tensor_tensor(tanh[:, halves[h]], tanh[:, halves[h]], 1.0, scaled[:], ALU.add, ALU.mult)
+
+        def half(name, tag=None):
+            return sbuf([P, 2 * K], F32, name, tag)
 
         def gradient(b, factor, da, use, r):
             col = b * PACK + r
@@ -210,81 +223,86 @@ def tile_attend_gxfull_sil_x_kernel(tc, xT, dyT, w1, w2, ts, tx, cf, offs, out):
                 gather(x_picked, x_win, t, b)
         w1d_stage = [stage(f"w1d_stage{b}") for b in range(EXPERTS)]
         w1_round0 = stage("w1_round0")
-        nc.vector.tensor_copy(w1_round0[:], w1_raw[0][:])
-        interleave(w1_round0, w1d_stage[0])
+        interleave(w1_raw0, w1d_stage[0])
+        nc.vector.tensor_copy(w1_round0[:], w1_raw0[:])
+        w1d0 = quantized("w1d0", w1d_stage[0][:], E4M3)
         gate = sbuf([P, EXPERTS * PACK], F32, "gate", "w1_raw0")
         for b in range(EXPERTS):
             cols = slice(b * PACK, (b + 1) * PACK)
             nc.vector.scalar_tensor_tensor(gate[:, cols], ts_turned[b], -0.5, tx_col[:, cols], ALU.mult, ALU.mult)
-        w1d0 = quantized("w1d0", w1d_stage[0][:], E4M3)
         gather(x_picked, x_win, 3, 0, nc.vector.tensor_copy)
         gather(x_picked, x_win, 3, 1)
         w1f_stage0 = stage("w1f_stage0", "x_win3")
         turn_weights(w1_round0, w1f_stage0, banks[4:6])
-        x_stage = [stage(f"x_stage{b}") for b in range(EXPERTS)]
+        x_stage = [stage("x_stage0")]
         interleave(x_picked[0], x_stage[0])
+        x_stage.append(stage("x_stage1", "x_picked0"))
+        w1f0 = quantized("w1f0", w1f_stage0[:], E4M3)
         xq0 = quantized("x0", x_stage[0][:], E4M3)
         products(banks[0:4], xq0, w1d0)
         interleave(x_picked[1], x_stage[1])
-        w2_round0 = stage("w2_round0")
-        nc.scalar.copy(w2_round0[:], w2_raw[0][:])
         for b in range(EXPERTS):
             gather(dy_picked, dy_win, 0, b)
+        w1_round1 = stage("w1_round1", "w1_round0")
+        for h in range(2):
+            nc.scalar.copy(w1_round1[:, halves[h]], w1_raw1[h][:])
 
         z0 = wide("z0", "x_win0")
-        xq1 = quantized("x1", x_stage[1][:], E4M3)
-        w1f0 = quantized("w1f0", w1f_stage0[:], E4M3)
         preactivation(0, z0, banks[0:4])
-        silu0 = wide("silu0", "x_win2")
-        activations(z0, silu0)
-        gather(dy_picked, dy_win, 1, 0)
+        xq1 = quantized("x1", x_stage[1][:], E4M3)
+        silu0 = [half(f"silu0{h}", f"w1_raw1{h}") for h in range(2)]
+        silu_of(z0, silu0)
+        for h in range(2):
+            tanh_of(z0, h)
         gather(dy_picked, dy_win, 2, 0)
-        w1_round1 = stage("w1_round1", "w1_round0")
-        nc.vector.tensor_copy(w1_round1[:], w1_raw[1][:])
-        scaled0 = wide("scaled0", "w1_raw1")
-        scaled_silu(silu0, scaled0, 0)
+        w2_stage0 = stage("w2_stage0")
+        turn_float32(w2_raw[0], w2_stage0, banks[4:8])
         interleave(w1_round1, w1d_stage[1])
-        scaled_silu(silu0, scaled0, 1)
-        w2_stage0 = stage("w2_stage0", "x_win2")
-        turn_weights(w2_round0, w2_stage0, banks[6:8])
-        gather(dy_picked, dy_win, 3, 0)
-        w1d1 = quantized("w1d1", w1d_stage[1][:], E4M3)
+        scaled0 = [half("scaled0a", "x_picked1"), half("scaled0b", "x_picked0")]
+        scaled_silu(silu0[0], scaled0[0])
+        w1d1 = quantized("w1d1", w1d_stage[1][:], E4M3, "w1_raw10")
         products(banks[0:4], xq1, w1d1)
-        slope(scaled0, z0, 0)
-        z1 = wide("z1", "x_win1")
+        scaled_silu(silu0[1], scaled0[1])
+        for h in range(2):
+            slope(scaled0[h], z0, h)
+        gather(dy_picked, dy_win, 3, 0)
+        for b in range(EXPERTS):
+            gather(dy_picked, dy_win, 1, b)
+        z1 = wide("z1", "x_picked1")
         preactivation(1, z1, banks[0:4])
-        dy_stage = [stage(f"dy_stage{b}", f"x_stage{b}") for b in range(EXPERTS)]
+        dy_stage = [stage("dy_stage0", "x_stage0"), stage("dy_stage1", "x_win1")]
         interleave(dy_picked[0], dy_stage[0])
-        slope(scaled0, z0, 1)
-        silu1 = wide("silu1", "w2_raw0")
-        activations(z1, silu1)
-        for t in (1, 2):
+        silu1_tile = wide("silu1", "dy_win1")
+        silu1 = [silu1_tile[:, h] for h in halves]
+        silu_of(z1, silu1)
+        tanh_of(z1, 0)
+        for t in (2, 3):
             gather(dy_picked, dy_win, t, 1)
-        dyq0 = quantized("dy0", dy_stage[0][:], E5M2)
         w2q0 = quantized("w2q0", w2_stage0[:], E4M3)
-        products(banks[4:8], dyq0, w2q0)
-        w2_round1 = stage("w2_round1", "w2_round0")
+        w2_round1 = stage("w2_round1", "w2_raw0")
         nc.vector.tensor_copy(w2_round1[:], w2_raw[1][:])
+        dyq0 = quantized("dy0", dy_stage[0][:], E5M2)
+        products(banks[4:8], dyq0, w2q0)
+        scaled_silu(silu1[0], silu1[0])
 
         da0 = stage("da0", "tx_picked")
-        da_stage0 = stage("da_stage0", "x_picked1")
-        for h in range(2):
-            for r in (2 * h, 2 * h + 1):
-                gradient(0, z0, da0, banks[4:8], r)
-            if h:
-                gather(dy_picked, dy_win, 3, 1)
-            turn_pair(da0, da_stage0, h, banks[4 + h])
+        da_stage0 = stage("da_stage0", "x_picked0")
+        for r in range(PACK):
+            gradient(0, z0, da0, banks[4:8], r)
+            if r % 2:
+                turn_pair(da0, da_stage0, r // 2, banks[4 + r // 2])
+        tanh_of(z1, 1)
         weight_stages = sbuf([P, 2 * PACK * K], BF16, "weight_stages", "tx_picked")
         w2_stage1 = weight_stages[:, : PACK * K]
         w1f_stage1 = weight_stages[:, PACK * K :]
-        turn_weights(w2_round1, w2_stage1, banks[0:2])
+        turn_weights(w2_round1, w2_stage1, [banks[7], banks[5]])
         turn_weights(w1_round1, w1f_stage1, banks[2:4])
-        for h in range(2):
-            scaled_silu(silu1, silu1, h)
-        daq0 = quantized("da0", da_stage0[:], E5M2)
+        scaled_silu(silu1[1], silu1[1])
         interleave(dy_picked[1], dy_stage[1])
-        w2q1 = quantized("w2q1", w2_stage1[:], E4M3)
+        daq0 = quantized("da0", da_stage0[:], E5M2)
+        slope(silu1[0], z1, 0)
         dyq1 = quantized("dy1", dy_stage[1][:], E5M2)
+        w2q1 = quantized("w2q1", w2_stage1[:], E4M3)
 
         rows = out.rearrange("(p j) n -> j p n", j=PACK)
         PIECE = SLOTS // 2
@@ -298,20 +316,19 @@ def tile_attend_gxfull_sil_x_kernel(tc, xT, dyT, w1, w2, ts, tx, cf, offs, out):
         def store(j):
             nc.sync.dma_start(rows[j], out_win[j][:])
 
-        dx_early = sbuf([P, 2 * SLOTS], F32, "dx_early", "dy_win0")
-        dh1 = [banks[6], banks[7], banks[0], banks[1]]
-        product(banks[4], w1f0, 0, daq0)
-        product(banks[5], w1f0, 1, daq0)
+        dx0 = sbuf([P, EXPERTS * SLOTS], F32, "dx0", "dy_win0")
+        dx1 = sbuf([P, SLOTS], F32, "dx1", "ts_win")
+        dh1 = [banks[4], banks[6], banks[7], banks[5]]
+        product(banks[0], w1f0, 1, daq0)
+        product(banks[1], w1f0, 0, daq0)
         products(dh1, dyq1, w2q1)
         product(banks[2], w1f0, 2, daq0)
         product(banks[3], w1f0, 3, daq0)
-        for j in range(2):
-            nc.scalar.copy(dx_early[:, parts[j]], banks[4 + j][:])
-        on_scalar(0, 0, dx_early[:, 0:PIECE])
-        on_scalar(1, 0, dx_early[:, SLOTS : SLOTS + PIECE])
-        on_scalar(0, PIECE, dx_early[:, PIECE:SLOTS])
-        for h in range(2):
-            slope(silu1, z1, h)
+        nc.scalar.copy(dx1[:], banks[0][:])
+        nc.scalar.copy(dx0[:, parts[0]], banks[1][:])
+        on_scalar(1, 0, dx1[:, 0:PIECE])
+        on_scalar(0, 0, dx0[:, 0:384])
+        slope(silu1[1], z1, 1)
         w1f1 = quantized("w1f1", w1f_stage1[:], E4M3)
         da1 = stage("da1", "dy_picked")
         da_stage1 = stage("da_stage1", "ts_picked")
@@ -319,7 +336,7 @@ def tile_attend_gxfull_sil_x_kernel(tc, xT, dyT, w1, w2, ts, tx, cf, offs, out):
             gradient(1, z1, da1, dh1, r)
             if r % 2:
                 turn_pair(da1, da_stage1, r // 2, dh1[r // 2])
-        on_vector(1, PIECE, dx_early[:, SLOTS + PIECE :])
+        on_vector(1, PIECE, dx1[:, PIECE:])
         daq1 = quantized("da1", da_stage1[:], E5M2)
         late = sbuf([P, 2 * EXPERTS * SLOTS], F32, "late", "dy_picked")
         dx2 = late[:, : EXPERTS * SLOTS]
@@ -329,18 +346,17 @@ def tile_attend_gxfull_sil_x_kernel(tc, xT, dyT, w1, w2, ts, tx, cf, offs, out):
         on_vector(2, 0, dx2[:, 0:PIECE])
         on_scalar(3, 0, dx3[:, 0:PIECE])
 
-        for j, acc in ((1, banks[4]), (0, banks[5]), (3, banks[0]), (2, banks[1])):
+        for j, acc in ((1, banks[0]), (0, banks[1]), (3, banks[7]), (2, banks[5])):
             product(acc, w1f1, j, daq1)
-        dx1 = sbuf([P, SLOTS], F32, "dx1", "dy_win1")
-        nc.vector.tensor_copy(dx1[:], banks[4][:])
-        on_vector(1, SLOTS, dx1[:])
+        dx1_last = sbuf([P, SLOTS], F32, "dx1_last", "tx_win")
+        nc.vector.tensor_copy(dx1_last[:], banks[0][:])
+        on_vector(1, SLOTS, dx1_last[:])
         store(1)
-        dx0 = sbuf([P, SLOTS], F32, "dx0", "dy_win3")
-        nc.scalar.copy(dx0[:], banks[5][:])
-        nc.scalar.copy(dx3[:, parts[1]], banks[0][:])
-        on_scalar(0, SLOTS, dx0[:, 0:PIECE])
-        nc.scalar.copy(dx2[:, parts[1]], banks[1][:])
-        on_scalar(0, SLOTS + PIECE, dx0[:, PIECE:])
+        nc.scalar.copy(dx0[:, parts[1]], banks[1][:])
+        nc.scalar.copy(dx3[:, parts[1]], banks[7][:])
+        on_scalar(0, 384, dx0[:, 384:640])
+        nc.scalar.copy(dx2[:, parts[1]], banks[5][:])
+        on_scalar(0, 640, dx0[:, 640:])
         store(0)
         on_vector(2, PIECE, dx2[:, PIECE:])
         store(2)

@@ -97,9 +97,10 @@ def tile_attend_gxfull_sil_x_kernel(tc, xT, dyT, w1, w2, ts, tx, cf, offs, out):
         for h in range(2):
             nc.sync.dma_start(w1_raw1[h][:], w1_rows[1][:, h * 2 * K : (h + 1) * 2 * K])
         load_w2(0)
-        for t in (2, 3, 1):
+        for t in (2, 3):
             nc.sync.dma_start(dy_win[t][:], dy_planes[t])
         load_w2(1)
+        nc.sync.dma_start(dy_win[1][:], dy_planes[1])
 
         zero = sbuf([P, 8], F32, "zero")
         nc.vector.memset(zero[:], 0.0)
@@ -184,8 +185,8 @@ def tile_attend_gxfull_sil_x_kernel(tc, xT, dyT, w1, w2, ts, tx, cf, offs, out):
             for h in range(2):
                 nc.scalar.activation(silu[h][:], z[:, halves[h]], ACT.Silu, scale=-1.0)
 
-        def tanh_of(z, h):
-            nc.scalar.activation(z[:, halves[h]], z[:, halves[h]], ACT.Tanh, scale=0.5)
+        def tanh_of(z, h, dst):
+            nc.scalar.activation(dst, z[:, halves[h]], ACT.Tanh, scale=0.5)
 
         def scaled_silu(silu, scaled):
             nc.vector.scalar_tensor_tensor(
@@ -197,8 +198,8 @@ def tile_attend_gxfull_sil_x_kernel(tc, xT, dyT, w1, w2, ts, tx, cf, offs, out):
                 ALU.mult,
             )
 
-        def slope(scaled, tanh, h):
-            nc.vector.scalar_tensor_tensor(tanh[:, halves[h]], tanh[:, halves[h]], 1.0, scaled[:], ALU.add, ALU.mult)
+        def slope(scaled, tanh, dst):
+            nc.vector.scalar_tensor_tensor(dst, tanh, 1.0, scaled[:], ALU.add, ALU.mult)
 
         def half(name, tag=None):
             return sbuf([P, 2 * K], F32, name, tag)
@@ -253,18 +254,23 @@ def tile_attend_gxfull_sil_x_kernel(tc, xT, dyT, w1, w2, ts, tx, cf, offs, out):
         silu0 = [half(f"silu0{h}", f"w1_raw1{h}") for h in range(2)]
         silu_of(z0, silu0)
         for h in range(2):
-            tanh_of(z0, h)
+            tanh_of(z0, h, z0[:, halves[h]])
         gather(dy_picked, dy_win, 2, 0)
         w2_stage0 = stage("w2_stage0")
         turn_float32(w2_raw[0], w2_stage0, banks[4:8])
         interleave(w1_round1, w1d_stage[1])
-        scaled0 = [half("scaled0a", "x_picked1"), half("scaled0b", "x_picked0")]
-        scaled_silu(silu0[0], scaled0[0])
+        scaled0a = half("scaled0a", "x_picked1")
+        scaled_silu(silu0[0], scaled0a)
         w1d1 = quantized("w1d1", w1d_stage[1][:], E4M3, "w1_raw10")
         products(banks[0:4], xq1, w1d1)
-        scaled_silu(silu0[1], scaled0[1])
-        for h in range(2):
-            slope(scaled0[h], z0, h)
+        scaled0b = [sbuf([P, K], F32, "scaled0c", "x_picked0"), sbuf([P, K], F32, "scaled0d")]
+        for r in range(2):
+            nc.vector.scalar_tensor_tensor(scaled0b[r][:], silu0[1][:, parts[r]], 1.0, cf_row[:], ALU.subtract, ALU.mult)
+        slope(scaled0a, z0[:, halves[0]], z0[:, halves[0]])
+        for r in range(2):
+            slope(scaled0b[r], z0[:, parts[2 + r]], z0[:, parts[2 + r]])
+        w2_round1 = stage("w2_round1", "x_picked0")
+        nc.gpsimd.tensor_scalar(w2_round1[:], w2_raw[1][:], 1.0, 0.0, ALU.mult, ALU.add)
         gather(dy_picked, dy_win, 3, 0)
         for b in range(EXPERTS):
             gather(dy_picked, dy_win, 1, b)
@@ -275,32 +281,30 @@ def tile_attend_gxfull_sil_x_kernel(tc, xT, dyT, w1, w2, ts, tx, cf, offs, out):
         silu1_tile = wide("silu1", "dy_win1")
         silu1 = [silu1_tile[:, h] for h in halves]
         silu_of(z1, silu1)
-        tanh_of(z1, 0)
+        tanh_of(z1, 0, z1[:, halves[0]])
         for t in (2, 3):
             gather(dy_picked, dy_win, t, 1)
-        w2q0 = quantized("w2q0", w2_stage0[:], E4M3)
-        w2_round1 = stage("w2_round1", "w2_raw0")
-        nc.vector.tensor_copy(w2_round1[:], w2_raw[1][:])
+        w2q0 = quantized("w2q0", w2_stage0[:], E4M3, "scaled0d")
         dyq0 = quantized("dy0", dy_stage[0][:], E5M2)
         products(banks[4:8], dyq0, w2q0)
         scaled_silu(silu1[0], silu1[0])
 
         da0 = stage("da0", "tx_picked")
-        da_stage0 = stage("da_stage0", "x_picked0")
+        da_stage0 = stage("da_stage0", "w2_raw0")
         for r in range(PACK):
             gradient(0, z0, da0, banks[4:8], r)
             if r % 2:
                 turn_pair(da0, da_stage0, r // 2, banks[4 + r // 2])
-        tanh_of(z1, 1)
-        weight_stages = sbuf([P, 2 * PACK * K], BF16, "weight_stages", "tx_picked")
-        w2_stage1 = weight_stages[:, : PACK * K]
-        w1f_stage1 = weight_stages[:, PACK * K :]
-        turn_weights(w2_round1, w2_stage1, [banks[7], banks[5]])
-        turn_weights(w1_round1, w1f_stage1, banks[2:4])
+        w2_stage1 = stage("w2_stage1", "x_stage0")
+        turn_weights(w2_round1, w2_stage1, banks[6:8])
+        tanh1b = half("tanh1b", "tx_picked")
+        tanh_of(z1, 1, tanh1b[:])
+        w1f_stage1 = stage("w1f_stage1", "x_win3")
+        turn_weights(w1_round1, w1f_stage1, banks[4:6])
         scaled_silu(silu1[1], silu1[1])
         interleave(dy_picked[1], dy_stage[1])
         daq0 = quantized("da0", da_stage0[:], E5M2)
-        slope(silu1[0], z1, 0)
+        slope(silu1[0], z1[:, halves[0]], z1[:, halves[0]])
         dyq1 = quantized("dy1", dy_stage[1][:], E5M2)
         w2q1 = quantized("w2q1", w2_stage1[:], E4M3)
 
@@ -318,17 +322,17 @@ def tile_attend_gxfull_sil_x_kernel(tc, xT, dyT, w1, w2, ts, tx, cf, offs, out):
 
         dx0 = sbuf([P, EXPERTS * SLOTS], F32, "dx0", "dy_win0")
         dx1 = sbuf([P, SLOTS], F32, "dx1", "ts_win")
-        dh1 = [banks[4], banks[6], banks[7], banks[5]]
+        dh1 = [banks[2], banks[3], banks[6], banks[7]]
         product(banks[0], w1f0, 1, daq0)
         product(banks[1], w1f0, 0, daq0)
         products(dh1, dyq1, w2q1)
-        product(banks[2], w1f0, 2, daq0)
-        product(banks[3], w1f0, 3, daq0)
+        product(banks[4], w1f0, 2, daq0)
+        product(banks[5], w1f0, 3, daq0)
         nc.scalar.copy(dx1[:], banks[0][:])
-        nc.scalar.copy(dx0[:, parts[0]], banks[1][:])
+        nc.scalar.copy(dx0[:, 0:PIECE], banks[1][:, 0:PIECE])
         on_scalar(1, 0, dx1[:, 0:PIECE])
-        on_scalar(0, 0, dx0[:, 0:384])
-        slope(silu1[1], z1, 1)
+        on_scalar(0, 0, dx0[:, 0:PIECE])
+        slope(silu1[1], tanh1b[:], z1[:, halves[1]])
         w1f1 = quantized("w1f1", w1f_stage1[:], E4M3)
         da1 = stage("da1", "dy_picked")
         da_stage1 = stage("da_stage1", "ts_picked")
@@ -338,28 +342,31 @@ def tile_attend_gxfull_sil_x_kernel(tc, xT, dyT, w1, w2, ts, tx, cf, offs, out):
                 turn_pair(da1, da_stage1, r // 2, dh1[r // 2])
         on_vector(1, PIECE, dx1[:, PIECE:])
         daq1 = quantized("da1", da_stage1[:], E5M2)
-        late = sbuf([P, 2 * EXPERTS * SLOTS], F32, "late", "dy_picked")
+        late = sbuf([P, 2 * EXPERTS * SLOTS + PIECE], F32, "late", "dy_picked")
         dx2 = late[:, : EXPERTS * SLOTS]
-        dx3 = late[:, EXPERTS * SLOTS :]
-        nc.scalar.copy(dx2[:, parts[0]], banks[2][:])
-        nc.scalar.copy(dx3[:, parts[0]], banks[3][:])
-        on_vector(2, 0, dx2[:, 0:PIECE])
-        on_scalar(3, 0, dx3[:, 0:PIECE])
+        dx3 = late[:, EXPERTS * SLOTS : 2 * EXPERTS * SLOTS]
+        dx0_rest = late[:, 2 * EXPERTS * SLOTS :]
+        nc.scalar.copy(dx0_rest, banks[1][:, PIECE:])
+        nc.scalar.copy(dx2[:, parts[0]], banks[4][:])
+        on_scalar(0, PIECE, dx0_rest)
+        nc.scalar.copy(dx3[:, parts[0]], banks[5][:])
+        on_vector(2, 0, dx2[:, 0:384])
 
-        for j, acc in ((1, banks[0]), (0, banks[1]), (3, banks[7]), (2, banks[5])):
+        for j, acc in ((0, banks[2]), (1, banks[0]), (3, banks[6]), (2, banks[7])):
             product(acc, w1f1, j, daq1)
+        nc.scalar.copy(dx0[:, parts[1]], banks[2][:])
         dx1_last = sbuf([P, SLOTS], F32, "dx1_last", "tx_win")
         nc.vector.tensor_copy(dx1_last[:], banks[0][:])
+        nc.vector.tensor_copy(dx3[:, parts[1]], banks[6][:])
         on_vector(1, SLOTS, dx1_last[:])
         store(1)
-        nc.scalar.copy(dx0[:, parts[1]], banks[1][:])
-        nc.scalar.copy(dx3[:, parts[1]], banks[7][:])
-        on_scalar(0, 384, dx0[:, 384:640])
-        nc.scalar.copy(dx2[:, parts[1]], banks[5][:])
-        on_scalar(0, 640, dx0[:, 640:])
+        on_scalar(3, 0, dx3[:, 0:320])
+        on_scalar(0, SLOTS, dx0[:, SLOTS : SLOTS + PIECE])
+        nc.scalar.copy(dx2[:, parts[1]], banks[7][:])
+        on_scalar(0, SLOTS + PIECE, dx0[:, SLOTS + PIECE :])
         store(0)
-        on_vector(2, PIECE, dx2[:, PIECE:])
+        on_vector(2, 384, dx2[:, 384:])
         store(2)
-        on_scalar(3, PIECE, dx3[:, PIECE:640])
-        on_scalar(3, 640, dx3[:, 640:])
+        on_scalar(3, 320, dx3[:, 320:704])
+        on_scalar(3, 704, dx3[:, 704:])
         store(3)

@@ -32,10 +32,14 @@ def tile_attend_gxfull_sil_x_kernel(tc, xT, dyT, w1, w2, ts, tx, cf, offs, out):
     nc = tc.nc
     with ExitStack() as ctx:
         keep = ctx.enter_context(tc.tile_pool(name="keep", bufs=1))
+        shared = ctx.enter_context(tc.tile_pool(name="shared", bufs=1))
         psum = ctx.enter_context(tc.psum_pool(name="psum", bufs=1))
 
         def sbuf(shape, dtype, name, tag=None):
             return keep.tile(shape, dtype, name=name, tag=tag or name, align_bytes=ALIGN)
+
+        def placed(shape, dtype, name, quarter):
+            return shared.tile(shape, dtype, name=name, offset=quarter * K * 4, align_bytes=ALIGN)
 
         banks = [psum.tile([P, SLOTS], F32, name=f"bank{n}") for n in range(8)]
         blocks = [slice(r * P, (r + 1) * P) for r in range(PACK)]
@@ -44,8 +48,8 @@ def tile_attend_gxfull_sil_x_kernel(tc, xT, dyT, w1, w2, ts, tx, cf, offs, out):
         def quarters(ap):
             return ap.rearrange("p (a m) -> p a m", m=P)
 
-        def quantized(name, woven, fmt, tag=None):
-            codes = sbuf([P, K], U32, name + "_codes", tag)
+        def quantized(name, woven, fmt, codes=None):
+            codes = sbuf([P, K], U32, name + "_codes") if codes is None else codes
             scales = sbuf([P, K], U8, name + "_scales")
             nc.vector.quantize_mx(out=codes[:].bitcast(fmt), scales=scales[:], in_=woven)
             return codes, scales, fmt
@@ -72,8 +76,7 @@ def tile_attend_gxfull_sil_x_kernel(tc, xT, dyT, w1, w2, ts, tx, cf, offs, out):
         x_win = [sbuf([P, TOKENS], F32, f"x_win{t}") for t in range(PACK)]
         dy_win = [sbuf([P, TOKENS], F32, f"dy_win{t}") for t in range(PACK)]
         out_win = [sbuf([P, TOKENS], F32, f"out_win{j}") for j in range(PACK)]
-        w1_raw0 = sbuf([P, PACK * K], F32, "w1_raw0")
-        w1_raw1 = [sbuf([P, 2 * K], F32, f"w1_raw1{h}") for h in range(2)]
+        w1_raw = [sbuf([P, PACK * K], F32, "w1_raw0"), placed([P, PACK * K], F32, "w1_raw1", 0)]
         w2_raw = [sbuf([P, PACK * K], F32, f"w2_raw{b}") for b in range(EXPERTS)]
         cf_col = sbuf([P, PACK], F32, "cf_col")
 
@@ -90,17 +93,15 @@ def tile_attend_gxfull_sil_x_kernel(tc, xT, dyT, w1, w2, ts, tx, cf, offs, out):
         nc.scalar.dma_start(cf_col[:], cf.rearrange("(p c) o -> p (c o)", c=PACK))
         nc.sync.dma_start(x_win[0][:], x_planes[0])
         nc.sync.dma_start(x_win[1][:], x_planes[1])
-        nc.sync.dma_start(w1_raw0[:], w1_rows[0])
+        nc.sync.dma_start(w1_raw[0][:], w1_rows[0])
         nc.sync.dma_start(x_win[2][:], x_planes[2])
         nc.sync.dma_start(x_win[3][:], x_planes[3])
         nc.sync.dma_start(dy_win[0][:], dy_planes[0])
-        for h in range(2):
-            nc.sync.dma_start(w1_raw1[h][:], w1_rows[1][:, h * 2 * K : (h + 1) * 2 * K])
         load_w2(0)
-        for t in (2, 3):
+        nc.sync.dma_start(w1_raw[1][:], w1_rows[1])
+        for t in (2, 3, 1):
             nc.sync.dma_start(dy_win[t][:], dy_planes[t])
         load_w2(1)
-        nc.sync.dma_start(dy_win[1][:], dy_planes[1])
 
         zero = sbuf([P, 8], F32, "zero")
         nc.vector.memset(zero[:], 0.0)
@@ -118,10 +119,11 @@ def tile_attend_gxfull_sil_x_kernel(tc, xT, dyT, w1, w2, ts, tx, cf, offs, out):
         def gather_on_scalar(dst, src):
             nc.scalar.activation(dst, src, ACT.Copy)
 
-        def interleave(src, stage):
-            nc.vector.tensor_copy(
-                stage[:].rearrange("p (c i t) -> p c t i", t=PACK, i=RUN),
-                src[:].rearrange("p (t c i) -> p c t i", t=PACK, i=RUN),
+        def interleave(src, stage, copy=nc.vector.tensor_copy, half=None):
+            runs = slice(None) if half is None else slice(half * P // 2, (half + 1) * P // 2)
+            copy(
+                stage[:].rearrange("p (c i t) -> p c t i", t=PACK, i=RUN)[:, runs],
+                src[:].rearrange("p (t c i) -> p c t i", t=PACK, i=RUN)[:, runs],
             )
 
         def turn_pair(src, dst, h, bank):
@@ -134,13 +136,10 @@ def tile_attend_gxfull_sil_x_kernel(tc, xT, dyT, w1, w2, ts, tx, cf, offs, out):
                 bank[:].rearrange("p (c u m) -> p c m u", c=2, u=2),
             )
 
-        def turn_float32(raw, dst, use):
-            for c in range(PACK):
-                for t in range(PACK):
-                    nc.tensor.transpose(use[c][:, blocks[t]], raw[:, c * K + t : (c + 1) * K : PACK], ident[:])
-                nc.scalar.copy(dst[:, parts[c]].rearrange("p (m t) -> p m t", t=PACK), quarters(use[c][:]).rearrange("p t m -> p m t"))
-
         halves = [slice(h * 2 * K, (h + 1) * 2 * K) for h in range(2)]
+
+        def on_gpsimd(dst, src):
+            nc.gpsimd.tensor_scalar(dst, src, 1.0, 0.0, ALU.mult, ALU.add)
 
         def turn_weights(src, dst, use):
             for h in range(2):
@@ -224,8 +223,8 @@ def tile_attend_gxfull_sil_x_kernel(tc, xT, dyT, w1, w2, ts, tx, cf, offs, out):
                 gather(x_picked, x_win, t, b)
         w1d_stage = [stage(f"w1d_stage{b}") for b in range(EXPERTS)]
         w1_round0 = stage("w1_round0")
-        interleave(w1_raw0, w1d_stage[0])
-        nc.vector.tensor_copy(w1_round0[:], w1_raw0[:])
+        interleave(w1_raw[0], w1d_stage[0])
+        nc.vector.tensor_copy(w1_round0[:], w1_raw[0][:])
         w1d0 = quantized("w1d0", w1d_stage[0][:], E4M3)
         gate = sbuf([P, EXPERTS * PACK], F32, "gate", "w1_raw0")
         for b in range(EXPERTS):
@@ -235,48 +234,49 @@ def tile_attend_gxfull_sil_x_kernel(tc, xT, dyT, w1, w2, ts, tx, cf, offs, out):
         gather(x_picked, x_win, 3, 1)
         w1f_stage0 = stage("w1f_stage0", "x_win3")
         turn_weights(w1_round0, w1f_stage0, banks[4:6])
-        x_stage = [stage("x_stage0")]
-        interleave(x_picked[0], x_stage[0])
-        x_stage.append(stage("x_stage1", "x_picked0"))
+        x_stage0 = stage("x_stage0")
+        interleave(x_picked[0], x_stage0)
+        xq0 = quantized("x0", x_stage0[:], E4M3)
         w1f0 = quantized("w1f0", w1f_stage0[:], E4M3)
-        xq0 = quantized("x0", x_stage[0][:], E4M3)
         products(banks[0:4], xq0, w1d0)
-        interleave(x_picked[1], x_stage[1])
+        x_stage1 = stage("x_stage1", "x_stage0")
+        interleave(x_picked[1], x_stage1, half=0)
+        w2_round0 = stage("w2_round0", "x_win3")
+        on_gpsimd(w2_round0[:], w2_raw[0][:])
         for b in range(EXPERTS):
             gather(dy_picked, dy_win, 0, b)
-        w1_round1 = stage("w1_round1", "w1_round0")
-        for h in range(2):
-            nc.scalar.copy(w1_round1[:, halves[h]], w1_raw1[h][:])
+        interleave(x_picked[1], x_stage1, nc.scalar.copy, half=1)
 
         z0 = wide("z0", "x_win0")
         preactivation(0, z0, banks[0:4])
-        xq1 = quantized("x1", x_stage[1][:], E4M3)
-        silu0 = [half(f"silu0{h}", f"w1_raw1{h}") for h in range(2)]
+        silu0_tile = wide("silu0", "x_picked1")
+        silu0 = [silu0_tile[:, h] for h in halves]
         silu_of(z0, silu0)
         for h in range(2):
             tanh_of(z0, h, z0[:, halves[h]])
         gather(dy_picked, dy_win, 2, 0)
-        w2_stage0 = stage("w2_stage0")
-        turn_float32(w2_raw[0], w2_stage0, banks[4:8])
-        interleave(w1_round1, w1d_stage[1])
-        scaled0a = half("scaled0a", "x_picked1")
-        scaled_silu(silu0[0], scaled0a)
-        w1d1 = quantized("w1d1", w1d_stage[1][:], E4M3, "w1_raw10")
+        interleave(w1_raw[1], w1d_stage[1])
+        xq1 = quantized("x1", x_stage1[:], E4M3, placed([P, K], U32, "x1_codes", 0))
+        w1d1 = quantized("w1d1", w1d_stage[1][:], E4M3)
         products(banks[0:4], xq1, w1d1)
-        scaled0b = [sbuf([P, K], F32, "scaled0c", "x_picked0"), sbuf([P, K], F32, "scaled0d")]
+        w2_stage0 = stage("w2_stage0", "w2_raw0")
+        scaled0a = half("scaled0a", "x_stage0")
+        scaled_silu(silu0[0], scaled0a)
+        scaled0b = [placed([P, K], F32, "scaled0c", 2), placed([P, K], F32, "scaled0d", 1)]
         for r in range(2):
             nc.vector.scalar_tensor_tensor(scaled0b[r][:], silu0[1][:, parts[r]], 1.0, cf_row[:], ALU.subtract, ALU.mult)
         slope(scaled0a, z0[:, halves[0]], z0[:, halves[0]])
         for r in range(2):
             slope(scaled0b[r], z0[:, parts[2 + r]], z0[:, parts[2 + r]])
-        w2_round1 = stage("w2_round1", "x_picked0")
-        nc.gpsimd.tensor_scalar(w2_round1[:], w2_raw[1][:], 1.0, 0.0, ALU.mult, ALU.add)
+        w1_round1 = placed([P, PACK * K], BF16, "w1_round1", 2)
+        on_gpsimd(w1_round1[:].rearrange("p (j f) -> p j f", j=PACK), w1d_stage[1][:].rearrange("p (f j) -> p j f", j=PACK))
+        turn_weights(w2_round0, w2_stage0, banks[4:6])
         gather(dy_picked, dy_win, 3, 0)
         for b in range(EXPERTS):
             gather(dy_picked, dy_win, 1, b)
-        z1 = wide("z1", "x_picked1")
+        z1 = wide("z1", "x_stage0")
         preactivation(1, z1, banks[0:4])
-        dy_stage = [stage("dy_stage0", "x_stage0"), stage("dy_stage1", "x_win1")]
+        dy_stage = [stage("dy_stage0", "x_win2"), stage("dy_stage1", "x_win1")]
         interleave(dy_picked[0], dy_stage[0])
         silu1_tile = wide("silu1", "dy_win1")
         silu1 = [silu1_tile[:, h] for h in halves]
@@ -284,22 +284,23 @@ def tile_attend_gxfull_sil_x_kernel(tc, xT, dyT, w1, w2, ts, tx, cf, offs, out):
         tanh_of(z1, 0, z1[:, halves[0]])
         for t in (2, 3):
             gather(dy_picked, dy_win, t, 1)
-        w2q0 = quantized("w2q0", w2_stage0[:], E4M3, "scaled0d")
+        tanh_of(z1, 1, z1[:, halves[1]])
+        w2q0 = quantized("w2q0", w2_stage0[:], E4M3, placed([P, K], U32, "w2q0_codes", 1))
         dyq0 = quantized("dy0", dy_stage[0][:], E5M2)
         products(banks[4:8], dyq0, w2q0)
+        w2_round1 = stage("w2_round1", "x_win2")
+        on_gpsimd(w2_round1[:], w2_raw[1][:])
         scaled_silu(silu1[0], silu1[0])
 
         da0 = stage("da0", "tx_picked")
-        da_stage0 = stage("da_stage0", "w2_raw0")
+        da_stage0 = stage("da_stage0", "x_picked1")
         for r in range(PACK):
             gradient(0, z0, da0, banks[4:8], r)
             if r % 2:
                 turn_pair(da0, da_stage0, r // 2, banks[4 + r // 2])
-        w2_stage1 = stage("w2_stage1", "x_stage0")
+        w2_stage1 = stage("w2_stage1", "dy_win0")
         turn_weights(w2_round1, w2_stage1, banks[6:8])
-        tanh1b = half("tanh1b", "tx_picked")
-        tanh_of(z1, 1, tanh1b[:])
-        w1f_stage1 = stage("w1f_stage1", "x_win3")
+        w1f_stage1 = stage("w1f_stage1", "w1_round0")
         turn_weights(w1_round1, w1f_stage1, banks[4:6])
         scaled_silu(silu1[1], silu1[1])
         interleave(dy_picked[1], dy_stage[1])
@@ -320,7 +321,7 @@ def tile_attend_gxfull_sil_x_kernel(tc, xT, dyT, w1, w2, ts, tx, cf, offs, out):
         def store(j):
             nc.sync.dma_start(rows[j], out_win[j][:])
 
-        dx0 = sbuf([P, EXPERTS * SLOTS], F32, "dx0", "dy_win0")
+        dx0 = sbuf([P, EXPERTS * SLOTS], F32, "dx0", "x_win0")
         dx1 = sbuf([P, SLOTS], F32, "dx1", "ts_win")
         dh1 = [banks[2], banks[3], banks[6], banks[7]]
         product(banks[0], w1f0, 1, daq0)
@@ -329,10 +330,10 @@ def tile_attend_gxfull_sil_x_kernel(tc, xT, dyT, w1, w2, ts, tx, cf, offs, out):
         product(banks[4], w1f0, 2, daq0)
         product(banks[5], w1f0, 3, daq0)
         nc.scalar.copy(dx1[:], banks[0][:])
-        nc.scalar.copy(dx0[:, 0:PIECE], banks[1][:, 0:PIECE])
+        nc.scalar.copy(dx0[:, parts[0]], banks[1][:])
         on_scalar(1, 0, dx1[:, 0:PIECE])
-        on_scalar(0, 0, dx0[:, 0:PIECE])
-        slope(silu1[1], tanh1b[:], z1[:, halves[1]])
+        on_scalar(0, 0, dx0[:, 0:384])
+        slope(silu1[1], z1[:, halves[1]], z1[:, halves[1]])
         w1f1 = quantized("w1f1", w1f_stage1[:], E4M3)
         da1 = stage("da1", "dy_picked")
         da_stage1 = stage("da_stage1", "ts_picked")
@@ -342,31 +343,28 @@ def tile_attend_gxfull_sil_x_kernel(tc, xT, dyT, w1, w2, ts, tx, cf, offs, out):
                 turn_pair(da1, da_stage1, r // 2, dh1[r // 2])
         on_vector(1, PIECE, dx1[:, PIECE:])
         daq1 = quantized("da1", da_stage1[:], E5M2)
-        late = sbuf([P, 2 * EXPERTS * SLOTS + PIECE], F32, "late", "dy_picked")
+        late = sbuf([P, 2 * EXPERTS * SLOTS], F32, "late", "dy_picked")
         dx2 = late[:, : EXPERTS * SLOTS]
-        dx3 = late[:, EXPERTS * SLOTS : 2 * EXPERTS * SLOTS]
-        dx0_rest = late[:, 2 * EXPERTS * SLOTS :]
-        nc.scalar.copy(dx0_rest, banks[1][:, PIECE:])
+        dx3 = late[:, EXPERTS * SLOTS :]
         nc.scalar.copy(dx2[:, parts[0]], banks[4][:])
-        on_scalar(0, PIECE, dx0_rest)
         nc.scalar.copy(dx3[:, parts[0]], banks[5][:])
-        on_vector(2, 0, dx2[:, 0:384])
+        on_vector(2, 0, dx2[:, 0:PIECE])
+        on_scalar(3, 0, dx3[:, 0:PIECE])
 
-        for j, acc in ((0, banks[2]), (1, banks[0]), (3, banks[6]), (2, banks[7])):
+        for j, acc in ((1, banks[0]), (0, banks[1]), (3, banks[6]), (2, banks[7])):
             product(acc, w1f1, j, daq1)
-        nc.scalar.copy(dx0[:, parts[1]], banks[2][:])
         dx1_last = sbuf([P, SLOTS], F32, "dx1_last", "tx_win")
         nc.vector.tensor_copy(dx1_last[:], banks[0][:])
-        nc.vector.tensor_copy(dx3[:, parts[1]], banks[6][:])
         on_vector(1, SLOTS, dx1_last[:])
         store(1)
-        on_scalar(3, 0, dx3[:, 0:320])
-        on_scalar(0, SLOTS, dx0[:, SLOTS : SLOTS + PIECE])
+        nc.scalar.copy(dx0[:, parts[1]], banks[1][:])
+        nc.scalar.copy(dx3[:, parts[1]], banks[6][:])
+        on_scalar(0, 384, dx0[:, 384:640])
         nc.scalar.copy(dx2[:, parts[1]], banks[7][:])
-        on_scalar(0, SLOTS + PIECE, dx0[:, SLOTS + PIECE :])
+        on_scalar(0, 640, dx0[:, 640:])
         store(0)
-        on_vector(2, 384, dx2[:, 384:])
+        on_vector(2, PIECE, dx2[:, PIECE:])
         store(2)
-        on_scalar(3, 320, dx3[:, 320:704])
-        on_scalar(3, 704, dx3[:, 704:])
+        on_scalar(3, PIECE, dx3[:, PIECE:640])
+        on_scalar(3, 640, dx3[:, 640:])
         store(3)

@@ -38,8 +38,8 @@ def tile_attend_gxfull_sil_x_kernel(tc, xT, dyT, w1, w2, ts, tx, cf, offs, out):
         def sbuf(shape, dtype, name, tag=None):
             return keep.tile(shape, dtype, name=name, tag=tag or name, align_bytes=ALIGN)
 
-        def placed(shape, dtype, name, quarter):
-            return shared.tile(shape, dtype, name=name, offset=quarter * K * 4, align_bytes=ALIGN)
+        def placed(shape, dtype, name, kib):
+            return shared.tile(shape, dtype, name=name, offset=kib * 1024, align_bytes=ALIGN)
 
         banks = [psum.tile([P, SLOTS], F32, name=f"bank{n}") for n in range(8)]
         blocks = [slice(r * P, (r + 1) * P) for r in range(PACK)]
@@ -76,7 +76,7 @@ def tile_attend_gxfull_sil_x_kernel(tc, xT, dyT, w1, w2, ts, tx, cf, offs, out):
         x_win = [sbuf([P, TOKENS], F32, f"x_win{t}") for t in range(PACK)]
         dy_win = [sbuf([P, TOKENS], F32, f"dy_win{t}") for t in range(PACK)]
         out_win = [sbuf([P, TOKENS], F32, f"out_win{j}") for j in range(PACK)]
-        w1_raw = [sbuf([P, PACK * K], F32, "w1_raw0"), placed([P, PACK * K], F32, "w1_raw1", 0)]
+        w1_raw = [sbuf([P, PACK * K], F32, f"w1_raw{b}") for b in range(EXPERTS)]
         w2_raw = [sbuf([P, PACK * K], F32, f"w2_raw{b}") for b in range(EXPERTS)]
         cf_col = sbuf([P, PACK], F32, "cf_col")
 
@@ -126,12 +126,13 @@ def tile_attend_gxfull_sil_x_kernel(tc, xT, dyT, w1, w2, ts, tx, cf, offs, out):
                 src[:].rearrange("p (t c i) -> p c t i", t=PACK, i=RUN)[:, runs],
             )
 
-        def turn_pair(src, dst, h, bank):
-            for c in (2 * h, 2 * h + 1):
-                pairs = src[:, parts[c]].bitcast(F32)
+        def turn_pair(src, dst, h, bank, copy=nc.scalar.copy, first=None):
+            first = 2 * h if first is None else first
+            for c in range(2):
+                pairs = src[:, parts[first + c]].bitcast(F32)
                 for u in range(2):
-                    nc.tensor.transpose(bank[:, blocks[2 * (c % 2) + u]], pairs[:, u : K // 2 : 2], ident[:])
-            nc.scalar.copy(
+                    nc.tensor.transpose(bank[:, blocks[2 * c + u]], pairs[:, u : K // 2 : 2], ident[:])
+            copy(
                 dst[:].bitcast(F32)[:, parts[h]].rearrange("p (c m u) -> p c m u", c=2, u=2),
                 bank[:].rearrange("p (c u m) -> p c m u", c=2, u=2),
             )
@@ -155,7 +156,7 @@ def tile_attend_gxfull_sil_x_kernel(tc, xT, dyT, w1, w2, ts, tx, cf, offs, out):
                     nc.tensor.transpose(use[b][:, blocks[r]], picked[n][:, first : first + P], ident[:])
             return [quarters(use[b][:])[:, :, ROW] for b in range(EXPERTS)]
 
-        x_picked = [sbuf([P, PACK * SLOTS], BF16, f"x_picked{b}") for b in range(EXPERTS)]
+        x_picked = [placed([P, PACK * SLOTS], BF16, "x_picked0", 0), sbuf([P, PACK * SLOTS], BF16, "x_picked1")]
         dy_planes_tile = sbuf([P, (PACK + 2) * SLOTS], BF16, "dy_picked")
         dy_picked = [dy_planes_tile[:, 2 * SLOTS :], dy_planes_tile[:, : PACK * SLOTS]]
 
@@ -221,8 +222,8 @@ def tile_attend_gxfull_sil_x_kernel(tc, xT, dyT, w1, w2, ts, tx, cf, offs, out):
         for t in (1, 2):
             for b in range(EXPERTS):
                 gather(x_picked, x_win, t, b)
-        w1d_stage = [stage(f"w1d_stage{b}") for b in range(EXPERTS)]
-        w1_round0 = stage("w1_round0")
+        w1d_stage = [placed([P, PACK * K], BF16, "w1d_stage0", 14), placed([P, PACK * K], BF16, "w1d_stage1", 9)]
+        w1_round0 = placed([P, PACK * K], BF16, "w1_round0", 4)
         interleave(w1_raw[0], w1d_stage[0])
         nc.vector.tensor_copy(w1_round0[:], w1_raw[0][:])
         w1d0 = quantized("w1d0", w1d_stage[0][:], E4M3)
@@ -234,12 +235,12 @@ def tile_attend_gxfull_sil_x_kernel(tc, xT, dyT, w1, w2, ts, tx, cf, offs, out):
         gather(x_picked, x_win, 3, 1)
         w1f_stage0 = stage("w1f_stage0", "x_win3")
         turn_weights(w1_round0, w1f_stage0, banks[4:6])
-        x_stage0 = stage("x_stage0")
+        x_stage0 = placed([P, PACK * K], BF16, "x_stage0", 18)
         interleave(x_picked[0], x_stage0)
         xq0 = quantized("x0", x_stage0[:], E4M3)
         w1f0 = quantized("w1f0", w1f_stage0[:], E4M3)
         products(banks[0:4], xq0, w1d0)
-        x_stage1 = stage("x_stage1", "x_stage0")
+        x_stage1 = placed([P, PACK * K], BF16, "x_stage1", 18)
         interleave(x_picked[1], x_stage1, half=0)
         w2_round0 = stage("w2_round0", "x_win3")
         on_gpsimd(w2_round0[:], w2_raw[0][:])
@@ -255,28 +256,28 @@ def tile_attend_gxfull_sil_x_kernel(tc, xT, dyT, w1, w2, ts, tx, cf, offs, out):
         for h in range(2):
             tanh_of(z0, h, z0[:, halves[h]])
         gather(dy_picked, dy_win, 2, 0)
+        xq1 = quantized("x1", x_stage1[:], E4M3)
         interleave(w1_raw[1], w1d_stage[1])
-        xq1 = quantized("x1", x_stage1[:], E4M3, placed([P, K], U32, "x1_codes", 0))
         w1d1 = quantized("w1d1", w1d_stage[1][:], E4M3)
         products(banks[0:4], xq1, w1d1)
-        w2_stage0 = stage("w2_stage0", "w2_raw0")
-        scaled0a = half("scaled0a", "x_stage0")
+        w2_stage0 = placed([P, PACK * K], BF16, "w2_stage0", 14)
+        scaled0a = placed([P, 2 * K], F32, "scaled0a", 6)
         scaled_silu(silu0[0], scaled0a)
-        scaled0b = [placed([P, K], F32, "scaled0c", 2), placed([P, K], F32, "scaled0d", 1)]
+        scaled0b = [placed([P, K], F32, "scaled0c", 10), placed([P, K], F32, "scaled0d", 12)]
         for r in range(2):
             nc.vector.scalar_tensor_tensor(scaled0b[r][:], silu0[1][:, parts[r]], 1.0, cf_row[:], ALU.subtract, ALU.mult)
         slope(scaled0a, z0[:, halves[0]], z0[:, halves[0]])
         for r in range(2):
             slope(scaled0b[r], z0[:, parts[2 + r]], z0[:, parts[2 + r]])
-        w1_round1 = placed([P, PACK * K], BF16, "w1_round1", 2)
-        on_gpsimd(w1_round1[:].rearrange("p (j f) -> p j f", j=PACK), w1d_stage[1][:].rearrange("p (f j) -> p j f", j=PACK))
+        w1_round1 = placed([P, PACK * K], BF16, "w1_round1", 8)
+        on_gpsimd(w1_round1[:], w1_raw[1][:])
         turn_weights(w2_round0, w2_stage0, banks[4:6])
         gather(dy_picked, dy_win, 3, 0)
         for b in range(EXPERTS):
             gather(dy_picked, dy_win, 1, b)
-        z1 = wide("z1", "x_stage0")
+        z1 = placed([P, PACK * K], F32, "z1", 0)
         preactivation(1, z1, banks[0:4])
-        dy_stage = [stage("dy_stage0", "x_win2"), stage("dy_stage1", "x_win1")]
+        dy_stage = [placed([P, PACK * K], BF16, "dy_stage0", 18), stage("dy_stage1", "x_win1")]
         interleave(dy_picked[0], dy_stage[0])
         silu1_tile = wide("silu1", "dy_win1")
         silu1 = [silu1_tile[:, h] for h in halves]
@@ -285,10 +286,10 @@ def tile_attend_gxfull_sil_x_kernel(tc, xT, dyT, w1, w2, ts, tx, cf, offs, out):
         for t in (2, 3):
             gather(dy_picked, dy_win, t, 1)
         tanh_of(z1, 1, z1[:, halves[1]])
-        w2q0 = quantized("w2q0", w2_stage0[:], E4M3, placed([P, K], U32, "w2q0_codes", 1))
+        w2q0 = quantized("w2q0", w2_stage0[:], E4M3, placed([P, K], U32, "w2q0_codes", 12))
         dyq0 = quantized("dy0", dy_stage[0][:], E5M2)
         products(banks[4:8], dyq0, w2q0)
-        w2_round1 = stage("w2_round1", "x_win2")
+        w2_round1 = placed([P, PACK * K], BF16, "w2_round1", 16)
         on_gpsimd(w2_round1[:], w2_raw[1][:])
         scaled_silu(silu1[0], silu1[0])
 
@@ -298,10 +299,10 @@ def tile_attend_gxfull_sil_x_kernel(tc, xT, dyT, w1, w2, ts, tx, cf, offs, out):
             gradient(0, z0, da0, banks[4:8], r)
             if r % 2:
                 turn_pair(da0, da_stage0, r // 2, banks[4 + r // 2])
+        w1f_stage1 = stage("w1f_stage1", "tx_picked")
+        turn_weights(w1_round1, w1f_stage1, banks[0:2])
         w2_stage1 = stage("w2_stage1", "dy_win0")
-        turn_weights(w2_round1, w2_stage1, banks[6:8])
-        w1f_stage1 = stage("w1f_stage1", "w1_round0")
-        turn_weights(w1_round1, w1f_stage1, banks[4:6])
+        turn_weights(w2_round1, w2_stage1, [banks[7], banks[5]])
         scaled_silu(silu1[1], silu1[1])
         interleave(dy_picked[1], dy_stage[1])
         daq0 = quantized("da0", da_stage0[:], E5M2)
@@ -323,14 +324,14 @@ def tile_attend_gxfull_sil_x_kernel(tc, xT, dyT, w1, w2, ts, tx, cf, offs, out):
 
         dx0 = sbuf([P, EXPERTS * SLOTS], F32, "dx0", "x_win0")
         dx1 = sbuf([P, SLOTS], F32, "dx1", "ts_win")
-        dh1 = [banks[2], banks[3], banks[6], banks[7]]
-        product(banks[0], w1f0, 1, daq0)
-        product(banks[1], w1f0, 0, daq0)
+        dh1 = [banks[4], banks[6], banks[7], banks[5]]
+        product(banks[2], w1f0, 1, daq0)
+        product(banks[3], w1f0, 0, daq0)
         products(dh1, dyq1, w2q1)
-        product(banks[4], w1f0, 2, daq0)
-        product(banks[5], w1f0, 3, daq0)
-        nc.scalar.copy(dx1[:], banks[0][:])
-        nc.scalar.copy(dx0[:, parts[0]], banks[1][:])
+        product(banks[0], w1f0, 2, daq0)
+        product(banks[1], w1f0, 3, daq0)
+        nc.scalar.copy(dx1[:], banks[2][:])
+        nc.scalar.copy(dx0[:, parts[0]], banks[3][:])
         on_scalar(1, 0, dx1[:, 0:PIECE])
         on_scalar(0, 0, dx0[:, 0:384])
         slope(silu1[1], z1[:, halves[1]], z1[:, halves[1]])
@@ -346,21 +347,21 @@ def tile_attend_gxfull_sil_x_kernel(tc, xT, dyT, w1, w2, ts, tx, cf, offs, out):
         late = sbuf([P, 2 * EXPERTS * SLOTS], F32, "late", "dy_picked")
         dx2 = late[:, : EXPERTS * SLOTS]
         dx3 = late[:, EXPERTS * SLOTS :]
-        nc.scalar.copy(dx2[:, parts[0]], banks[4][:])
-        nc.scalar.copy(dx3[:, parts[0]], banks[5][:])
+        nc.scalar.copy(dx2[:, parts[0]], banks[0][:])
+        nc.scalar.copy(dx3[:, parts[0]], banks[1][:])
         on_vector(2, 0, dx2[:, 0:PIECE])
         on_scalar(3, 0, dx3[:, 0:PIECE])
 
-        for j, acc in ((1, banks[0]), (0, banks[1]), (3, banks[6]), (2, banks[7])):
+        for j, acc in ((1, banks[2]), (0, banks[3]), (3, banks[7]), (2, banks[5])):
             product(acc, w1f1, j, daq1)
         dx1_last = sbuf([P, SLOTS], F32, "dx1_last", "tx_win")
-        nc.vector.tensor_copy(dx1_last[:], banks[0][:])
+        nc.vector.tensor_copy(dx1_last[:], banks[2][:])
         on_vector(1, SLOTS, dx1_last[:])
         store(1)
-        nc.scalar.copy(dx0[:, parts[1]], banks[1][:])
-        nc.scalar.copy(dx3[:, parts[1]], banks[6][:])
+        nc.scalar.copy(dx0[:, parts[1]], banks[3][:])
+        nc.scalar.copy(dx3[:, parts[1]], banks[7][:])
         on_scalar(0, 384, dx0[:, 384:640])
-        nc.scalar.copy(dx2[:, parts[1]], banks[7][:])
+        nc.scalar.copy(dx2[:, parts[1]], banks[5][:])
         on_scalar(0, 640, dx0[:, 640:])
         store(0)
         on_vector(2, PIECE, dx2[:, PIECE:])

@@ -73,7 +73,7 @@ def tile_attend_gxfull_sil_x_kernel(tc, xT, dyT, w1, w2, ts, tx, cf, offs, out):
 
         tx_win = sbuf([P, TOKENS], F32, "tx_win")
         ts_win = sbuf([P, TOKENS], F32, "ts_win")
-        x_win = [sbuf([P, TOKENS], F32, f"x_win{t}") for t in range(PACK)]
+        x_win = [sbuf([P, TOKENS], F32, f"x_win{t}") for t in range(PACK - 1)] + [placed([P, TOKENS], F32, "x_win3", 0)]
         dy_win = [sbuf([P, TOKENS], F32, f"dy_win{t}") for t in range(PACK)]
         out_win = [sbuf([P, TOKENS], F32, f"out_win{j}") for j in range(PACK)]
         w1_raw = [sbuf([P, PACK * K], F32, f"w1_raw{b}") for b in range(EXPERTS)]
@@ -156,7 +156,7 @@ def tile_attend_gxfull_sil_x_kernel(tc, xT, dyT, w1, w2, ts, tx, cf, offs, out):
                     nc.tensor.transpose(use[b][:, blocks[r]], picked[n][:, first : first + P], ident[:])
             return [quarters(use[b][:])[:, :, ROW] for b in range(EXPERTS)]
 
-        x_picked = [placed([P, PACK * SLOTS], BF16, "x_picked0", 0), sbuf([P, PACK * SLOTS], BF16, "x_picked1")]
+        x_picked = [placed([P, PACK * SLOTS], BF16, "x_picked0", 22), sbuf([P, PACK * SLOTS], BF16, "x_picked1")]
         dy_planes_tile = sbuf([P, (PACK + 2) * SLOTS], BF16, "dy_picked")
         dy_picked = [dy_planes_tile[:, 2 * SLOTS :], dy_planes_tile[:, : PACK * SLOTS]]
 
@@ -222,8 +222,8 @@ def tile_attend_gxfull_sil_x_kernel(tc, xT, dyT, w1, w2, ts, tx, cf, offs, out):
         for t in (1, 2):
             for b in range(EXPERTS):
                 gather(x_picked, x_win, t, b)
-        w1d_stage = [placed([P, PACK * K], BF16, "w1d_stage0", 14), placed([P, PACK * K], BF16, "w1d_stage1", 9)]
-        w1_round0 = placed([P, PACK * K], BF16, "w1_round0", 4)
+        w1d_stage = [stage("w1d_stage0"), placed([P, PACK * K], BF16, "w1d_stage1", 17)]
+        w1_round0 = stage("w1_round0")
         interleave(w1_raw[0], w1d_stage[0])
         nc.vector.tensor_copy(w1_round0[:], w1_raw[0][:])
         w1d0 = quantized("w1d0", w1d_stage[0][:], E4M3)
@@ -233,16 +233,16 @@ def tile_attend_gxfull_sil_x_kernel(tc, xT, dyT, w1, w2, ts, tx, cf, offs, out):
             nc.vector.scalar_tensor_tensor(gate[:, cols], ts_turned[b], -0.5, tx_col[:, cols], ALU.mult, ALU.mult)
         gather(x_picked, x_win, 3, 0, nc.vector.tensor_copy)
         gather(x_picked, x_win, 3, 1)
-        w1f_stage0 = stage("w1f_stage0", "x_win3")
+        w1f_stage0 = placed([P, PACK * K], BF16, "w1f_stage0", 6)
         turn_weights(w1_round0, w1f_stage0, banks[4:6])
-        x_stage0 = placed([P, PACK * K], BF16, "x_stage0", 18)
+        x_stage0 = placed([P, PACK * K], BF16, "x_stage0", 11)
         interleave(x_picked[0], x_stage0)
-        xq0 = quantized("x0", x_stage0[:], E4M3)
         w1f0 = quantized("w1f0", w1f_stage0[:], E4M3)
+        xq0 = quantized("x0", x_stage0[:], E4M3)
         products(banks[0:4], xq0, w1d0)
-        x_stage1 = placed([P, PACK * K], BF16, "x_stage1", 18)
+        x_stage1 = placed([P, PACK * K], BF16, "x_stage1", 22)
         interleave(x_picked[1], x_stage1, half=0)
-        w2_round0 = stage("w2_round0", "x_win3")
+        w2_round0 = placed([P, PACK * K], BF16, "w2_round0", 9)
         on_gpsimd(w2_round0[:], w2_raw[0][:])
         for b in range(EXPERTS):
             gather(dy_picked, dy_win, 0, b)
@@ -260,24 +260,24 @@ def tile_attend_gxfull_sil_x_kernel(tc, xT, dyT, w1, w2, ts, tx, cf, offs, out):
         interleave(w1_raw[1], w1d_stage[1])
         w1d1 = quantized("w1d1", w1d_stage[1][:], E4M3)
         products(banks[0:4], xq1, w1d1)
-        w2_stage0 = placed([P, PACK * K], BF16, "w2_stage0", 14)
-        scaled0a = placed([P, 2 * K], F32, "scaled0a", 6)
+        w2_stage0 = placed([P, PACK * K], BF16, "w2_stage0", 0)
+        scaled0a = placed([P, 2 * K], F32, "scaled0a", 14)
         scaled_silu(silu0[0], scaled0a)
-        scaled0b = [placed([P, K], F32, "scaled0c", 10), placed([P, K], F32, "scaled0d", 12)]
+        scaled0b = [placed([P, K], F32, "scaled0c", 18), placed([P, K], F32, "scaled0d", 20)]
         for r in range(2):
             nc.vector.scalar_tensor_tensor(scaled0b[r][:], silu0[1][:, parts[r]], 1.0, cf_row[:], ALU.subtract, ALU.mult)
         slope(scaled0a, z0[:, halves[0]], z0[:, halves[0]])
         for r in range(2):
             slope(scaled0b[r], z0[:, parts[2 + r]], z0[:, parts[2 + r]])
-        w1_round1 = placed([P, PACK * K], BF16, "w1_round1", 8)
+        w1_round1 = placed([P, PACK * K], BF16, "w1_round1", 16)
         on_gpsimd(w1_round1[:], w1_raw[1][:])
         turn_weights(w2_round0, w2_stage0, banks[4:6])
         gather(dy_picked, dy_win, 3, 0)
         for b in range(EXPERTS):
             gather(dy_picked, dy_win, 1, b)
-        z1 = placed([P, PACK * K], F32, "z1", 0)
+        z1 = placed([P, PACK * K], F32, "z1", 8)
         preactivation(1, z1, banks[0:4])
-        dy_stage = [placed([P, PACK * K], BF16, "dy_stage0", 18), stage("dy_stage1", "x_win1")]
+        dy_stage = [placed([P, PACK * K], BF16, "dy_stage0", 4), stage("dy_stage1", "x_win1")]
         interleave(dy_picked[0], dy_stage[0])
         silu1_tile = wide("silu1", "dy_win1")
         silu1 = [silu1_tile[:, h] for h in halves]
@@ -286,10 +286,10 @@ def tile_attend_gxfull_sil_x_kernel(tc, xT, dyT, w1, w2, ts, tx, cf, offs, out):
         for t in (2, 3):
             gather(dy_picked, dy_win, t, 1)
         tanh_of(z1, 1, z1[:, halves[1]])
-        w2q0 = quantized("w2q0", w2_stage0[:], E4M3, placed([P, K], U32, "w2q0_codes", 12))
+        w2q0 = quantized("w2q0", w2_stage0[:], E4M3, placed([P, K], U32, "w2q0_codes", 20))
         dyq0 = quantized("dy0", dy_stage[0][:], E5M2)
         products(banks[4:8], dyq0, w2q0)
-        w2_round1 = placed([P, PACK * K], BF16, "w2_round1", 16)
+        w2_round1 = placed([P, PACK * K], BF16, "w2_round1", 2)
         on_gpsimd(w2_round1[:], w2_raw[1][:])
         scaled_silu(silu1[0], silu1[0])
 

@@ -24,6 +24,7 @@ LIST_COLS = SLOTS // 16
 ROW = P - 1
 ALIGN = 64
 RUN = 4
+BESIDE = 1600
 
 FLOPS = 3 * EXPERTS * 2 * K * K * SLOTS
 
@@ -139,8 +140,11 @@ def tile_attend_gxfull_sil_x_kernel(tc, xT, dyT, w1, w2, ts, tx, cf, offs, out):
 
         halves = [slice(h * 2 * K, (h + 1) * 2 * K) for h in range(2)]
 
-        def on_gpsimd(dst, src):
-            nc.gpsimd.tensor_scalar(dst, src, 1.0, 0.0, ALU.mult, ALU.add)
+        def round_beside(dst, raw):
+            nc.gpsimd.tensor_scalar(dst[:, :BESIDE], raw[:, :BESIDE], 1.0, 0.0, ALU.mult, ALU.add)
+
+        def round_rest(dst, raw):
+            nc.vector.tensor_copy(dst[:, BESIDE:], raw[:, BESIDE:])
 
         def turn_weights(src, dst, use):
             for h in range(2):
@@ -243,7 +247,7 @@ def tile_attend_gxfull_sil_x_kernel(tc, xT, dyT, w1, w2, ts, tx, cf, offs, out):
         x_stage1 = placed([P, PACK * K], BF16, "x_stage1", 22)
         interleave(x_picked[1], x_stage1, half=0)
         w2_round0 = placed([P, PACK * K], BF16, "w2_round0", 9)
-        on_gpsimd(w2_round0[:], w2_raw[0][:])
+        round_beside(w2_round0, w2_raw[0])
         for b in range(EXPERTS):
             gather(dy_picked, dy_win, 0, b)
         interleave(x_picked[1], x_stage1, nc.scalar.copy, half=1)
@@ -256,6 +260,7 @@ def tile_attend_gxfull_sil_x_kernel(tc, xT, dyT, w1, w2, ts, tx, cf, offs, out):
         for h in range(2):
             tanh_of(z0, h, z0[:, halves[h]])
         gather(dy_picked, dy_win, 2, 0)
+        round_rest(w2_round0, w2_raw[0])
         xq1 = quantized("x1", x_stage1[:], E4M3)
         interleave(w1_raw[1], w1d_stage[1])
         w1d1 = quantized("w1d1", w1d_stage[1][:], E4M3)
@@ -270,7 +275,7 @@ def tile_attend_gxfull_sil_x_kernel(tc, xT, dyT, w1, w2, ts, tx, cf, offs, out):
         for r in range(2):
             slope(scaled0b[r], z0[:, parts[2 + r]], z0[:, parts[2 + r]])
         w1_round1 = placed([P, PACK * K], BF16, "w1_round1", 16)
-        on_gpsimd(w1_round1[:], w1_raw[1][:])
+        round_beside(w1_round1, w1_raw[1])
         turn_weights(w2_round0, w2_stage0, banks[4:6])
         gather(dy_picked, dy_win, 3, 0)
         for b in range(EXPERTS):
@@ -279,6 +284,7 @@ def tile_attend_gxfull_sil_x_kernel(tc, xT, dyT, w1, w2, ts, tx, cf, offs, out):
         preactivation(1, z1, banks[0:4])
         dy_stage = [placed([P, PACK * K], BF16, "dy_stage0", 4), stage("dy_stage1", "x_win1")]
         interleave(dy_picked[0], dy_stage[0])
+        round_rest(w1_round1, w1_raw[1])
         silu1_tile = wide("silu1", "dy_win1")
         silu1 = [silu1_tile[:, h] for h in halves]
         silu_of(z1, silu1)
@@ -290,7 +296,7 @@ def tile_attend_gxfull_sil_x_kernel(tc, xT, dyT, w1, w2, ts, tx, cf, offs, out):
         dyq0 = quantized("dy0", dy_stage[0][:], E5M2)
         products(banks[4:8], dyq0, w2q0)
         w2_round1 = placed([P, PACK * K], BF16, "w2_round1", 2)
-        on_gpsimd(w2_round1[:], w2_raw[1][:])
+        round_beside(w2_round1, w2_raw[1])
         scaled_silu(silu1[0], silu1[0])
 
         da0 = stage("da0", "tx_picked")
@@ -299,6 +305,7 @@ def tile_attend_gxfull_sil_x_kernel(tc, xT, dyT, w1, w2, ts, tx, cf, offs, out):
             gradient(0, z0, da0, banks[4:8], r)
             if r % 2:
                 turn_pair(da0, da_stage0, r // 2, banks[4 + r // 2])
+        round_rest(w2_round1, w2_raw[1])
         w1f_stage1 = stage("w1f_stage1", "tx_picked")
         turn_weights(w1_round1, w1f_stage1, banks[0:2])
         w2_stage1 = stage("w2_stage1", "dy_win0")

@@ -239,13 +239,13 @@ def tile_attend_gxfull_sil_x_kernel(tc, xT, dyT, w1, w2, ts, tx, cf, offs, out):
         gather(x_picked, x_win, 3, 1)
         w1f_stage0 = placed([P, PACK * K], BF16, "w1f_stage0", 6)
         turn_weights(w1_round0, w1f_stage0, banks[4:6])
-        x_stage0 = placed([P, PACK * K], BF16, "x_stage0", 11)
+        x_stage0 = placed([P, PACK * K], BF16, "x_stage0", 26)
         interleave(x_picked[0], x_stage0)
-        w1f0 = quantized("w1f0", w1f_stage0[:], E4M3)
         xq0 = quantized("x0", x_stage0[:], E4M3)
         products(banks[0:4], xq0, w1d0)
         x_stage1 = placed([P, PACK * K], BF16, "x_stage1", 22)
         interleave(x_picked[1], x_stage1, half=0)
+        w1f0 = quantized("w1f0", w1f_stage0[:], E4M3, placed([P, K], U32, "w1f0_codes", 26))
         w2_round0 = placed([P, PACK * K], BF16, "w2_round0", 9)
         round_beside(w2_round0, w2_raw[0])
         for b in range(EXPERTS):
@@ -260,9 +260,9 @@ def tile_attend_gxfull_sil_x_kernel(tc, xT, dyT, w1, w2, ts, tx, cf, offs, out):
         for h in range(2):
             tanh_of(z0, h, z0[:, halves[h]])
         gather(dy_picked, dy_win, 2, 0)
-        round_rest(w2_round0, w2_raw[0])
         xq1 = quantized("x1", x_stage1[:], E4M3)
         interleave(w1_raw[1], w1d_stage[1])
+        round_rest(w2_round0, w2_raw[0])
         w1d1 = quantized("w1d1", w1d_stage[1][:], E4M3)
         products(banks[0:4], xq1, w1d1)
         w2_stage0 = placed([P, PACK * K], BF16, "w2_stage0", 0)

@@ -140,8 +140,11 @@ def tile_attend_gxfull_sil_x_kernel(tc, xT, dyT, w1, w2, ts, tx, cf, offs, out):
 
         halves = [slice(h * 2 * K, (h + 1) * 2 * K) for h in range(2)]
 
+        def on_gpsimd(dst, src):
+            nc.gpsimd.tensor_scalar(dst, src, 1.0, 0.0, ALU.mult, ALU.add)
+
         def round_beside(dst, raw):
-            nc.gpsimd.tensor_scalar(dst[:, :BESIDE], raw[:, :BESIDE], 1.0, 0.0, ALU.mult, ALU.add)
+            on_gpsimd(dst[:, :BESIDE], raw[:, :BESIDE])
 
         def round_rest(dst, raw):
             nc.vector.tensor_copy(dst[:, BESIDE:], raw[:, BESIDE:])
@@ -174,7 +177,6 @@ def tile_attend_gxfull_sil_x_kernel(tc, xT, dyT, w1, w2, ts, tx, cf, offs, out):
             return sbuf([P, PACK * K], F32, name, tag)
 
         cf_row = sbuf([P, K], F32, "cf_row")
-        cf_rows = cf_row[:].unsqueeze(1).to_broadcast([P, 2, K])
 
         def products(use, stat, moving):
             for r in range(PACK):
@@ -192,14 +194,11 @@ def tile_attend_gxfull_sil_x_kernel(tc, xT, dyT, w1, w2, ts, tx, cf, offs, out):
         def tanh_of(z, h, dst):
             nc.scalar.activation(dst, z[:, halves[h]], ACT.Tanh, scale=0.5)
 
+        cf_turned = quarters(banks[0][:]).rearrange("p c m -> p m c")
+
         def scaled_silu(silu, scaled):
             nc.vector.scalar_tensor_tensor(
-                scaled[:].rearrange("p (r f) -> p r f", r=2),
-                silu[:].rearrange("p (r f) -> p r f", r=2),
-                1.0,
-                cf_rows,
-                ALU.subtract,
-                ALU.mult,
+                scaled.rearrange("p (m c) -> p m c", c=PACK), silu.rearrange("p (m c) -> p m c", c=PACK), 1.0, cf_turned, ALU.subtract, ALU.mult
             )
 
         def slope(scaled, tanh, dst):
@@ -216,11 +215,11 @@ def tile_attend_gxfull_sil_x_kernel(tc, xT, dyT, w1, w2, ts, tx, cf, offs, out):
         nc.vector.tensor_copy(picked[1][:], listed(ts_win, 0, EXPERTS * SLOTS))
         for b in range(EXPERTS):
             gather(x_picked, x_win, 0, b)
-        tx_turned = turn_scales(0, banks[0:2])
+        tx_turned = turn_scales(0, banks[1:3])
         for c in range(PACK):
-            nc.tensor.transpose(banks[4][:, blocks[c]], cf_col[:, c : c + 1].to_broadcast([P, P]), ident[:])
-        nc.scalar.copy(cf_row[:].rearrange("p (m c) -> p m c", c=PACK), quarters(banks[4][:]).rearrange("p c m -> p m c"))
-        ts_turned = turn_scales(1, banks[2:4])
+            nc.tensor.transpose(banks[0][:, blocks[c]], cf_col[:, c : c + 1].to_broadcast([P, P]), ident[:])
+        nc.scalar.copy(cf_row[:].rearrange("p (m c) -> p m c", c=PACK), cf_turned)
+        ts_turned = turn_scales(1, banks[3:5])
         for b in range(EXPERTS):
             nc.vector.tensor_copy(tx_col[:, b * PACK : (b + 1) * PACK], tx_turned[b])
         for t in (1, 2):
@@ -238,11 +237,11 @@ def tile_attend_gxfull_sil_x_kernel(tc, xT, dyT, w1, w2, ts, tx, cf, offs, out):
         gather(x_picked, x_win, 3, 0, nc.vector.tensor_copy)
         gather(x_picked, x_win, 3, 1)
         w1f_stage0 = placed([P, PACK * K], BF16, "w1f_stage0", 6)
-        turn_weights(w1_round0, w1f_stage0, banks[4:6])
+        turn_weights(w1_round0, w1f_stage0, banks[5:7])
         x_stage0 = placed([P, PACK * K], BF16, "x_stage0", 26)
         interleave(x_picked[0], x_stage0)
         xq0 = quantized("x0", x_stage0[:], E4M3)
-        products(banks[0:4], xq0, w1d0)
+        products(banks[1:5], xq0, w1d0)
         x_stage1 = placed([P, PACK * K], BF16, "x_stage1", 22)
         interleave(x_picked[1], x_stage1, half=0)
         w1f0 = quantized("w1f0", w1f_stage0[:], E4M3, placed([P, K], U32, "w1f0_codes", 26))
@@ -253,7 +252,7 @@ def tile_attend_gxfull_sil_x_kernel(tc, xT, dyT, w1, w2, ts, tx, cf, offs, out):
         interleave(x_picked[1], x_stage1, nc.scalar.copy, half=1)
 
         z0 = wide("z0", "x_win0")
-        preactivation(0, z0, banks[0:4])
+        preactivation(0, z0, banks[1:5])
         silu0_tile = wide("silu0", "x_picked1")
         silu0 = [silu0_tile[:, h] for h in halves]
         silu_of(z0, silu0)
@@ -264,24 +263,25 @@ def tile_attend_gxfull_sil_x_kernel(tc, xT, dyT, w1, w2, ts, tx, cf, offs, out):
         interleave(w1_raw[1], w1d_stage[1])
         round_rest(w2_round0, w2_raw[0])
         w1d1 = quantized("w1d1", w1d_stage[1][:], E4M3)
-        products(banks[0:4], xq1, w1d1)
+        products(banks[1:5], xq1, w1d1)
         w2_stage0 = placed([P, PACK * K], BF16, "w2_stage0", 0)
         scaled0a = placed([P, 2 * K], F32, "scaled0a", 14)
-        scaled_silu(silu0[0], scaled0a)
+        for r in range(2):
+            scaled_silu(silu0[0][:, parts[r]], scaled0a[:, parts[r]])
         scaled0b = [placed([P, K], F32, "scaled0c", 18), placed([P, K], F32, "scaled0d", 20)]
         for r in range(2):
-            nc.vector.scalar_tensor_tensor(scaled0b[r][:], silu0[1][:, parts[r]], 1.0, cf_row[:], ALU.subtract, ALU.mult)
+            scaled_silu(silu0[1][:, parts[r]], scaled0b[r][:])
         slope(scaled0a, z0[:, halves[0]], z0[:, halves[0]])
         for r in range(2):
             slope(scaled0b[r], z0[:, parts[2 + r]], z0[:, parts[2 + r]])
         w1_round1 = placed([P, PACK * K], BF16, "w1_round1", 16)
         round_beside(w1_round1, w1_raw[1])
-        turn_weights(w2_round0, w2_stage0, banks[4:6])
+        turn_weights(w2_round0, w2_stage0, banks[5:7])
         gather(dy_picked, dy_win, 3, 0)
         for b in range(EXPERTS):
             gather(dy_picked, dy_win, 1, b)
         z1 = placed([P, PACK * K], F32, "z1", 8)
-        preactivation(1, z1, banks[0:4])
+        preactivation(1, z1, banks[1:5])
         dy_stage = [placed([P, PACK * K], BF16, "dy_stage0", 4), stage("dy_stage1", "x_win1")]
         interleave(dy_picked[0], dy_stage[0])
         round_rest(w1_round1, w1_raw[1])
@@ -294,24 +294,29 @@ def tile_attend_gxfull_sil_x_kernel(tc, xT, dyT, w1, w2, ts, tx, cf, offs, out):
         tanh_of(z1, 1, z1[:, halves[1]])
         w2q0 = quantized("w2q0", w2_stage0[:], E4M3, placed([P, K], U32, "w2q0_codes", 20))
         dyq0 = quantized("dy0", dy_stage[0][:], E5M2)
-        products(banks[4:8], dyq0, w2q0)
+        products(banks[1:5], dyq0, w2q0)
         w2_round1 = placed([P, PACK * K], BF16, "w2_round1", 2)
-        round_beside(w2_round1, w2_raw[1])
-        scaled_silu(silu1[0], silu1[0])
+        on_gpsimd(w2_round1[:], w2_raw[1][:])
+        on_gpsimd(
+            dy_stage[1][:].rearrange("p (s t) -> p s t", t=PACK)[:, SLOTS // 2 :],
+            dy_picked[1][:].rearrange("p (t s) -> p s t", t=PACK)[:, SLOTS // 2 :],
+        )
+        for r in range(2):
+            scaled_silu(silu1[0][:, parts[r]], silu1[0][:, parts[r]])
 
         da0 = stage("da0", "tx_picked")
         da_stage0 = stage("da_stage0", "x_picked1")
         for r in range(PACK):
-            gradient(0, z0, da0, banks[4:8], r)
-            if r % 2:
-                turn_pair(da0, da_stage0, r // 2, banks[4 + r // 2])
-        round_rest(w2_round1, w2_raw[1])
+            gradient(0, z0, da0, banks[1:5], r)
+        turn_pair(da0, da_stage0, 0, banks[1], nc.vector.tensor_copy)
+        turn_pair(da0, da_stage0, 1, banks[2])
         w1f_stage1 = stage("w1f_stage1", "tx_picked")
-        turn_weights(w1_round1, w1f_stage1, banks[0:2])
+        turn_weights(w1_round1, w1f_stage1, banks[5:7])
         w2_stage1 = stage("w2_stage1", "dy_win0")
-        turn_weights(w2_round1, w2_stage1, [banks[7], banks[5]])
-        scaled_silu(silu1[1], silu1[1])
-        interleave(dy_picked[1], dy_stage[1])
+        turn_weights(w2_round1, w2_stage1, [banks[4], banks[2]])
+        for r in range(2):
+            scaled_silu(silu1[1][:, parts[r]], silu1[1][:, parts[r]])
+        interleave(dy_picked[1], dy_stage[1], half=0)
         daq0 = quantized("da0", da_stage0[:], E5M2)
         slope(silu1[0], z1[:, halves[0]], z1[:, halves[0]])
         dyq1 = quantized("dy1", dy_stage[1][:], E5M2)
@@ -331,13 +336,13 @@ def tile_attend_gxfull_sil_x_kernel(tc, xT, dyT, w1, w2, ts, tx, cf, offs, out):
 
         dx0 = sbuf([P, EXPERTS * SLOTS], F32, "dx0", "x_win0")
         dx1 = sbuf([P, SLOTS], F32, "dx1", "ts_win")
-        dh1 = [banks[4], banks[6], banks[7], banks[5]]
-        product(banks[2], w1f0, 1, daq0)
+        dh1 = [banks[1], banks[0], banks[4], banks[2]]
+        product(banks[7], w1f0, 1, daq0)
         product(banks[3], w1f0, 0, daq0)
         products(dh1, dyq1, w2q1)
-        product(banks[0], w1f0, 2, daq0)
-        product(banks[1], w1f0, 3, daq0)
-        nc.scalar.copy(dx1[:], banks[2][:])
+        product(banks[5], w1f0, 2, daq0)
+        product(banks[6], w1f0, 3, daq0)
+        nc.scalar.copy(dx1[:], banks[7][:])
         nc.scalar.copy(dx0[:, parts[0]], banks[3][:])
         on_scalar(1, 0, dx1[:, 0:PIECE])
         on_scalar(0, 0, dx0[:, 0:384])
@@ -354,21 +359,21 @@ def tile_attend_gxfull_sil_x_kernel(tc, xT, dyT, w1, w2, ts, tx, cf, offs, out):
         late = sbuf([P, 2 * EXPERTS * SLOTS], F32, "late", "dy_picked")
         dx2 = late[:, : EXPERTS * SLOTS]
         dx3 = late[:, EXPERTS * SLOTS :]
-        nc.scalar.copy(dx2[:, parts[0]], banks[0][:])
-        nc.scalar.copy(dx3[:, parts[0]], banks[1][:])
+        nc.scalar.copy(dx2[:, parts[0]], banks[5][:])
+        nc.scalar.copy(dx3[:, parts[0]], banks[6][:])
         on_vector(2, 0, dx2[:, 0:PIECE])
         on_scalar(3, 0, dx3[:, 0:PIECE])
 
-        for j, acc in ((1, banks[2]), (0, banks[3]), (3, banks[7]), (2, banks[5])):
+        for j, acc in ((1, banks[7]), (0, banks[3]), (3, banks[4]), (2, banks[2])):
             product(acc, w1f1, j, daq1)
         dx1_last = sbuf([P, SLOTS], F32, "dx1_last", "tx_win")
-        nc.vector.tensor_copy(dx1_last[:], banks[2][:])
+        nc.vector.tensor_copy(dx1_last[:], banks[7][:])
         on_vector(1, SLOTS, dx1_last[:])
         store(1)
         nc.scalar.copy(dx0[:, parts[1]], banks[3][:])
-        nc.scalar.copy(dx3[:, parts[1]], banks[7][:])
+        nc.scalar.copy(dx3[:, parts[1]], banks[4][:])
         on_scalar(0, 384, dx0[:, 384:640])
-        nc.scalar.copy(dx2[:, parts[1]], banks[5][:])
+        nc.scalar.copy(dx2[:, parts[1]], banks[2][:])
         on_scalar(0, 640, dx0[:, 640:])
         store(0)
         on_vector(2, PIECE, dx2[:, PIECE:])

from contextlib import ExitStack

import concourse.mybir as mybir
from concourse.masks import make_identity

F32 = mybir.dt.float32
BF16 = mybir.dt.bfloat16
U32 = mybir.dt.uint32
I32 = mybir.dt.int32
U16 = mybir.dt.uint16
U8 = mybir.dt.uint8
E4M3 = mybir.dt.float8_e4m3fn_x4
E5M2 = mybir.dt.float8_e5m2_x4
ACT = mybir.ActivationFunctionType
ALU = mybir.AluOpType

P = 128
PACK = 4
K = P * PACK
EXPERTS = 2
SLOTS = 512
TOKENS = 2048
LIST_COLS = SLOTS // 16
ROW = P - 1
ALIGN = 64
RUN = 4
BESIDE = 1600

FLOPS = 3 * EXPERTS * 2 * K * K * SLOTS


def tile_attend_gxfull_sil_x_kernel(tc, xT, dyT, w1, w2, ts, tx, cf, offs, out):
    nc = tc.nc
    with ExitStack() as ctx:
        keep = ctx.enter_context(tc.tile_pool(name="keep", bufs=1))
        shared = ctx.enter_context(tc.tile_pool(name="shared", bufs=1))
        psum = ctx.enter_context(tc.psum_pool(name="psum", bufs=1))

        def sbuf(shape, dtype, name, tag=None):
            return keep.tile(shape, dtype, name=name, tag=tag or name, align_bytes=ALIGN)

        def placed(shape, dtype, name, kib):
            return shared.tile(shape, dtype, name=name, offset=kib * 1024, align_bytes=ALIGN)

        banks = [psum.tile([P, SLOTS], F32, name=f"bank{n}") for n in range(8)]
        blocks = [slice(r * P, (r + 1) * P) for r in range(PACK)]
        parts = [slice(r * K, (r + 1) * K) for r in range(PACK)]

        def quarters(ap):
            return ap.rearrange("p (a m) -> p a m", m=P)

        def quantized(name, woven, fmt, codes=None):
            codes = sbuf([P, K], U32, name + "_codes") if codes is None else codes
            scales = sbuf([P, K], U8, name + "_scales")
            nc.vector.quantize_mx(out=codes[:].bitcast(fmt), scales=scales[:], in_=woven)
            return codes, scales, fmt

        def product(acc, stat, block, moving):
            nc.tensor.matmul_mx(
                out=acc[:],
                lhsT=stat[0][:, blocks[block]].bitcast(stat[2]),
                lhsT_scale=stat[1][:, blocks[block]],
                rhs=moving[0][:].bitcast(moving[2]),
                rhs_scale=moving[1][:],
                start=True,
                stop=True,
            )

        offsets = keep.tile([P, EXPERTS * LIST_COLS], U16, name="offsets")
        nc.sync.dma_start(offsets[:], offs)

        def listed(window, first, count):
            return window[:].indirect(offsets[:, first // 16 : (first + count) // 16])

        tx_win = sbuf([P, TOKENS], F32, "tx_win")
        ts_win = sbuf([P, TOKENS], F32, "ts_win")
        x_win = [sbuf([P, TOKENS], F32, f"x_win{t}") for t in range(PACK - 1)] + [placed([P, TOKENS], F32, "x_win3", 0)]
        dy_win = [sbuf([P, TOKENS], F32, f"dy_win{t}") for t in range(PACK)]
        out_win = [sbuf([P, TOKENS], F32, f"out_win{j}") for j in range(PACK)]
        w1_raw = [sbuf([P, PACK * K], F32, f"w1_raw{b}") for b in range(EXPERTS)]
        w2_raw = [sbuf([P, PACK * K], F32, f"w2_raw{b}") for b in range(EXPERTS)]
        cf_col = sbuf([P, PACK], F32, "cf_col")

        x_planes = xT.rearrange("(p t) n -> t p n", t=PACK)
        dy_planes = dyT.rearrange("(p t) n -> t p n", t=PACK)

        w1_rows = [w1[b].rearrange("(p j) f -> p (j f)", j=PACK) for b in range(EXPERTS)]

        def load_w2(b):
            nc.sync.dma_start(w2_raw[b][:].rearrange("p (c e) -> p c e", c=PACK), w2[b].rearrange("(c p) e -> p c e", p=P))

        nc.scalar.dma_start(tx_win[ROW:P, :], tx[0:1, :])
        nc.scalar.dma_start(ts_win[ROW:P, :], ts[0:1, :])
        nc.scalar.dma_start(cf_col[:], cf.rearrange("(p c) o -> p (c o)", c=PACK))
        nc.sync.dma_start(x_win[0][:], x_planes[0])
        nc.sync.dma_start(x_win[1][:], x_planes[1])
        nc.sync.dma_start(w1_raw[0][:], w1_rows[0])
        nc.sync.dma_start(x_win[2][:], x_planes[2])
        nc.sync.dma_start(x_win[3][:], x_planes[3])
        nc.sync.dma_start(dy_win[0][:], dy_planes[0])
        load_w2(0)
        nc.sync.dma_start(w1_raw[1][:], w1_rows[1])
        for t in (2, 3, 1):
            nc.sync.dma_start(dy_win[t][:], dy_planes[t])
        load_w2(1)

        zero = sbuf([P, 8], F32, "zero")
        nc.vector.memset(zero[:], 0.0)
        warm = sbuf([P, 1], F32, "warm")
        nc.scalar.activation(warm[:], zero[:, 0:1], ACT.Silu)

        ident = sbuf([P, P], F32, "ident")
        make_identity(nc, ident[:])

        nc.vector.memset(tx_win[0:ROW, :].bitcast(I32), 0)
        nc.vector.memset(ts_win[0:ROW, :].bitcast(I32), 0)
        for win in out_win:
            nc.vector.memset(win[:].bitcast(I32), 0)

        def gather_on_scalar(dst, src):
            nc.scalar.activation(dst, src, ACT.Copy)

        def interleave(src, stage, copy=nc.vector.tensor_copy, half=None):
            runs = slice(None) if half is None else slice(half * P // 2, (half + 1) * P // 2)
            copy(
                stage[:].rearrange("p (c i t) -> p c t i", t=PACK, i=RUN)[:, runs],
                src[:].rearrange("p (t c i) -> p c t i", t=PACK, i=RUN)[:, runs],
            )

        def turn_pair(src, dst, h, bank, copy=nc.scalar.copy, first=None):
            first = 2 * h if first is None else first
            for c in range(2):
                pairs = src[:, parts[first + c]].bitcast(F32)
                for u in range(2):
                    nc.tensor.transpose(bank[:, blocks[2 * c + u]], pairs[:, u : K // 2 : 2], ident[:])
            copy(
                dst[:].bitcast(F32)[:, parts[h]].rearrange("p (c m u) -> p c m u", c=2, u=2),
                bank[:].rearrange("p (c u m) -> p c m u", c=2, u=2),
            )

        halves = [slice(h * 2 * K, (h + 1) * 2 * K) for h in range(2)]

        def on_gpsimd(dst, src):
            nc.gpsimd.tensor_scalar(dst, src, 1.0, 0.0, ALU.mult, ALU.add)

        def round_beside(dst, raw):
            on_gpsimd(dst[:, :BESIDE], raw[:, :BESIDE])

        def round_rest(dst, raw):
            nc.vector.tensor_copy(dst[:, BESIDE:], raw[:, BESIDE:])

        def turn_weights(src, dst, use):
            for h in range(2):
                turn_pair(src, dst, h, use[h])

        picked = [sbuf([P, EXPERTS * SLOTS], F32, "tx_picked"), sbuf([P, EXPERTS * SLOTS], F32, "ts_picked")]
        tx_col = sbuf([P, EXPERTS * PACK], F32, "tx_col")

        def turn_scales(n, use):
            for b in range(EXPERTS):
                for r in range(PACK):
                    first = b * SLOTS + r * P
                    nc.tensor.transpose(use[b][:, blocks[r]], picked[n][:, first : first + P], ident[:])
            return [quarters(use[b][:])[:, :, ROW] for b in range(EXPERTS)]

        x_picked = [placed([P, PACK * SLOTS], BF16, "x_picked0", 22), sbuf([P, PACK * SLOTS], BF16, "x_picked1")]
        dy_planes_tile = sbuf([P, (PACK + 2) * SLOTS], BF16, "dy_picked")
        dy_picked = [dy_planes_tile[:, 2 * SLOTS :], dy_planes_tile[:, : PACK * SLOTS]]

        def gather(dst, windows, t, b, copy=gather_on_scalar):
            copy(dst[b][:, parts[t]], listed(windows[t], b * SLOTS, SLOTS))

        def stage(name, tag=None):
            return sbuf([P, PACK * K], BF16, name, tag)

        def wide(name, tag=None):
            return sbuf([P, PACK * K], F32, name, tag)

        cf_row = sbuf([P, K], F32, "cf_row")

        def products(use, stat, moving):
            for r in range(PACK):
                product(use[r], stat, r, moving)

        def preactivation(b, z, use):
            for r in range(PACK):
                col = b * PACK + r
                nc.vector.scalar_tensor_tensor(z[:, parts[r]], use[r][:], tx_col[:, col : col + 1], cf_row[:], ALU.mult, ALU.mult)

        def silu_of(z, silu):
            for h in range(2):
                nc.scalar.activation(silu[h][:], z[:, halves[h]], ACT.Silu, scale=-1.0)

        def tanh_of(z, h, dst):
            nc.scalar.activation(dst, z[:, halves[h]], ACT.Tanh, scale=0.5)

        cf_turned = quarters(banks[0][:]).rearrange("p c m -> p m c")

        def scaled_silu(silu, scaled):
            nc.vector.scalar_tensor_tensor(
                scaled.rearrange("p (m c) -> p m c", c=PACK), silu.rearrange("p (m c) -> p m c", c=PACK), 1.0, cf_turned, ALU.subtract, ALU.mult
            )

        def slope(scaled, tanh, dst):
            nc.vector.scalar_tensor_tensor(dst, tanh, 1.0, scaled[:], ALU.add, ALU.mult)

        def half(name, tag=None):
            return sbuf([P, 2 * K], F32, name, tag)

        def gradient(b, factor, da, use, r):
            col = b * PACK + r
            nc.vector.scalar_tensor_tensor(da[:, parts[r]], use[r][:], gate[:, col : col + 1], factor[:, parts[r]], ALU.mult, ALU.mult)

        gather_on_scalar(picked[0][:], listed(tx_win, 0, EXPERTS * SLOTS))
        nc.vector.tensor_copy(picked[1][:], listed(ts_win, 0, EXPERTS * SLOTS))
        for b in range(EXPERTS):
            gather(x_picked, x_win, 0, b)
        tx_turned = turn_scales(0, banks[1:3])
        for c in range(PACK):
            nc.tensor.transpose(banks[0][:, blocks[c]], cf_col[:, c : c + 1].to_broadcast([P, P]), ident[:])
        nc.scalar.copy(cf_row[:].rearrange("p (m c) -> p m c", c=PACK), cf_turned)
        ts_turned = turn_scales(1, banks[3:5])
        for b in range(EXPERTS):
            nc.vector.tensor_copy(tx_col[:, b * PACK : (b + 1) * PACK], tx_turned[b])
        for t in (1, 2):
            for b in range(EXPERTS):
                gather(x_picked, x_win, t, b)
        w1d_stage = [stage("w1d_stage0"), placed([P, PACK * K], BF16, "w1d_stage1", 17)]
        w1_round0 = stage("w1_round0")
        interleave(w1_raw[0], w1d_stage[0])
        nc.vector.tensor_copy(w1_round0[:], w1_raw[0][:])
        w1d0 = quantized("w1d0", w1d_stage[0][:], E4M3)
        gate = sbuf([P, EXPERTS * PACK], F32, "gate", "w1_raw0")
        for b in range(EXPERTS):
            cols = slice(b * PACK, (b + 1) * PACK)
            nc.vector.scalar_tensor_tensor(gate[:, cols], ts_turned[b], -0.5, tx_col[:, cols], ALU.mult, ALU.mult)
        gather(x_picked, x_win, 3, 0, nc.vector.tensor_copy)
        gather(x_picked, x_win, 3, 1)
        w1f_stage0 = placed([P, PACK * K], BF16, "w1f_stage0", 6)
        turn_weights(w1_round0, w1f_stage0, banks[5:7])
        x_stage0 = placed([P, PACK * K], BF16, "x_stage0", 26)
        interleave(x_picked[0], x_stage0)
        xq0 = quantized("x0", x_stage0[:], E4M3)
        products(banks[1:5], xq0, w1d0)
        x_stage1 = placed([P, PACK * K], BF16, "x_stage1", 22)
        interleave(x_picked[1], x_stage1, half=0)
        w1f0 = quantized("w1f0", w1f_stage0[:], E4M3, placed([P, K], U32, "w1f0_codes", 26))
        w2_round0 = placed([P, PACK * K], BF16, "w2_round0", 9)
        round_beside(w2_round0, w2_raw[0])
        for b in range(EXPERTS):
            gather(dy_picked, dy_win, 0, b)
        interleave(x_picked[1], x_stage1, nc.scalar.copy, half=1)

        z0 = wide("z0", "x_win0")
        preactivation(0, z0, banks[1:5])
        silu0_tile = wide("silu0", "x_picked1")
        silu0 = [silu0_tile[:, h] for h in halves]
        silu_of(z0, silu0)
        for h in range(2):
            tanh_of(z0, h, z0[:, halves[h]])
        gather(dy_picked, dy_win, 2, 0)
        xq1 = quantized("x1", x_stage1[:], E4M3)
        interleave(w1_raw[1], w1d_stage[1])
        round_rest(w2_round0, w2_raw[0])
        w1d1 = quantized("w1d1", w1d_stage[1][:], E4M3)
        products(banks[1:5], xq1, w1d1)
        w2_stage0 = placed([P, PACK * K], BF16, "w2_stage0", 0)
        scaled0a = placed([P, 2 * K], F32, "scaled0a", 14)
        for r in range(2):
            scaled_silu(silu0[0][:, parts[r]], scaled0a[:, parts[r]])
        scaled0b = [placed([P, K], F32, "scaled0c", 18), placed([P, K], F32, "scaled0d", 20)]
        for r in range(2):
            scaled_silu(silu0[1][:, parts[r]], scaled0b[r][:])
        slope(scaled0a, z0[:, halves[0]], z0[:, halves[0]])
        for r in range(2):
            slope(scaled0b[r], z0[:, parts[2 + r]], z0[:, parts[2 + r]])
        w1_round1 = placed([P, PACK * K], BF16, "w1_round1", 16)
        round_beside(w1_round1, w1_raw[1])
        turn_weights(w2_round0, w2_stage0, banks[5:7])
        gather(dy_picked, dy_win, 3, 0)
        for b in range(EXPERTS):
            gather(dy_picked, dy_win, 1, b)
        z1 = placed([P, PACK * K], F32, "z1", 8)
        preactivation(1, z1, banks[1:5])
        dy_stage = [placed([P, PACK * K], BF16, "dy_stage0", 4), stage("dy_stage1", "x_win1")]
        interleave(dy_picked[0], dy_stage[0])
        round_rest(w1_round1, w1_raw[1])
        silu1_tile = wide("silu1", "dy_win1")
        silu1 = [silu1_tile[:, h] for h in halves]
        silu_of(z1, silu1)
        tanh_of(z1, 0, z1[:, halves[0]])
        for t in (2, 3):
            gather(dy_picked, dy_win, t, 1)
        tanh_of(z1, 1, z1[:, halves[1]])
        w2q0 = quantized("w2q0", w2_stage0[:], E4M3, placed([P, K], U32, "w2q0_codes", 20))
        dyq0 = quantized("dy0", dy_stage[0][:], E5M2)
        products(banks[1:5], dyq0, w2q0)
        w2_round1 = placed([P, PACK * K], BF16, "w2_round1", 2)
        on_gpsimd(w2_round1[:], w2_raw[1][:])
        on_gpsimd(
            dy_stage[1][:].rearrange("p (s t) -> p s t", t=PACK)[:, SLOTS // 2 :],
            dy_picked[1][:].rearrange("p (t s) -> p s t", t=PACK)[:, SLOTS // 2 :],
        )
        for r in range(2):
            scaled_silu(silu1[0][:, parts[r]], silu1[0][:, parts[r]])

        da0 = stage("da0", "tx_picked")
        da_stage0 = stage("da_stage0", "x_picked1")
        for r in range(PACK):
            gradient(0, z0, da0, banks[1:5], r)
        turn_pair(da0, da_stage0, 0, banks[1], nc.vector.tensor_copy)
        turn_pair(da0, da_stage0, 1, banks[2])
        w1f_stage1 = stage("w1f_stage1", "tx_picked")
        turn_weights(w1_round1, w1f_stage1, banks[5:7])
        w2_stage1 = stage("w2_stage1", "dy_win0")
        turn_weights(w2_round1, w2_stage1, [banks[4], banks[2]])
        for r in range(2):
            scaled_silu(silu1[1][:, parts[r]], silu1[1][:, parts[r]])
        interleave(dy_picked[1], dy_stage[1], half=0)
        daq0 = quantized("da0", da_stage0[:], E5M2)
        slope(silu1[0], z1[:, halves[0]], z1[:, halves[0]])
        dyq1 = quantized("dy1", dy_stage[1][:], E5M2)
        w2q1 = quantized("w2q1", w2_stage1[:], E4M3)

        rows = out.rearrange("(p j) n -> j p n", j=PACK)
        PIECE = SLOTS // 2

        def on_vector(j, first, src):
            nc.vector.tensor_copy(listed(out_win[j], first, src.shape[1]), src)

        def on_scalar(j, first, src):
            nc.scalar.activation(listed(out_win[j], first, src.shape[1]), src, ACT.Copy)

        def store(j):
            nc.sync.dma_start(rows[j], out_win[j][:])

        dx0 = sbuf([P, EXPERTS * SLOTS], F32, "dx0", "x_win0")
        dx1 = sbuf([P, SLOTS], F32, "dx1", "ts_win")
        dh1 = [banks[1], banks[0], banks[4], banks[2]]
        product(banks[7], w1f0, 1, daq0)
        product(banks[3], w1f0, 0, daq0)
        products(dh1, dyq1, w2q1)
        product(banks[5], w1f0, 2, daq0)
        product(banks[6], w1f0, 3, daq0)
        nc.scalar.copy(dx1[:], banks[7][:])
        nc.scalar.copy(dx0[:, parts[0]], banks[3][:])
        on_scalar(1, 0, dx1[:, 0:PIECE])
        on_scalar(0, 0, dx0[:, 0:384])
        slope(silu1[1], z1[:, halves[1]], z1[:, halves[1]])
        w1f1 = quantized("w1f1", w1f_stage1[:], E4M3)
        da1 = stage("da1", "dy_picked")
        da_stage1 = stage("da_stage1", "ts_picked")
        for r in range(PACK):
            gradient(1, z1, da1, dh1, r)
            if r % 2:
                turn_pair(da1, da_stage1, r // 2, dh1[r // 2])
        on_vector(1, PIECE, dx1[:, PIECE:])
        daq1 = quantized("da1", da_stage1[:], E5M2)
        late = sbuf([P, 2 * EXPERTS * SLOTS], F32, "late", "dy_picked")
        dx2 = late[:, : EXPERTS * SLOTS]
        dx3 = late[:, EXPERTS * SLOTS :]
        nc.scalar.copy(dx2[:, parts[0]], banks[5][:])
        nc.scalar.copy(dx3[:, parts[0]], banks[6][:])
        on_vector(2, 0, dx2[:, 0:PIECE])
        on_scalar(3, 0, dx3[:, 0:PIECE])

        for j, acc in ((1, banks[7]), (0, banks[3]), (3, banks[4]), (2, banks[2])):
            product(acc, w1f1, j, daq1)
        dx1_last = sbuf([P, SLOTS], F32, "dx1_last", "tx_win")
        nc.vector.tensor_copy(dx1_last[:], banks[7][:])
        on_vector(1, SLOTS, dx1_last[:])
        store(1)
        nc.scalar.copy(dx0[:, parts[1]], banks[3][:])
        nc.scalar.copy(dx3[:, parts[1]], banks[4][:])
        on_scalar(0, 384, dx0[:, 384:640])
        nc.scalar.copy(dx2[:, parts[1]], banks[2][:])
        on_scalar(0, 640, dx0[:, 640:])
        store(0)
        on_vector(2, PIECE, dx2[:, PIECE:])
        store(2)
        on_scalar(3, PIECE, dx3[:, PIECE:640])
        on_scalar(3, 640, dx3[:, 640:])
        store(3)
